import numpy as np
import ml_dtypes


def mxq(x, axis, fmt="e4m3"):
    dtype, down = {"e4m3": (ml_dtypes.float8_e4m3fn, 7), "e5m2": (ml_dtypes.float8_e5m2, 14)}[fmt]
    v = np.moveaxis(np.asarray(x, np.float32).astype(ml_dtypes.bfloat16).astype(np.float64), axis, -1)
    blocks = v.reshape(v.shape[:-1] + (-1, 32))
    amax = np.abs(blocks).max(-1, keepdims=True)
    byte = np.maximum(np.where(amax > 0, np.frexp(amax)[1] - 1 + 127, 0) - down, 1)
    scale = np.exp2(byte - 127.0)
    codes = (blocks / scale).astype(np.float32).astype(dtype).astype(np.float64)
    return np.moveaxis((codes * scale).reshape(v.shape), -1, axis)


WIDE = False


def mx_kscale(k):
    if not WIDE:
        return np.ones(k)
    levels = np.array([10, -10, 5, -5, 0])
    if k % 512:
        return np.exp2(np.random.permutation(np.resize(levels, k // 32))).repeat(32)
    a = np.empty((k // 512, 16))
    for p in range(k // 512):
        a[p, :8] = np.random.permutation(np.resize(levels, 8))
        for g in range(8):
            far = levels[np.abs(levels - a[p, g]) >= 10]
            a[p, g + 8] = far[np.random.randint(len(far))]
    return np.exp2(a.ravel()).repeat(32)


BF16 = ml_dtypes.bfloat16


def bf(x):
    return np.asarray(x, np.float32).astype(BF16)


def f64(x):
    return np.asarray(x).astype(np.float64)


E2M1 = np.array([0.0, 0.5, 1.0, 1.5, 2.0, 3.0, 4.0, 6.0, -0.0, -0.5, -1.0, -1.5, -2.0, -3.0, -4.0, -6.0])


def pack_weight(w, fmt):
    k, n = w.shape
    w = f64(bf(w)).reshape(k // 32, 32, n)
    amax = np.abs(w).max(1)
    if fmt == "e4m3":
        byte = np.frexp(amax)[1] - 1 + 127 - 7
    else:
        mant, ex = np.frexp(amax / 6.0)
        byte = np.where(mant > 0.5, ex, ex - 1) + 127
    byte = np.clip(np.where(amax > 0, byte, 1), 1, 254)
    scaled = (w * np.exp2(127.0 - byte)[:, None, :]).reshape(k, n).astype(np.float32)
    by_word = np.ascontiguousarray(scaled.reshape(k // 512, 128, 4, n).transpose(0, 1, 3, 2))
    if fmt == "e4m3":
        words = by_word.astype(ml_dtypes.float8_e4m3fn).view(np.uint8)
    else:
        c = by_word.astype(ml_dtypes.float4_e2m1fn).view(np.uint8) & 0xF
        words = c[..., 0::2] | (c[..., 1::2] << 4)
    return np.ascontiguousarray(words), np.ascontiguousarray(byte.astype(np.uint8).reshape(k // 512, 16, n))


def unpack_weight(words, scales, fmt):
    g, p, n, _ = words.shape
    if fmt == "e4m3":
        vals = np.ascontiguousarray(words).view(ml_dtypes.float8_e4m3fn).astype(np.float64)
    else:
        nib = np.empty((g, p, n, 4), np.uint8)
        nib[..., 0::2] = words & 0xF
        nib[..., 1::2] = words >> 4
        vals = E2M1[nib]
    vals = vals * np.repeat(np.exp2(scales.astype(np.float64) - 127.0), 8, axis=1)[..., None]
    return vals.transpose(0, 1, 3, 2).reshape(g * 512, n)
def pack4(w):
    words, scales = pack_weight(w, "e2m1")
    return words.reshape(words.shape[0], 128, -1), scales


def unpack4(words, scales):
    return unpack_weight(words.reshape(words.shape[0], 128, -1, 2), scales, "e2m1")


T1, T2, M, R, E = 512, 1536, 1024, 1024, 512


def draw0():
    s1, s2, u = mx_kscale(T1), mx_kscale(T2), mx_kscale(R)
    archive = np.random.standard_normal((T2, R)) * 0.11 / np.sqrt(T2) / s2[:, None]
    old_words, old_scales = pack4(archive)
    net = np.random.standard_normal((R, E)) / np.sqrt(R) / u[:, None]
    net_words, net_scales = pack4(net)
    return {"seeds_new": bf(np.random.standard_normal((T1, M)) * s1[:, None]),
            "regions_new": bf(np.random.standard_normal((T1, R)) * 0.09 / np.sqrt(T1) / s1[:, None]),
            "seeds_old": bf(np.random.standard_normal((T2, M)) * s2[:, None]),
            "old_words": old_words, "old_scales": old_scales,
            "precision": bf(3.0 * (1 + 0.1 * np.random.standard_normal(R)) * u),
            "net_words": net_words, "net_scales": net_scales}


def core(seeds_new, regions_new, seeds_old, old_words, old_scales, precision, net_words, net_scales):
    r_new = mxq(f64(seeds_new), 0, "e4m3").T @ mxq(f64(regions_new), 0, "e4m3")
    r_old = mxq(f64(seeds_old), 0, "e4m3").T @ unpack4(old_words, old_scales)
    r = r_new + r_old
    z = np.log((1.0 + r) / (1.0 - r)) * f64(precision)
    return mxq(z, 1, "e4m3") @ unpack4(net_words, net_scales)


def e4m3fn_bytes(y):
    return np.clip(np.asarray(y, np.float64), -448.0, 448.0).astype(np.float32).astype(ml_dtypes.float8_e4m3fn).view(np.uint8)


def e4m3fn_values(b):
    return np.asarray(b, np.uint8).view(ml_dtypes.float8_e4m3fn).astype(np.float64)


def setup_inputs():
    d = draw0()
    x0 = np.asarray(d['seeds_old']).astype(np.float64)
    s = (np.max(np.abs(x0), axis=(1,), keepdims=True) / 448.0).astype(np.float32)
    out = {}
    for k, v in d.items():
        if k == 'seeds_old':
            out['seeds_old_bytes'] = e4m3fn_bytes(x0 / s.astype(np.float64))
            out['seeds_old_scale'] = s
        else:
            out[k] = v
    return out


def reference(seeds_new, regions_new, seeds_old_bytes, seeds_old_scale, old_words, old_scales, precision, net_words, net_scales):
    return core(seeds_new, regions_new, e4m3fn_values(seeds_old_bytes) * seeds_old_scale.astype(np.float64), old_words, old_scales, precision, net_words, net_scales)

@@ -1,0 +1,377 @@
+from contextlib import ExitStack
+
+import concourse.mybir as mybir
+from concourse.masks import make_identity
+
+T1, T2, M, R, E = 512, 1536, 1024, 1024, 512
+FLOPS = 2 * M * R * (T1 + T2) + 2 * M * R * E
+
+F32 = mybir.dt.float32
+BF16 = mybir.dt.bfloat16
+U32 = mybir.dt.uint32
+I32 = mybir.dt.int32
+U8 = mybir.dt.uint8
+FP8 = mybir.dt.float8_e4m3fn
+FP8X4 = mybir.dt.float8_e4m3fn_x4
+FP4X4 = mybir.dt.float4_e2m1fn_x4
+ACT = mybir.ActivationFunctionType
+ALU = mybir.AluOpType
+
+P = 128
+PACK = 4
+GROUPS = T2 // (P * PACK)
+PASSES = 1 + GROUPS
+HALF = 512
+CHUNK = 256
+TILES = M // P
+
+PASS_ORDER = (2, 1, 3, 0)
+
+WIDEN = {0: ((2, 2),), 1: ((2, 3), (3, 2)), 2: ((3, 3),)}
+SCALAR_INTERLEAVE = {2: ((3, 0),), 3: ((3, 2),)}
+BEFORE_DIFFERENCE = {1: ((2, 0),)}
+AFTER_TURN = {0: ((1, 3),), 1: ((3, 1), (2, 2)), 2: ((2, 3), (3, 3))}
+QUANTISE_CHUNK = {2: 2, 4: 3}
+
+PSUM_DIFFERENCE = (1, 2)
+WEIGH_LATE = (2, 4)
+
+
+def tile_pooled_fisher_connectivity_s3_kernel(
+    tc,
+    seeds_new,
+    regions_new,
+    seeds_old_bytes,
+    seeds_old_scale,
+    old_words,
+    old_scales,
+    precision,
+    net_words,
+    net_scales,
+    out,
+):
+    nc = tc.nc
+    with ExitStack() as ctx:
+        keep = ctx.enter_context(tc.tile_pool(name="keep", bufs=1))
+        old_pool = ctx.enter_context(tc.tile_pool(name="old", bufs=2 * GROUPS))
+        chunk_pool = ctx.enter_context(tc.tile_pool(name="chunks", bufs=M // CHUNK))
+        work = ctx.enter_context(tc.tile_pool(name="work", bufs=4))
+        psum_r = ctx.enter_context(tc.psum_pool(name="psum_r", bufs=4))
+        psum_turn = ctx.enter_context(tc.psum_pool(name="psum_turn", bufs=2))
+        psum_out = ctx.enter_context(tc.psum_pool(name="psum_out", bufs=2))
+        ctx.enter_context(tc.manual_schedule())
+
+        regions_a = keep.tile([P, PACK, 256], BF16, align_bytes=64)
+        regions_b = keep.tile([P, PACK, 256], BF16, align_bytes=64)
+        regions_c = keep.tile([P, PACK, HALF], BF16, align_bytes=64)
+        region_loads = ((regions_a, 0), (regions_b, 256), (regions_c, HALF))
+        new_a = keep.tile([P, PACK, HALF], BF16, align_bytes=64)
+        new_b = keep.tile([P, PACK, HALF], BF16, align_bytes=64)
+        new_raw = (new_a, new_b)
+        old_bytes = {}
+        for g in range(GROUPS):
+            for half in range(2):
+                old_bytes_tile = old_pool.tile([P, PACK, HALF], U8, align_bytes=64)
+                old_bytes[g, half] = old_bytes_tile
+        old_factor = keep.tile([P, GROUPS, PACK], F32)
+        d_words_a = keep.tile([P, GROUPS, 2 * HALF], U8, align_bytes=64)
+        d_words_b = keep.tile([P, GROUPS, 2 * HALF], U8, align_bytes=64)
+        d_words = (d_words_a, d_words_b)
+        d_scales = keep.tile([P, GROUPS, R], U8, align_bytes=64)
+        p_words = keep.tile([P, 2, 2 * E], U8, align_bytes=64)
+        p_scales = keep.tile([P, 2, E], U8, align_bytes=64)
+        weights = keep.tile([P, 2, PACK], BF16)
+
+        regions_grouped = keep.tile([P, R, PACK], BF16, align_bytes=64)
+        regions_codes = keep.tile([P, R], U32, align_bytes=64)
+        regions_scales = keep.tile([P, R], U8, align_bytes=64)
+        wide, grouped, codes, scales = [], [], [], []
+        for c in range(M // CHUNK):
+            wide_tile = chunk_pool.tile([P, GROUPS, PACK, CHUNK], BF16, align_bytes=64)
+            grouped_tile = chunk_pool.tile([P, PASSES, CHUNK, PACK], BF16, align_bytes=64)
+            codes_tile = chunk_pool.tile([P, PASSES, CHUNK], U32, align_bytes=64)
+            scales_tile = chunk_pool.tile([P, PASSES, CHUNK], U8, align_bytes=64)
+            wide.append(wide_tile)
+            grouped.append(grouped_tile)
+            codes.append(codes_tile)
+            scales.append(scales_tile)
+
+        identity = keep.tile([P, P], F32)
+        one = keep.tile([P, 1], F32)
+
+        nc.gpsimd.memset(d_scales[:].rearrange("p g n -> p (g n)").bitcast(I32), 0)
+        nc.gpsimd.memset(p_scales[:].rearrange("p g n -> p (g n)").bitcast(I32), 0)
+        nc.vector.memset(one[:], 1.0)
+        make_identity(nc, identity[:])
+
+        def load_regions(j):
+            tile, lo = region_loads[j]
+            nc.sync.dma_start(
+                out=tile[:], in_=regions_new.rearrange("(p t) n -> p t n", t=PACK)[:, :, lo : lo + tile[:].shape[2]]
+            )
+
+        def load_new(half):
+            nc.sync.dma_start(
+                out=new_raw[half][:],
+                in_=seeds_new.rearrange("(p t) n -> p t n", t=PACK)[:, :, HALF * half : HALF * half + HALF],
+            )
+
+        def load_old(g, half):
+            rows = seeds_old_bytes.rearrange("(g p t) n -> g p t n", p=P, t=PACK)[g]
+            nc.sync.dma_start(out=old_bytes[g, half][:], in_=rows[:, :, HALF * half : HALF * half + HALF])
+
+        def load_d(half):
+            words = old_words.rearrange("g p w -> p g w")
+            nc.sync.dma_start(out=d_words[half][:], in_=words[:, :, 2 * HALF * half : 2 * HALF * half + 2 * HALF])
+
+        def load_scale_rows(tile, rows, groups):
+            for q in range(4):
+                quadrant = tile[32 * q : 32 * q + 4].rearrange("p g n -> p (g n)").bitcast(I32)
+                nc.sync.dma_start(
+                    out=quadrant.rearrange("p (g n) -> p g n", g=groups),
+                    in_=rows[:, 4 * q : 4 * q + 4, :].bitcast(I32).rearrange("g r n -> r g n"),
+                )
+
+        nc.scalar.dma_start(
+            out=old_factor[:], in_=seeds_old_scale.rearrange("(g p t) o -> p g (t o)", p=P, t=PACK)
+        )
+        load_old(0, 0)
+        load_regions(0)
+        load_regions(1)
+        load_scale_rows(d_scales, old_scales, GROUPS)
+        load_old(1, 0)
+        load_old(2, 0)
+        load_new(0)
+        load_d(0)
+        load_d(1)
+        load_regions(2)
+        for g in range(GROUPS):
+            load_old(g, 1)
+        load_new(1)
+        nc.sync.dma_start(out=p_words[:], in_=net_words.rearrange("g p w -> p g w"))
+        load_scale_rows(p_scales, net_scales, 2)
+        nc.sync.dma_start(out=weights[:], in_=precision.rearrange("(h p t) -> p h t", p=P, t=PACK))
+
+        nc.scalar.activation(out=one[:], in_=one[:], func=ACT.Ln)
+
+        def widen(c, k):
+            cols = slice(CHUNK * (c % 2), CHUNK * (c % 2) + CHUNK)
+            for t in range(PACK):
+                nc.scalar.activation(
+                    out=wide[c][:, k - 1, t, :],
+                    in_=old_bytes[k - 1, c // 2][:, t, cols].bitcast(FP8),
+                    func=ACT.Copy,
+                    scale=old_factor[:, k - 1, t : t + 1],
+                )
+
+        def interleave(copy, dst, src):
+            copy(out=dst, in_=src.rearrange("p t n -> p n t"))
+
+        def interleave_regions(j):
+            tile, lo = region_loads[j]
+            interleave(nc.vector.tensor_copy, regions_grouped[:, lo : lo + tile[:].shape[2], :], tile[:])
+
+        def quantise_regions(h):
+            cols = slice(HALF * h, HALF * h + HALF)
+            nc.vector.quantize_mx(
+                out=regions_codes[:, cols].bitcast(FP8X4),
+                scales=regions_scales[:, cols],
+                in_=regions_grouped[:, cols, :].rearrange("p n t -> p (n t)"),
+            )
+
+        def interleave_seeds(c, k, copy=nc.vector.tensor_copy):
+            if k == 0:
+                src = new_raw[c // 2][:, :, CHUNK * (c % 2) : CHUNK * (c % 2) + CHUNK]
+            else:
+                src = wide[c][:, k - 1, :, :]
+            interleave(copy, grouped[c][:, k, :, :], src)
+
+        def quantise_seeds(c, first, last):
+            nc.vector.quantize_mx(
+                out=codes[c][:, first:last, :].rearrange("p k n -> p (k n)").bitcast(FP8X4),
+                scales=scales[c][:, first:last, :].rearrange("p k n -> p (k n)"),
+                in_=grouped[c][:, first:last, :, :].rearrange("p k n t -> p (k n t)"),
+            )
+
+        r = {}
+
+        def take_banks(i):
+            for h in range(2):
+                r_bank = psum_r.tile([P, HALF], F32)
+                r[i, h] = r_bank
+
+        def correlate(tiles, h):
+            for n, k in enumerate(PASS_ORDER):
+                if k == 0:
+                    moving = regions_codes[:, HALF * h : HALF * h + HALF].bitcast(FP8X4)
+                    moving_scale = regions_scales[:, HALF * h : HALF * h + HALF]
+                else:
+                    moving = d_words[h][:, k - 1, :].bitcast(FP4X4)
+                    moving_scale = d_scales[:, k - 1, HALF * h : HALF * h + HALF]
+                for i in tiles:
+                    c, j = divmod(i, CHUNK // P)
+                    cols = slice(P * j, P * j + P)
+                    nc.tensor.matmul_mx(
+                        out=r[i, h][:],
+                        lhsT=codes[c][:, k, cols].bitcast(FP8X4),
+                        lhsT_scale=scales[c][:, k, cols],
+                        rhs=moving,
+                        rhs_scale=moving_scale,
+                        start=(n == 0),
+                        stop=(n == PASSES - 1),
+                    )
+
+        ln_plus, ln_minus, difference = {}, {}, {}
+
+        def take_logarithms(i, h):
+            if h == 0:
+                ln_plus_tile = work.tile([P, 2, PACK, P], F32)
+                ln_minus_tile = work.tile([P, 2, PACK, P], F32)
+                ln_plus[i], ln_minus[i] = ln_plus_tile, ln_minus_tile
+            by_t = r[i, h][:].rearrange("s (p t) -> s t p", t=PACK)
+            nc.scalar.activation(out=ln_plus[i][:, h], in_=by_t, func=ACT.Ln, bias=1.0, scale=1.0)
+            nc.scalar.activation(out=ln_minus[i][:, h], in_=by_t, func=ACT.Ln, bias=1.0, scale=-1.0)
+
+        def form_difference(i, h):
+            if h == 0:
+                difference_tile = work.tile([P, 2, PACK, P], F32)
+                difference[i] = difference_tile
+            if i in PSUM_DIFFERENCE:
+                nc.vector.tensor_scalar(
+                    out=difference[i][:, h], in0=ln_minus[i][:, h], scalar1=-1.0, scalar2=None, op0=ALU.mult
+                )
+            else:
+                nc.vector.tensor_tensor(
+                    out=difference[i][:, h], in0=ln_plus[i][:, h], in1=ln_minus[i][:, h], op=ALU.subtract
+                )
+
+        turned = {}
+
+        def turn(i, h):
+            turned_bank = psum_turn.tile([P, PACK, P], F32)
+            turned[i, h] = turned_bank
+            parts = (ln_plus[i], difference[i]) if i in PSUM_DIFFERENCE else (difference[i],)
+            for t in range(PACK):
+                for n, part in enumerate(parts):
+                    nc.tensor.matmul(
+                        turned_bank[:, t, :],
+                        lhsT=part[:, h, t, :],
+                        rhs=identity[:],
+                        start=(n == 0),
+                        stop=(n == len(parts) - 1),
+                        is_transpose=True,
+                    )
+
+        z_codes, z_scales = {}, {}
+
+        def weigh_and_quantise(i):
+            z_grouped = work.tile([P, 2, P, PACK], BF16, align_bytes=64)
+            z_codes_tile = work.tile([P, 2, P], U32, align_bytes=64)
+            z_scales_tile = work.tile([P, 2, P], U8, align_bytes=64)
+            z_codes[i], z_scales[i] = z_codes_tile, z_scales_tile
+            for h in range(2):
+                nc.vector.tensor_tensor(
+                    out=z_grouped[:, h, :, :],
+                    in0=turned[i, h][:].rearrange("p t n -> p n t"),
+                    in1=weights[:, h, :].unsqueeze(1).to_broadcast([P, P, PACK]),
+                    op=ALU.mult,
+                )
+            for h in range(2):
+                nc.vector.quantize_mx(
+                    out=z_codes_tile[:, h, :].bitcast(FP8X4),
+                    scales=z_scales_tile[:, h, :],
+                    in_=z_grouped[:, h, :, :].rearrange("p n t -> p (n t)"),
+                )
+
+        out_bank = {}
+
+        def project(i):
+            out_bank_tile = psum_out.tile([P, E], F32)
+            out_bank[i] = out_bank_tile
+            for h in range(2):
+                nc.tensor.matmul_mx(
+                    out=out_bank_tile[:],
+                    lhsT=z_codes[i][:, h, :].bitcast(FP8X4),
+                    lhsT_scale=z_scales[i][:, h, :],
+                    rhs=p_words[:, h, :].bitcast(FP4X4),
+                    rhs_scale=p_scales[:, h, :],
+                    start=(h == 0),
+                    stop=(h == 1),
+                )
+
+        def store(i):
+            result = work.tile([P, E], F32)
+            nc.scalar.copy(out=result[:], in_=out_bank[i][:])
+            nc.sync.dma_start(out=out[P * i : P * i + P, :], in_=result[:])
+
+        def store_in_halves(i):
+            result_a = work.tile([P, E // 2], F32)
+            result_b = work.tile([P, E // 2], F32)
+            nc.scalar.copy(out=result_a[:], in_=out_bank[i][:, : E // 2])
+            nc.vector.tensor_copy(out=result_b[:], in_=out_bank[i][:, E // 2 :])
+            nc.sync.dma_start(out=out[P * i : P * i + P, : E // 2], in_=result_a[:])
+            nc.sync.dma_start(out=out[P * i : P * i + P, E // 2 :], in_=result_b[:])
+
+        for k in range(1, PASSES):
+            widen(0, k)
+            widen(1, k)
+        widen(2, 1)
+        widen(3, 1)
+        interleave_regions(0)
+        interleave_regions(1)
+        quantise_regions(0)
+        interleave_seeds(0, 1)
+        interleave_seeds(0, 2)
+        quantise_seeds(0, 1, 2)
+        interleave_seeds(0, 0)
+        quantise_seeds(0, 2, 3)
+        interleave_seeds(1, 0)
+        interleave_seeds(0, 3)
+        quantise_seeds(0, 0, 1)
+        quantise_seeds(0, 3, 4)
+        interleave_regions(2)
+        quantise_regions(1)
+        take_banks(0)
+        take_banks(1)
+        correlate((0, 1), 0)
+        correlate((0, 1), 1)
+
+        for i in range(TILES):
+            take_logarithms(i, 0)
+            for c, k in WIDEN.get(i, ()):
+                widen(c, k)
+            take_logarithms(i, 1)
+            if i > 1:
+                store(i - 2)
+            for c, k in SCALAR_INTERLEAVE.get(i, ()):
+                interleave_seeds(c, k, nc.scalar.copy)
+            if i == 0:
+                interleave_seeds(1, 1)
+                quantise_seeds(1, 0, 2)
+                interleave_seeds(1, 2)
+            for c, k in BEFORE_DIFFERENCE.get(i, ()):
+                interleave_seeds(c, k)
+            form_difference(i, 0)
+            form_difference(i, 1)
+            if i - 1 in WEIGH_LATE:
+                weigh_and_quantise(i - 1)
+            turn(i, 0)
+            turn(i, 1)
+            for c, k in AFTER_TURN.get(i, ()):
+                interleave_seeds(c, k)
+            if i == 0:
+                quantise_seeds(1, 2, 4)
+                interleave_seeds(2, 1)
+            if i in QUANTISE_CHUNK:
+                quantise_seeds(QUANTISE_CHUNK[i], 0, PASSES)
+            if i not in WEIGH_LATE:
+                weigh_and_quantise(i)
+            if i > 0:
+                project(i - 1)
+            if i + 2 < TILES:
+                take_banks(i + 2)
+                correlate((i + 2,), 0)
+                correlate((i + 2,), 1)
+        store(TILES - 2)
+        project(TILES - 1)
+        store_in_halves(TILES - 1)

@@ -25,16 +25,11 @@ HALF = 512
 CHUNK = 256
 TILES = M // P
 
-PASS_ORDER = (2, 1, 3, 0)
-
-WIDEN = {0: ((2, 2),), 1: ((2, 3), (3, 2)), 2: ((3, 3),)}
-SCALAR_INTERLEAVE = {2: ((3, 0),), 3: ((3, 2),)}
-BEFORE_DIFFERENCE = {1: ((2, 0),)}
-AFTER_TURN = {0: ((1, 3),), 1: ((3, 1), (2, 2)), 2: ((2, 3), (3, 3))}
-QUANTISE_CHUNK = {2: 2, 4: 3}
-
-PSUM_DIFFERENCE = (1, 2)
-WEIGH_LATE = (2, 4)
+PASS_ORDER = (1, 2, 3, 0)
+OLD_RANGES = ((0, 512), (512, 1024))
+NEW_RANGES = ((0, 256), (256, 512), (512, 1024))
+REGION_RANGES = ((0, 256), (256, 512), (512, 1024))
+PSUM_DIFFERENCE = [(i, h) for i in range(TILES) for h in range(2) if (i, h) not in ((6,0),(6,1),(7,0))]
 
 
 def tile_pooled_fisher_connectivity_s3_kernel(
@@ -53,72 +48,54 @@ def tile_pooled_fisher_connectivity_s3_kernel(
     nc = tc.nc
     with ExitStack() as ctx:
         keep = ctx.enter_context(tc.tile_pool(name="keep", bufs=1))
-        old_pool = ctx.enter_context(tc.tile_pool(name="old", bufs=2 * GROUPS))
-        chunk_pool = ctx.enter_context(tc.tile_pool(name="chunks", bufs=M // CHUNK))
-        work = ctx.enter_context(tc.tile_pool(name="work", bufs=4))
-        psum_r = ctx.enter_context(tc.psum_pool(name="psum_r", bufs=4))
-        psum_turn = ctx.enter_context(tc.psum_pool(name="psum_turn", bufs=2))
-        psum_out = ctx.enter_context(tc.psum_pool(name="psum_out", bufs=2))
+        work = ctx.enter_context(tc.tile_pool(name="work", bufs=3))
+        psum = ctx.enter_context(tc.psum_pool(name="psum", bufs=1))
         ctx.enter_context(tc.manual_schedule())
 
-        regions_a = keep.tile([P, PACK, 256], BF16, align_bytes=64)
-        regions_b = keep.tile([P, PACK, 256], BF16, align_bytes=64)
-        regions_c = keep.tile([P, PACK, HALF], BF16, align_bytes=64)
-        region_loads = ((regions_a, 0), (regions_b, 256), (regions_c, HALF))
-        new_a = keep.tile([P, PACK, HALF], BF16, align_bytes=64)
-        new_b = keep.tile([P, PACK, HALF], BF16, align_bytes=64)
-        new_raw = (new_a, new_b)
-        old_bytes = {}
-        for g in range(GROUPS):
-            for half in range(2):
-                old_bytes_tile = old_pool.tile([P, PACK, HALF], U8, align_bytes=64)
-                old_bytes[g, half] = old_bytes_tile
+        regions_raw = [
+            keep.tile([P, PACK, hi - lo], BF16, align_bytes=64, name=f"regions_raw_{lo}") for lo, hi in REGION_RANGES
+        ]
+        new_raw = [keep.tile([P, PACK, hi - lo], BF16, align_bytes=64, name=f"new_raw_{lo}") for lo, hi in NEW_RANGES]
+        old_bytes = [
+            [keep.tile([P, PACK, hi - lo], U8, align_bytes=64, name=f"old_bytes_{g}_{lo}") for lo, hi in OLD_RANGES]
+            for g in range(GROUPS)
+        ]
         old_factor = keep.tile([P, GROUPS, PACK], F32)
-        d_words_a = keep.tile([P, GROUPS, 2 * HALF], U8, align_bytes=64)
-        d_words_b = keep.tile([P, GROUPS, 2 * HALF], U8, align_bytes=64)
-        d_words = (d_words_a, d_words_b)
+        d_words = [keep.tile([P, GROUPS, 2 * HALF], U8, align_bytes=64, name=f"d_words_{h}") for h in range(2)]
         d_scales = keep.tile([P, GROUPS, R], U8, align_bytes=64)
         p_words = keep.tile([P, 2, 2 * E], U8, align_bytes=64)
         p_scales = keep.tile([P, 2, E], U8, align_bytes=64)
         weights = keep.tile([P, 2, PACK], BF16)
 
-        regions_grouped = keep.tile([P, R, PACK], BF16, align_bytes=64)
-        regions_codes = keep.tile([P, R], U32, align_bytes=64)
-        regions_scales = keep.tile([P, R], U8, align_bytes=64)
-        wide, grouped, codes, scales = [], [], [], []
-        for c in range(M // CHUNK):
-            wide_tile = chunk_pool.tile([P, GROUPS, PACK, CHUNK], BF16, align_bytes=64)
-            grouped_tile = chunk_pool.tile([P, PASSES, CHUNK, PACK], BF16, align_bytes=64)
-            codes_tile = chunk_pool.tile([P, PASSES, CHUNK], U32, align_bytes=64)
-            scales_tile = chunk_pool.tile([P, PASSES, CHUNK], U8, align_bytes=64)
-            wide.append(wide_tile)
-            grouped.append(grouped_tile)
-            codes.append(codes_tile)
-            scales.append(scales_tile)
+        regions_grouped = [keep.tile([P, HALF, PACK], BF16, align_bytes=64, name=f"regions_grouped_{h}") for h in range(2)]
+        regions_codes = [keep.tile([P, HALF], U32, align_bytes=64, name=f"regions_codes_{h}") for h in range(2)]
+        regions_scales = [keep.tile([P, HALF], U8, align_bytes=64, name=f"regions_scales_{h}") for h in range(2)]
 
         identity = keep.tile([P, P], F32)
         one = keep.tile([P, 1], F32)
 
-        nc.gpsimd.memset(d_scales[:].rearrange("p g n -> p (g n)").bitcast(I32), 0)
-        nc.gpsimd.memset(p_scales[:].rearrange("p g n -> p (g n)").bitcast(I32), 0)
         nc.vector.memset(one[:], 1.0)
+        nc.vector.memset(d_scales[:].rearrange("p g n -> p (g n)").bitcast(I32), 0)
+        nc.gpsimd.memset(p_scales[:].rearrange("p g n -> p (g n)").bitcast(I32), 0)
         make_identity(nc, identity[:])
 
-        def load_regions(j):
-            tile, lo = region_loads[j]
-            nc.sync.dma_start(
-                out=tile[:], in_=regions_new.rearrange("(p t) n -> p t n", t=PACK)[:, :, lo : lo + tile[:].shape[2]]
-            )
+        def find(ranges, column):
+            for n, (lo, hi) in enumerate(ranges):
+                if lo <= column < hi:
+                    return n, column - lo
 
-        def load_new(half):
-            nc.sync.dma_start(
-                out=new_raw[half][:],
-                in_=seeds_new.rearrange("(p t) n -> p t n", t=PACK)[:, :, HALF * half : HALF * half + HALF],
-            )
+        def load_regions(n):
+            lo, hi = REGION_RANGES[n]
+            nc.sync.dma_start(out=regions_raw[n][:], in_=regions_new.rearrange("(p t) n -> p t n", t=PACK)[:, :, lo:hi])
 
-        def load_old(g, half):
+        def load_new(n):
+            lo, hi = NEW_RANGES[n]
+            nc.sync.dma_start(out=new_raw[n][:], in_=seeds_new.rearrange("(p t) n -> p t n", t=PACK)[:, :, lo:hi])
+
+        def load_old(g, n):
+            lo, hi = OLD_RANGES[n]
             rows = seeds_old_bytes.rearrange("(g p t) n -> g p t n", p=P, t=PACK)[g]
-            nc.sync.dma_start(out=old_bytes[g, half][:], in_=rows[:, :, HALF * half : HALF * half + HALF])
+            nc.sync.dma_start(out=old_bytes[g][n][:], in_=rows[:, :, lo:hi])
 
         def load_d(half):
             words = old_words.rearrange("g p w -> p g w")
@@ -135,162 +112,171 @@ def tile_pooled_fisher_connectivity_s3_kernel(
         nc.scalar.dma_start(
             out=old_factor[:], in_=seeds_old_scale.rearrange("(g p t) o -> p g (t o)", p=P, t=PACK)
         )
+        nc.scalar.dma_start(out=weights[:], in_=precision.rearrange("(h p t) -> p h t", p=P, t=PACK))
         load_old(0, 0)
         load_regions(0)
+        load_old(1, 0)
         load_regions(1)
         load_scale_rows(d_scales, old_scales, GROUPS)
-        load_old(1, 0)
         load_old(2, 0)
-        load_new(0)
         load_d(0)
-        load_d(1)
+        load_new(0)
         load_regions(2)
+        load_d(1)
+        load_new(1)
         for g in range(GROUPS):
             load_old(g, 1)
-        load_new(1)
+        load_new(2)
         nc.sync.dma_start(out=p_words[:], in_=net_words.rearrange("g p w -> p g w"))
         load_scale_rows(p_scales, net_scales, 2)
-        nc.sync.dma_start(out=weights[:], in_=precision.rearrange("(h p t) -> p h t", p=P, t=PACK))
 
         nc.scalar.activation(out=one[:], in_=one[:], func=ACT.Ln)
 
-        def widen(c, k):
-            cols = slice(CHUNK * (c % 2), CHUNK * (c % 2) + CHUNK)
-            for t in range(PACK):
-                nc.scalar.activation(
-                    out=wide[c][:, k - 1, t, :],
-                    in_=old_bytes[k - 1, c // 2][:, t, cols].bitcast(FP8),
-                    func=ACT.Copy,
-                    scale=old_factor[:, k - 1, t : t + 1],
-                )
+        wide = {}
 
-        def interleave(copy, dst, src):
+        def widen(i, g, engine, planes=range(PACK)):
+            if (i, g) not in wide:
+                wide[i, g] = work.tile([P, PACK, P], BF16, align_bytes=64, name="wide", bufs=4 * GROUPS)
+            n, lo = find(OLD_RANGES, P * i)
+            for t in planes:
+                src = old_bytes[g][n][:, t, lo : lo + P].bitcast(FP8)
+                factor = old_factor[:, g, t : t + 1]
+                if engine == "scalar":
+                    nc.scalar.activation(out=wide[i, g][:, t, :], in_=src, func=ACT.Copy, scale=factor)
+                else:
+                    nc.vector.tensor_scalar(out=wide[i, g][:, t, :], in0=src, scalar1=factor, scalar2=None, op0=ALU.mult)
+
+        def interleave(dst, src, copy=nc.vector.tensor_copy):
             copy(out=dst, in_=src.rearrange("p t n -> p n t"))
 
-        def interleave_regions(j):
-            tile, lo = region_loads[j]
-            interleave(nc.vector.tensor_copy, regions_grouped[:, lo : lo + tile[:].shape[2], :], tile[:])
+        def interleave_regions(n, copy=nc.vector.tensor_copy):
+            lo, hi = REGION_RANGES[n]
+            h = lo // HALF
+            interleave(regions_grouped[h][:, lo - HALF * h : hi - HALF * h, :], regions_raw[n][:], copy)
 
         def quantise_regions(h):
-            cols = slice(HALF * h, HALF * h + HALF)
             nc.vector.quantize_mx(
-                out=regions_codes[:, cols].bitcast(FP8X4),
-                scales=regions_scales[:, cols],
-                in_=regions_grouped[:, cols, :].rearrange("p n t -> p (n t)"),
+                out=regions_codes[h][:].bitcast(FP8X4),
+                scales=regions_scales[h][:],
+                in_=regions_grouped[h][:].rearrange("p n t -> p (n t)"),
             )
 
-        def interleave_seeds(c, k, copy=nc.vector.tensor_copy):
-            if k == 0:
-                src = new_raw[c // 2][:, :, CHUNK * (c % 2) : CHUNK * (c % 2) + CHUNK]
-            else:
-                src = wide[c][:, k - 1, :, :]
-            interleave(copy, grouped[c][:, k, :, :], src)
+        grouped, codes, scales = {}, {}, {}
 
-        def quantise_seeds(c, first, last):
+        def interleave_seeds(i, k, copy=nc.vector.tensor_copy):
+            if i not in grouped:
+                grouped[i] = work.tile([P, PASSES, P, PACK], BF16, align_bytes=64, name="grouped")
+                codes[i] = work.tile([P, PASSES, P], U32, align_bytes=64, name="codes")
+                scales[i] = work.tile([P, PASSES, P], U8, align_bytes=64, name="scales")
+            if k == 0:
+                n, lo = find(NEW_RANGES, P * i)
+                src = new_raw[n][:, :, lo : lo + P]
+            else:
+                src = wide[i, k - 1][:]
+            interleave(grouped[i][:, k, :, :], src, copy)
+
+        def quantise_seeds(i, first, last):
             nc.vector.quantize_mx(
-                out=codes[c][:, first:last, :].rearrange("p k n -> p (k n)").bitcast(FP8X4),
-                scales=scales[c][:, first:last, :].rearrange("p k n -> p (k n)"),
-                in_=grouped[c][:, first:last, :, :].rearrange("p k n t -> p (k n t)"),
+                out=codes[i][:, first:last, :].rearrange("p k n -> p (k n)").bitcast(FP8X4),
+                scales=scales[i][:, first:last, :].rearrange("p k n -> p (k n)"),
+                in_=grouped[i][:, first:last, :, :].rearrange("p k n t -> p (k n t)"),
             )
 
         r = {}
 
-        def take_banks(i):
-            for h in range(2):
-                r_bank = psum_r.tile([P, HALF], F32)
-                r[i, h] = r_bank
-
-        def correlate(tiles, h):
+        def correlate_pair(units):
+            for i, h in units:
+                r[i, h] = psum.tile([P, HALF], F32, name=f"bank_{len(r) % 4}")
             for n, k in enumerate(PASS_ORDER):
-                if k == 0:
-                    moving = regions_codes[:, HALF * h : HALF * h + HALF].bitcast(FP8X4)
-                    moving_scale = regions_scales[:, HALF * h : HALF * h + HALF]
-                else:
-                    moving = d_words[h][:, k - 1, :].bitcast(FP4X4)
-                    moving_scale = d_scales[:, k - 1, HALF * h : HALF * h + HALF]
-                for i in tiles:
-                    c, j = divmod(i, CHUNK // P)
-                    cols = slice(P * j, P * j + P)
+                for i, h in units:
+                    if k == 0:
+                        moving = regions_codes[h][:].bitcast(FP8X4)
+                        moving_scale = regions_scales[h][:]
+                    else:
+                        moving = d_words[h][:, k - 1, :].bitcast(FP4X4)
+                        moving_scale = d_scales[:, k - 1, HALF * h : HALF * h + HALF]
                     nc.tensor.matmul_mx(
                         out=r[i, h][:],
-                        lhsT=codes[c][:, k, cols].bitcast(FP8X4),
-                        lhsT_scale=scales[c][:, k, cols],
+                        lhsT=codes[i][:, k, :].bitcast(FP8X4),
+                        lhsT_scale=scales[i][:, k, :],
                         rhs=moving,
                         rhs_scale=moving_scale,
                         start=(n == 0),
                         stop=(n == PASSES - 1),
                     )
 
+        def correlate(i, h):
+            correlate_pair(((i, h),))
+
         ln_plus, ln_minus, difference = {}, {}, {}
 
-        def take_logarithms(i, h):
-            if h == 0:
-                ln_plus_tile = work.tile([P, 2, PACK, P], F32)
-                ln_minus_tile = work.tile([P, 2, PACK, P], F32)
-                ln_plus[i], ln_minus[i] = ln_plus_tile, ln_minus_tile
-            by_t = r[i, h][:].rearrange("s (p t) -> s t p", t=PACK)
-            nc.scalar.activation(out=ln_plus[i][:, h], in_=by_t, func=ACT.Ln, bias=1.0, scale=1.0)
-            nc.scalar.activation(out=ln_minus[i][:, h], in_=by_t, func=ACT.Ln, bias=1.0, scale=-1.0)
+        def take_logarithms(i, h, planes=slice(0, PACK)):
+            if planes.start == 0:
+                ln_plus[i, h] = work.tile([P, PACK, P], F32, name="ln_plus", bufs=4)
+                ln_minus[i, h] = work.tile([P, PACK, P], F32, name="ln_minus", bufs=4)
+            by_t = r[i, h][:].rearrange("s (p t) -> s t p", t=PACK)[:, planes, :]
+            nc.scalar.activation(out=ln_minus[i, h][:, planes, :], in_=by_t, func=ACT.Ln, bias=1.0, scale=-1.0)
+            nc.scalar.activation(out=ln_plus[i, h][:, planes, :], in_=by_t, func=ACT.Ln, bias=1.0, scale=1.0)
 
-        def form_difference(i, h):
-            if h == 0:
-                difference_tile = work.tile([P, 2, PACK, P], F32)
-                difference[i] = difference_tile
-            if i in PSUM_DIFFERENCE:
+        def form_difference(i, h, planes=slice(0, PACK)):
+            if planes.start == 0:
+                difference[i, h] = work.tile([P, PACK, P], F32, name="difference", bufs=4)
+            dst = difference[i, h][:, planes, :]
+            if (i, h) in PSUM_DIFFERENCE:
                 nc.vector.tensor_scalar(
-                    out=difference[i][:, h], in0=ln_minus[i][:, h], scalar1=-1.0, scalar2=None, op0=ALU.mult
+                    out=dst, in0=ln_minus[i, h][:, planes, :], scalar1=-1.0, scalar2=None, op0=ALU.mult
                 )
             else:
                 nc.vector.tensor_tensor(
-                    out=difference[i][:, h], in0=ln_plus[i][:, h], in1=ln_minus[i][:, h], op=ALU.subtract
+                    out=dst, in0=ln_plus[i, h][:, planes, :], in1=ln_minus[i, h][:, planes, :], op=ALU.subtract
                 )
 
         turned = {}
 
-        def turn(i, h):
-            turned_bank = psum_turn.tile([P, PACK, P], F32)
-            turned[i, h] = turned_bank
-            parts = (ln_plus[i], difference[i]) if i in PSUM_DIFFERENCE else (difference[i],)
-            for t in range(PACK):
+        def turn(i, h, bank, planes=slice(0, PACK)):
+            if planes.start == 0:
+                turned[i, h] = psum.tile([P, PACK, P], F32, name=f"bank_{bank}")
+            parts = (difference[i, h], ln_plus[i, h]) if (i, h) in PSUM_DIFFERENCE else (difference[i, h],)
+            for t in range(planes.start, planes.stop):
                 for n, part in enumerate(parts):
                     nc.tensor.matmul(
-                        turned_bank[:, t, :],
-                        lhsT=part[:, h, t, :],
+                        turned[i, h][:, t, :],
+                        lhsT=part[:, t, :],
                         rhs=identity[:],
                         start=(n == 0),
                         stop=(n == len(parts) - 1),
                         is_transpose=True,
                     )
 
-        z_codes, z_scales = {}, {}
+        z_grouped, z_codes, z_scales = {}, {}, {}
 
-        def weigh_and_quantise(i):
-            z_grouped = work.tile([P, 2, P, PACK], BF16, align_bytes=64)
-            z_codes_tile = work.tile([P, 2, P], U32, align_bytes=64)
-            z_scales_tile = work.tile([P, 2, P], U8, align_bytes=64)
-            z_codes[i], z_scales[i] = z_codes_tile, z_scales_tile
-            for h in range(2):
-                nc.vector.tensor_tensor(
-                    out=z_grouped[:, h, :, :],
-                    in0=turned[i, h][:].rearrange("p t n -> p n t"),
-                    in1=weights[:, h, :].unsqueeze(1).to_broadcast([P, P, PACK]),
-                    op=ALU.mult,
-                )
-            for h in range(2):
-                nc.vector.quantize_mx(
-                    out=z_codes_tile[:, h, :].bitcast(FP8X4),
-                    scales=z_scales_tile[:, h, :],
-                    in_=z_grouped[:, h, :, :].rearrange("p n t -> p (n t)"),
-                )
+        def weigh(i, h):
+            if h == 0:
+                z_grouped[i] = work.tile([P, 2, P, PACK], BF16, align_bytes=64, name="z_grouped")
+                z_codes[i] = work.tile([P, 2, P], U32, align_bytes=64, name="z_codes")
+                z_scales[i] = work.tile([P, 2, P], U8, align_bytes=64, name="z_scales")
+            nc.vector.tensor_tensor(
+                out=z_grouped[i][:, h, :, :],
+                in0=turned[i, h][:].rearrange("p t n -> p n t"),
+                in1=weights[:, h, :].unsqueeze(1).to_broadcast([P, P, PACK]),
+                op=ALU.mult,
+            )
+
+        def quantise_z(i, first, last):
+            nc.vector.quantize_mx(
+                out=z_codes[i][:, first:last, :].rearrange("p h n -> p (h n)").bitcast(FP8X4),
+                scales=z_scales[i][:, first:last, :].rearrange("p h n -> p (h n)"),
+                in_=z_grouped[i][:, first:last, :, :].rearrange("p h n t -> p (h n t)"),
+            )
 
         out_bank = {}
 
-        def project(i):
-            out_bank_tile = psum_out.tile([P, E], F32)
-            out_bank[i] = out_bank_tile
-            for h in range(2):
+        def project(i, bank, halves=(0, 1)):
+            for h in halves:
+                if h == 0:
+                    out_bank[i] = psum.tile([P, E], F32, name=f"bank_{bank}")
                 nc.tensor.matmul_mx(
-                    out=out_bank_tile[:],
+                    out=out_bank[i][:],
                     lhsT=z_codes[i][:, h, :].bitcast(FP8X4),
                     lhsT_scale=z_scales[i][:, h, :],
                     rhs=p_words[:, h, :].bitcast(FP4X4),
@@ -299,79 +285,114 @@ def tile_pooled_fisher_connectivity_s3_kernel(
                     stop=(h == 1),
                 )
 
-        def store(i):
-            result = work.tile([P, E], F32)
-            nc.scalar.copy(out=result[:], in_=out_bank[i][:])
+        def store(i, copy):
+            result = work.tile([P, E], F32, bufs=4)
+            copy(out=result[:], in_=out_bank[i][:])
             nc.sync.dma_start(out=out[P * i : P * i + P, :], in_=result[:])
 
-        def store_in_halves(i):
-            result_a = work.tile([P, E // 2], F32)
-            result_b = work.tile([P, E // 2], F32)
-            nc.scalar.copy(out=result_a[:], in_=out_bank[i][:, : E // 2])
-            nc.vector.tensor_copy(out=result_b[:], in_=out_bank[i][:, E // 2 :])
-            nc.sync.dma_start(out=out[P * i : P * i + P, : E // 2], in_=result_a[:])
-            nc.sync.dma_start(out=out[P * i : P * i + P, E // 2 :], in_=result_b[:])
-
-        for k in range(1, PASSES):
-            widen(0, k)
-            widen(1, k)
-        widen(2, 1)
-        widen(3, 1)
-        interleave_regions(0)
-        interleave_regions(1)
-        quantise_regions(0)
+        widen(0, 0, "vector")
+        widen(1, 0, "scalar")
         interleave_seeds(0, 1)
-        interleave_seeds(0, 2)
+        widen(2, 0, "scalar")
+        for g in (1, 2):
+            widen(0, g, "scalar")
+            widen(1, g, "scalar")
+            if g == 1:
+                widen(2, g, "scalar")
+        interleave_regions(0)
+        interleave_seeds(1, 1)
         quantise_seeds(0, 1, 2)
-        interleave_seeds(0, 0)
-        quantise_seeds(0, 2, 3)
-        interleave_seeds(1, 0)
+        interleave_seeds(0, 2)
+        quantise_seeds(1, 1, 2)
+        interleave_seeds(1, 2)
+        interleave_regions(1)
+        interleave_seeds(2, 1)
+        quantise_regions(0)
         interleave_seeds(0, 3)
+        interleave_seeds(1, 3)
+        quantise_seeds(0, 2, 4)
+        interleave_seeds(0, 0)
+        quantise_seeds(1, 2, 4)
+        interleave_seeds(1, 0)
         quantise_seeds(0, 0, 1)
-        quantise_seeds(0, 3, 4)
+        interleave_seeds(2, 2)
+        quantise_seeds(1, 0, 1)
+        correlate_pair(((0, 0), (1, 0)))
+        widen(2, 2, "scalar")
+        widen(3, 0, "scalar")
+        widen(3, 1, "scalar")
+        widen(3, 2, "scalar")
         interleave_regions(2)
+        interleave_seeds(2, 3)
         quantise_regions(1)
-        take_banks(0)
-        take_banks(1)
-        correlate((0, 1), 0)
-        correlate((0, 1), 1)
+        correlate_pair(((0, 1), (1, 1)))
 
-        for i in range(TILES):
-            take_logarithms(i, 0)
-            for c, k in WIDEN.get(i, ()):
-                widen(c, k)
-            take_logarithms(i, 1)
-            if i > 1:
-                store(i - 2)
-            for c, k in SCALAR_INTERLEAVE.get(i, ()):
-                interleave_seeds(c, k, nc.scalar.copy)
-            if i == 0:
-                interleave_seeds(1, 1)
-                quantise_seeds(1, 0, 2)
-                interleave_seeds(1, 2)
-            for c, k in BEFORE_DIFFERENCE.get(i, ()):
-                interleave_seeds(c, k)
-            form_difference(i, 0)
-            form_difference(i, 1)
-            if i - 1 in WEIGH_LATE:
-                weigh_and_quantise(i - 1)
-            turn(i, 0)
-            turn(i, 1)
-            for c, k in AFTER_TURN.get(i, ()):
-                interleave_seeds(c, k)
-            if i == 0:
-                quantise_seeds(1, 2, 4)
-                interleave_seeds(2, 1)
-            if i in QUANTISE_CHUNK:
-                quantise_seeds(QUANTISE_CHUNK[i], 0, PASSES)
-            if i not in WEIGH_LATE:
-                weigh_and_quantise(i)
-            if i > 0:
-                project(i - 1)
-            if i + 2 < TILES:
-                take_banks(i + 2)
-                correlate((i + 2,), 0)
-                correlate((i + 2,), 1)
-        store(TILES - 2)
-        project(TILES - 1)
-        store_in_halves(TILES - 1)
+        steps = [((0, 0), (1, 0)), ((0, 1), (1, 1))] + [((i, 0), (i, 1)) for i in range(2, TILES)]
+        last = TILES - 1
+        for s in range(-1, last - 1):
+            projected = {2: (0, 1), last - 2: ()}.get(s, (s - 1,)) if s >= 2 else ()
+            if s >= 0:
+                for n, (i, h) in enumerate(steps[s]):
+                    turn(i, h, 4 + n)
+            for i, h in steps[s + 1]:
+                take_logarithms(i, h)
+            if s >= 0:
+                for i, h in steps[s]:
+                    weigh(i, h)
+            for n, (i, h) in enumerate(steps[s + 1]):
+                form_difference(i, h)
+                if s == -1 and n == 0:
+                    interleave_seeds(2, 0)
+            for i in projected:
+                project(i, 6 + i % 2)
+            if s >= 0:
+                correlate(s + 2, 0)
+                correlate(s + 2, 1)
+            if s + 4 < TILES:
+                if s >= 0:
+                    widen(s + 4, 0, "scalar")
+                    widen(s + 4, 1, "scalar")
+                    widen(s + 4, 2, "scalar", range(2))
+            if 3 <= s + 3 < TILES:
+                if s >= 1:
+                    widen(s + 3, 2, "vector", range(2, PACK))
+                for k in PASS_ORDER:
+                    interleave_seeds(s + 3, k, nc.scalar.copy if (s + 3, k) in () else nc.vector.tensor_copy)
+            for i in projected:
+                store(i, nc.scalar.copy)
+            if s >= 0:
+                if s < 2:
+                    for i, h in steps[s]:
+                        quantise_z(i, h, h + 1)
+                else:
+                    quantise_z(s, 0, 2)
+            if s + 3 < TILES:
+                quantise_seeds(s + 3, 0, PASSES)
+        first, second = slice(0, 2), slice(2, 4)
+        project(last - 3, 6)
+        take_logarithms(last, 0)
+        turn(last - 1, 0, 4)
+        turn(last - 1, 1, 5)
+        project(last - 2, 7)
+        form_difference(last, 0)
+        take_logarithms(last, 1, first)
+        take_logarithms(last, 1, second)
+        weigh(last - 1, 0)
+        turn(last, 0, 0)
+        form_difference(last, 1, first)
+        weigh(last - 1, 1)
+        form_difference(last, 1, second)
+        turn(last, 1, 1, first)
+        turn(last, 1, 1, second)
+        store(last - 3, nc.scalar.copy)
+        store(last - 2, nc.scalar.copy)
+        weigh(last, 0)
+        quantise_z(last - 1, 0, 2)
+        weigh(last, 1)
+        quantise_z(last, 0, 1)
+        project(last - 1, 2)
+        project(last, 3, (0,))
+        quantise_z(last, 1, 2)
+        project(last, 3, (1,))
+        store(last - 1, nc.scalar.copy)
+        store(last, nc.vector.tensor_copy)

@@ -114,11 +114,11 @@ def tile_pooled_fisher_connectivity_s3_kernel(
         )
         nc.scalar.dma_start(out=weights[:], in_=precision.rearrange("(h p t) -> p h t", p=P, t=PACK))
         load_old(0, 0)
-        load_regions(0)
         load_old(1, 0)
+        load_regions(0)
+        load_old(2, 0)
         load_regions(1)
         load_scale_rows(d_scales, old_scales, GROUPS)
-        load_old(2, 0)
         load_d(0)
         load_new(0)
         load_regions(2)
@@ -132,19 +132,19 @@ def tile_pooled_fisher_connectivity_s3_kernel(
 
         nc.scalar.activation(out=one[:], in_=one[:], func=ACT.Ln)
 
-        wide = {}
+        wide = [
+            keep.tile([P, PACK, GROUPS, CHUNK], BF16, align_bytes=64, name=f"wide_{c}") for c in range(M // CHUNK)
+        ]
 
-        def widen(i, g, engine, planes=range(PACK)):
-            if (i, g) not in wide:
-                wide[i, g] = work.tile([P, PACK, P], BF16, align_bytes=64, name="wide", bufs=4 * GROUPS)
-            n, lo = find(OLD_RANGES, P * i)
+        def widen(c, g, engine, planes=range(PACK), cols=slice(0, CHUNK)):
+            n, lo = find(OLD_RANGES, CHUNK * c)
             for t in planes:
-                src = old_bytes[g][n][:, t, lo : lo + P].bitcast(FP8)
+                src = old_bytes[g][n][:, t, lo + cols.start : lo + cols.stop].bitcast(FP8)
                 factor = old_factor[:, g, t : t + 1]
                 if engine == "scalar":
-                    nc.scalar.activation(out=wide[i, g][:, t, :], in_=src, func=ACT.Copy, scale=factor)
+                    nc.scalar.activation(out=wide[c][:, t, g, cols], in_=src, func=ACT.Copy, scale=factor)
                 else:
-                    nc.vector.tensor_scalar(out=wide[i, g][:, t, :], in0=src, scalar1=factor, scalar2=None, op0=ALU.mult)
+                    nc.vector.tensor_scalar(out=wide[c][:, t, g, cols], in0=src, scalar1=factor, scalar2=None, op0=ALU.mult)
 
         def interleave(dst, src, copy=nc.vector.tensor_copy):
             copy(out=dst, in_=src.rearrange("p t n -> p n t"))
@@ -172,8 +172,35 @@ def tile_pooled_fisher_connectivity_s3_kernel(
                 n, lo = find(NEW_RANGES, P * i)
                 src = new_raw[n][:, :, lo : lo + P]
             else:
-                src = wide[i, k - 1][:]
+                c, j = divmod(i, CHUNK // P)
+                src = wide[c][:, :, k - 1, P * j : P * j + P]
             interleave(grouped[i][:, k, :, :], src, copy)
+
+        first_grouped = keep.tile([P, PASSES, CHUNK, PACK], BF16, align_bytes=64)
+        first_codes = keep.tile([P, PASSES, CHUNK], U32, align_bytes=64)
+        first_scales = keep.tile([P, PASSES, CHUNK], U8, align_bytes=64)
+
+        def interleave_first(k):
+            interleave(first_grouped[:, k, :, :], new_raw[0][:] if k == 0 else wide[0][:, :, k - 1, :])
+
+        def quantise_first(k):
+            nc.vector.quantize_mx(
+                out=first_codes[:, k, :].bitcast(FP8X4),
+                scales=first_scales[:, k, :],
+                in_=first_grouped[:, k, :, :].rearrange("p n t -> p (n t)"),
+            )
+
+        def stationary(i, k):
+            if P * i < CHUNK:
+                return first_codes[:, k, P * i : P * i + P], first_scales[:, k, P * i : P * i + P]
+            return codes[i][:, k, :], scales[i][:, k, :]
+
+        def interleave_old(i):
+            c, j = divmod(i, CHUNK // P)
+            nc.vector.tensor_copy(
+                out=grouped[i][:, 1:, :, :].rearrange("p g (a n) t -> p a g n t", a=2),
+                in_=wide[c][:, :, :, P * j : P * j + P].rearrange("p t g (a n) -> p a g n t", a=2),
+            )
 
         def quantise_seeds(i, first, last):
             nc.vector.quantize_mx(
@@ -197,8 +224,8 @@ def tile_pooled_fisher_connectivity_s3_kernel(
                         moving_scale = d_scales[:, k - 1, HALF * h : HALF * h + HALF]
                     nc.tensor.matmul_mx(
                         out=r[i, h][:],
-                        lhsT=codes[i][:, k, :].bitcast(FP8X4),
-                        lhsT_scale=scales[i][:, k, :],
+                        lhsT=stationary(i, k)[0].bitcast(FP8X4),
+                        lhsT_scale=stationary(i, k)[1],
                         rhs=moving,
                         rhs_scale=moving_scale,
                         start=(n == 0),
@@ -208,43 +235,44 @@ def tile_pooled_fisher_connectivity_s3_kernel(
         def correlate(i, h):
             correlate_pair(((i, h),))
 
+        steps = [((0, 0), (1, 0)), ((0, 1), (1, 1))] + [((i, 0), (i, 1)) for i in range(2, TILES)]
         ln_plus, ln_minus, difference = {}, {}, {}
 
-        def take_logarithms(i, h, planes=slice(0, PACK)):
-            if planes.start == 0:
-                ln_plus[i, h] = work.tile([P, PACK, P], F32, name="ln_plus", bufs=4)
-                ln_minus[i, h] = work.tile([P, PACK, P], F32, name="ln_minus", bufs=4)
-            by_t = r[i, h][:].rearrange("s (p t) -> s t p", t=PACK)[:, planes, :]
-            nc.scalar.activation(out=ln_minus[i, h][:, planes, :], in_=by_t, func=ACT.Ln, bias=1.0, scale=-1.0)
-            nc.scalar.activation(out=ln_plus[i, h][:, planes, :], in_=by_t, func=ACT.Ln, bias=1.0, scale=1.0)
+        def take_logarithms(s, n, planes=slice(0, PACK)):
+            if n == 0 and planes.start == 0:
+                ln_plus[s] = work.tile([P, 2, PACK, P], F32, name="ln_plus")
+                ln_minus[s] = work.tile([P, 2, PACK, P], F32, name="ln_minus")
+                difference[s] = work.tile([P, 2, PACK, P], F32, name="difference")
+            by_t = r[steps[s][n]][:].rearrange("s (p t) -> s t p", t=PACK)[:, planes, :]
+            nc.scalar.activation(out=ln_minus[s][:, n, planes, :], in_=by_t, func=ACT.Ln, bias=1.0, scale=-1.0)
+            nc.scalar.activation(out=ln_plus[s][:, n, planes, :], in_=by_t, func=ACT.Ln, bias=1.0, scale=1.0)
 
-        def form_difference(i, h, planes=slice(0, PACK)):
-            if planes.start == 0:
-                difference[i, h] = work.tile([P, PACK, P], F32, name="difference", bufs=4)
-            dst = difference[i, h][:, planes, :]
-            if (i, h) in PSUM_DIFFERENCE:
+        def form_difference(s, units=slice(0, 2), planes=slice(0, PACK)):
+            dst = difference[s][:, units, planes, :]
+            if (s, units.start) in PSUM_DIFFERENCE:
                 nc.vector.tensor_scalar(
-                    out=dst, in0=ln_minus[i, h][:, planes, :], scalar1=-1.0, scalar2=None, op0=ALU.mult
+                    out=dst, in0=ln_minus[s][:, units, planes, :], scalar1=-1.0, scalar2=None, op0=ALU.mult
                 )
             else:
                 nc.vector.tensor_tensor(
-                    out=dst, in0=ln_plus[i, h][:, planes, :], in1=ln_minus[i, h][:, planes, :], op=ALU.subtract
+                    out=dst, in0=ln_plus[s][:, units, planes, :], in1=ln_minus[s][:, units, planes, :], op=ALU.subtract
                 )
 
         turned = {}
 
-        def turn(i, h, bank, planes=slice(0, PACK)):
+        def turn(s, n, bank, planes=slice(0, PACK)):
+            unit = steps[s][n]
             if planes.start == 0:
-                turned[i, h] = psum.tile([P, PACK, P], F32, name=f"bank_{bank}")
-            parts = (difference[i, h], ln_plus[i, h]) if (i, h) in PSUM_DIFFERENCE else (difference[i, h],)
+                turned[unit] = psum.tile([P, PACK, P], F32, name=f"bank_{bank}")
+            parts = (difference[s], ln_plus[s]) if (s, n) in PSUM_DIFFERENCE else (difference[s],)
             for t in range(planes.start, planes.stop):
-                for n, part in enumerate(parts):
+                for m, part in enumerate(parts):
                     nc.tensor.matmul(
-                        turned[i, h][:, t, :],
-                        lhsT=part[:, t, :],
+                        turned[unit][:, t, :],
+                        lhsT=part[:, n, t, :],
                         rhs=identity[:],
-                        start=(n == 0),
-                        stop=(n == len(parts) - 1),
+                        start=(m == 0),
+                        stop=(m == len(parts) - 1),
                         is_transpose=True,
                     )
 
@@ -252,9 +280,9 @@ def tile_pooled_fisher_connectivity_s3_kernel(
 
         def weigh(i, h):
             if h == 0:
-                z_grouped[i] = work.tile([P, 2, P, PACK], BF16, align_bytes=64, name="z_grouped")
-                z_codes[i] = work.tile([P, 2, P], U32, align_bytes=64, name="z_codes")
-                z_scales[i] = work.tile([P, 2, P], U8, align_bytes=64, name="z_scales")
+                z_grouped[i] = work.tile([P, 2, P, PACK], BF16, align_bytes=64, name="z_grouped", bufs=4)
+                z_codes[i] = work.tile([P, 2, P], U32, align_bytes=64, name="z_codes", bufs=4)
+                z_scales[i] = work.tile([P, 2, P], U8, align_bytes=64, name="z_scales", bufs=4)
             nc.vector.tensor_tensor(
                 out=z_grouped[i][:, h, :, :],
                 in0=turned[i, h][:].rearrange("p t n -> p n t"),
@@ -292,72 +320,55 @@ def tile_pooled_fisher_connectivity_s3_kernel(
 
         widen(0, 0, "vector")
         widen(1, 0, "scalar")
-        interleave_seeds(0, 1)
-        widen(2, 0, "scalar")
-        for g in (1, 2):
-            widen(0, g, "scalar")
-            widen(1, g, "scalar")
-            if g == 1:
-                widen(2, g, "scalar")
+        widen(0, 1, "scalar")
+        widen(0, 2, "scalar")
+        interleave_first(1)
         interleave_regions(0)
-        interleave_seeds(1, 1)
-        quantise_seeds(0, 1, 2)
-        interleave_seeds(0, 2)
-        quantise_seeds(1, 1, 2)
-        interleave_seeds(1, 2)
-        interleave_regions(1)
-        interleave_seeds(2, 1)
+        quantise_first(1)
+        interleave_first(2)
+        interleave_regions(1, nc.scalar.copy)
+        quantise_first(2)
+        interleave_first(3)
+        interleave_first(0)
+        quantise_first(3)
         quantise_regions(0)
-        interleave_seeds(0, 3)
-        interleave_seeds(1, 3)
-        quantise_seeds(0, 2, 4)
-        interleave_seeds(0, 0)
-        quantise_seeds(1, 2, 4)
-        interleave_seeds(1, 0)
-        quantise_seeds(0, 0, 1)
-        interleave_seeds(2, 2)
-        quantise_seeds(1, 0, 1)
+        quantise_first(0)
         correlate_pair(((0, 0), (1, 0)))
-        widen(2, 2, "scalar")
-        widen(3, 0, "scalar")
-        widen(3, 1, "scalar")
-        widen(3, 2, "scalar")
+        widen(1, 1, "scalar")
+        widen(1, 2, "scalar")
         interleave_regions(2)
-        interleave_seeds(2, 3)
+        interleave_seeds(2, 0)
         quantise_regions(1)
         correlate_pair(((0, 1), (1, 1)))
 
-        steps = [((0, 0), (1, 0)), ((0, 1), (1, 1))] + [((i, 0), (i, 1)) for i in range(2, TILES)]
         last = TILES - 1
         for s in range(-1, last - 1):
-            projected = {2: (0, 1), last - 2: ()}.get(s, (s - 1,)) if s >= 2 else ()
+            projected = {2: (0, 1), 3: (2,), 4: (3,)}.get(s, ())
             if s >= 0:
-                for n, (i, h) in enumerate(steps[s]):
-                    turn(i, h, 4 + n)
-            for i, h in steps[s + 1]:
-                take_logarithms(i, h)
+                turn(s, 0, 4)
+                turn(s, 1, 5)
+            take_logarithms(s + 1, 0)
+            take_logarithms(s + 1, 1)
             if s >= 0:
                 for i, h in steps[s]:
                     weigh(i, h)
-            for n, (i, h) in enumerate(steps[s + 1]):
-                form_difference(i, h)
-                if s == -1 and n == 0:
-                    interleave_seeds(2, 0)
+            c, j = divmod(s + 5, 2)
+            jobs = [(g, t) for g in range(GROUPS) for t in range(PACK)][6 * j : 6 * j + 6] if c < M // CHUNK else []
+            for g, t in jobs[: 1]:
+                widen(c, g, "vector", (t,))
+            form_difference(s + 1)
+            if s < 0:
+                interleave_old(2)
             for i in projected:
                 project(i, 6 + i % 2)
             if s >= 0:
                 correlate(s + 2, 0)
                 correlate(s + 2, 1)
-            if s + 4 < TILES:
-                if s >= 0:
-                    widen(s + 4, 0, "scalar")
-                    widen(s + 4, 1, "scalar")
-                    widen(s + 4, 2, "scalar", range(2))
+            for g, t in jobs[1 :]:
+                widen(c, g, "scalar", (t,))
             if 3 <= s + 3 < TILES:
-                if s >= 1:
-                    widen(s + 3, 2, "vector", range(2, PACK))
-                for k in PASS_ORDER:
-                    interleave_seeds(s + 3, k, nc.scalar.copy if (s + 3, k) in () else nc.vector.tensor_copy)
+                interleave_seeds(s + 3, 0, nc.scalar.copy if s + 3 in (6,7) else nc.vector.tensor_copy)
+                interleave_old(s + 3)
             for i in projected:
                 store(i, nc.scalar.copy)
             if s >= 0:
@@ -374,14 +385,14 @@ def tile_pooled_fisher_connectivity_s3_kernel(
         turn(last - 1, 0, 4)
         turn(last - 1, 1, 5)
         project(last - 2, 7)
-        form_difference(last, 0)
+        form_difference(last, slice(0, 1))
         take_logarithms(last, 1, first)
         take_logarithms(last, 1, second)
         weigh(last - 1, 0)
         turn(last, 0, 0)
-        form_difference(last, 1, first)
+        form_difference(last, slice(1, 2), first)
         weigh(last - 1, 1)
-        form_difference(last, 1, second)
+        form_difference(last, slice(1, 2), second)
         turn(last, 1, 1, first)
         turn(last, 1, 1, second)
         store(last - 3, nc.scalar.copy)

@@ -29,7 +29,7 @@ PASS_ORDER = (1, 2, 3, 0)
 OLD_RANGES = ((0, 512), (512, 1024))
 NEW_RANGES = ((0, 256), (256, 512), (512, 1024))
 REGION_RANGES = ((0, 256), (256, 512), (512, 1024))
-PSUM_DIFFERENCE = [(i, h) for i in range(TILES) for h in range(2) if (i, h) not in ((6,0),(6,1),(7,0))]
+PSUM_DIFFERENCE = [(i, h) for i in range(TILES) for h in range(2) if (i, h) not in ((3,0),(3,1),(4,0),(4,1),(5,0),(5,1),(6,0),(6,1),(7,0),)]
 
 
 def tile_pooled_fisher_connectivity_s3_kernel(
@@ -149,6 +149,9 @@ def tile_pooled_fisher_connectivity_s3_kernel(
         def interleave(dst, src, copy=nc.vector.tensor_copy):
             copy(out=dst, in_=src.rearrange("p t n -> p n t"))
 
+        def gpsimd_copy(out, in_):
+            nc.gpsimd.tensor_scalar(out=out, in0=in_, scalar1=1.0, scalar2=0.0, op0=ALU.mult, op1=ALU.add)
+
         def interleave_regions(n, copy=nc.vector.tensor_copy):
             lo, hi = REGION_RANGES[n]
             h = lo // HALF
@@ -165,7 +168,7 @@ def tile_pooled_fisher_connectivity_s3_kernel(
 
         def interleave_seeds(i, k, copy=nc.vector.tensor_copy):
             if i not in grouped:
-                grouped[i] = work.tile([P, PASSES, P, PACK], BF16, align_bytes=64, name="grouped")
+                grouped[i] = work.tile([P, PASSES, P, PACK], BF16, align_bytes=64, name="grouped", bufs=1)
                 codes[i] = work.tile([P, PASSES, P], U32, align_bytes=64, name="codes")
                 scales[i] = work.tile([P, PASSES, P], U8, align_bytes=64, name="scales")
             if k == 0:
@@ -195,11 +198,11 @@ def tile_pooled_fisher_connectivity_s3_kernel(
                 return first_codes[:, k, P * i : P * i + P], first_scales[:, k, P * i : P * i + P]
             return codes[i][:, k, :], scales[i][:, k, :]
 
-        def interleave_old(i):
+        def interleave_old(i, groups=slice(0, GROUPS)):
             c, j = divmod(i, CHUNK // P)
             nc.vector.tensor_copy(
-                out=grouped[i][:, 1:, :, :].rearrange("p g (a n) t -> p a g n t", a=2),
-                in_=wide[c][:, :, :, P * j : P * j + P].rearrange("p t g (a n) -> p a g n t", a=2),
+                out=grouped[i][:, 1 + groups.start : 1 + groups.stop, :, :].rearrange("p g (a n) t -> p a g n t", a=2),
+                in_=wide[c][:, :, groups, P * j : P * j + P].rearrange("p t g (a n) -> p a g n t", a=2),
             )
 
         def quantise_seeds(i, first, last):
@@ -263,12 +266,12 @@ def tile_pooled_fisher_connectivity_s3_kernel(
         def turn(s, n, bank, planes=slice(0, PACK)):
             unit = steps[s][n]
             if planes.start == 0:
-                turned[unit] = psum.tile([P, PACK, P], F32, name=f"bank_{bank}")
+                turned[unit] = psum.tile([P, P // 2, PACK, 2], F32, name=f"bank_{bank}")
             parts = (difference[s], ln_plus[s]) if (s, n) in PSUM_DIFFERENCE else (difference[s],)
             for t in range(planes.start, planes.stop):
                 for m, part in enumerate(parts):
                     nc.tensor.matmul(
-                        turned[unit][:, t, :],
+                        turned[unit][:, :, t, :],
                         lhsT=part[:, n, t, :],
                         rhs=identity[:],
                         start=(m == 0),
@@ -284,9 +287,9 @@ def tile_pooled_fisher_connectivity_s3_kernel(
                 z_codes[i] = work.tile([P, 2, P], U32, align_bytes=64, name="z_codes", bufs=4)
                 z_scales[i] = work.tile([P, 2, P], U8, align_bytes=64, name="z_scales", bufs=4)
             nc.vector.tensor_tensor(
-                out=z_grouped[i][:, h, :, :],
-                in0=turned[i, h][:].rearrange("p t n -> p n t"),
-                in1=weights[:, h, :].unsqueeze(1).to_broadcast([P, P, PACK]),
+                out=z_grouped[i][:, h, :, :].rearrange("p (n e) t -> p n t e", e=2),
+                in0=turned[i, h][:],
+                in1=weights[:, h, :].unsqueeze(1).unsqueeze(3).to_broadcast([P, P // 2, PACK, 2]),
                 op=ALU.mult,
             )
 
@@ -326,12 +329,12 @@ def tile_pooled_fisher_connectivity_s3_kernel(
         interleave_regions(0)
         quantise_first(1)
         interleave_first(2)
-        interleave_regions(1, nc.scalar.copy)
+        interleave_regions(1)
         quantise_first(2)
         interleave_first(3)
-        interleave_first(0)
-        quantise_first(3)
         quantise_regions(0)
+        quantise_first(3)
+        interleave_first(0)
         quantise_first(0)
         correlate_pair(((0, 0), (1, 0)))
         widen(1, 1, "scalar")
@@ -343,7 +346,7 @@ def tile_pooled_fisher_connectivity_s3_kernel(
 
         last = TILES - 1
         for s in range(-1, last - 1):
-            projected = {2: (0, 1), 3: (2,), 4: (3,)}.get(s, ())
+            projected = {2: (0,), 3: (1,), 4: (2,3)}.get(s, ())
             if s >= 0:
                 turn(s, 0, 4)
                 turn(s, 1, 5)
@@ -367,8 +370,12 @@ def tile_pooled_fisher_connectivity_s3_kernel(
             for g, t in jobs[1 :]:
                 widen(c, g, "scalar", (t,))
             if 3 <= s + 3 < TILES:
-                interleave_seeds(s + 3, 0, nc.scalar.copy if s + 3 in (6,7) else nc.vector.tensor_copy)
-                interleave_old(s + 3)
+                interleave_seeds(s + 3, 0, gpsimd_copy if s + 3 in range(8) else nc.vector.tensor_copy)
+                if s + 3 in (6,7):
+                    interleave_seeds(s + 3, GROUPS, nc.scalar.copy)
+                    interleave_old(s + 3, slice(0, GROUPS - 1))
+                else:
+                    interleave_old(s + 3)
             for i in projected:
                 store(i, nc.scalar.copy)
             if s >= 0:
@@ -380,16 +387,16 @@ def tile_pooled_fisher_connectivity_s3_kernel(
             if s + 3 < TILES:
                 quantise_seeds(s + 3, 0, PASSES)
         first, second = slice(0, 2), slice(2, 4)
-        project(last - 3, 6)
         take_logarithms(last, 0)
         turn(last - 1, 0, 4)
         turn(last - 1, 1, 5)
+        project(last - 3, 6)
         project(last - 2, 7)
         form_difference(last, slice(0, 1))
         take_logarithms(last, 1, first)
         take_logarithms(last, 1, second)
-        weigh(last - 1, 0)
         turn(last, 0, 0)
+        weigh(last - 1, 0)
         form_difference(last, slice(1, 2), first)
         weigh(last - 1, 1)
         form_difference(last, slice(1, 2), second)
@@ -397,13 +404,17 @@ def tile_pooled_fisher_connectivity_s3_kernel(
         turn(last, 1, 1, second)
         store(last - 3, nc.scalar.copy)
         store(last - 2, nc.scalar.copy)
-        weigh(last, 0)
         quantise_z(last - 1, 0, 2)
+        weigh(last, 0)
         weigh(last, 1)
-        quantise_z(last, 0, 1)
         project(last - 1, 2)
+        quantise_z(last, 0, 1)
         project(last, 3, (0,))
         quantise_z(last, 1, 2)
         project(last, 3, (1,))
         store(last - 1, nc.scalar.copy)
-        store(last, nc.vector.tensor_copy)
+        for half in range(2):
+            cols = slice(half * E // 2, (half + 1) * E // 2)
+            result_half = work.tile([P, E // 2], F32)
+            nc.vector.tensor_copy(out=result_half[:], in_=out_bank[last][:, cols])
+            nc.sync.dma_start(out=out[P * last : P * last + P, cols], in_=result_half[:])

@@ -24,12 +24,20 @@ PASSES = 1 + GROUPS
 HALF = 512
 CHUNK = 256
 TILES = M // P
+CHUNKS = M // CHUNK
+LAST = TILES - 1
 
 PASS_ORDER = (1, 2, 3, 0)
-OLD_RANGES = ((0, 512), (512, 1024))
-NEW_RANGES = ((0, 256), (256, 512), (512, 1024))
-REGION_RANGES = ((0, 256), (256, 512), (512, 1024))
-PSUM_DIFFERENCE = [(i, h) for i in range(TILES) for h in range(2) if (i, h) not in ((3,0),(3,1),(4,0),(4,1),(5,0),(5,1),(6,0),(6,1),(7,0),)]
+NEW_RANGES = ((0, CHUNK), (CHUNK, HALF), (HALF, M))
+
+STEPS = [((0, 0), (1, 0)), ((0, 1), (1, 1))] + [((i, 0), (i, 1)) for i in range(2, TILES)]
+VECTOR_PLANES = {2: 2, 3: 1}
+WIDENING_ENDS = 3
+R_BANKS, TURN_BANK, OUT_BANK = 4, 4, 6
+
+
+def adds_in_psum(s, n):
+    return n == 1 and (s <= WIDENING_ENDS or s == LAST)
 
 
 def tile_pooled_fisher_connectivity_s3_kernel(
@@ -52,24 +60,25 @@ def tile_pooled_fisher_connectivity_s3_kernel(
         psum = ctx.enter_context(tc.psum_pool(name="psum", bufs=1))
         ctx.enter_context(tc.manual_schedule())
 
-        regions_raw = [
-            keep.tile([P, PACK, hi - lo], BF16, align_bytes=64, name=f"regions_raw_{lo}") for lo, hi in REGION_RANGES
-        ]
+        def kept(name, count, shape, dtype):
+            return [keep.tile(shape, dtype, align_bytes=64, name=f"{name}_{n}") for n in range(count)]
+
+        def bank(number, shape):
+            return psum.tile(shape, F32, name=f"bank_{number}")
+
+        regions_raw = kept("regions_raw", 2, [P, PACK, HALF], BF16)
         new_raw = [keep.tile([P, PACK, hi - lo], BF16, align_bytes=64, name=f"new_raw_{lo}") for lo, hi in NEW_RANGES]
-        old_bytes = [
-            [keep.tile([P, PACK, hi - lo], U8, align_bytes=64, name=f"old_bytes_{g}_{lo}") for lo, hi in OLD_RANGES]
-            for g in range(GROUPS)
-        ]
+        old_bytes = [kept(f"old_bytes_{g}", 2, [P, PACK, HALF], U8) for g in range(GROUPS)]
         old_factor = keep.tile([P, GROUPS, PACK], F32)
-        d_words = [keep.tile([P, GROUPS, 2 * HALF], U8, align_bytes=64, name=f"d_words_{h}") for h in range(2)]
+        d_words = kept("d_words", 2, [P, GROUPS, 2 * HALF], U8)
         d_scales = keep.tile([P, GROUPS, R], U8, align_bytes=64)
         p_words = keep.tile([P, 2, 2 * E], U8, align_bytes=64)
         p_scales = keep.tile([P, 2, E], U8, align_bytes=64)
         weights = keep.tile([P, 2, PACK], BF16)
 
-        regions_grouped = [keep.tile([P, HALF, PACK], BF16, align_bytes=64, name=f"regions_grouped_{h}") for h in range(2)]
-        regions_codes = [keep.tile([P, HALF], U32, align_bytes=64, name=f"regions_codes_{h}") for h in range(2)]
-        regions_scales = [keep.tile([P, HALF], U8, align_bytes=64, name=f"regions_scales_{h}") for h in range(2)]
+        regions_grouped = kept("regions_grouped", 2, [P, HALF, PACK], BF16)
+        regions_codes = kept("regions_codes", 2, [P, HALF], U32)
+        regions_scales = kept("regions_scales", 2, [P, HALF], U8)
 
         identity = keep.tile([P, P], F32)
         one = keep.tile([P, 1], F32)
@@ -79,27 +88,22 @@ def tile_pooled_fisher_connectivity_s3_kernel(
         nc.gpsimd.memset(p_scales[:].rearrange("p g n -> p (g n)").bitcast(I32), 0)
         make_identity(nc, identity[:])
 
-        def find(ranges, column):
-            for n, (lo, hi) in enumerate(ranges):
-                if lo <= column < hi:
-                    return n, column - lo
-
-        def load_regions(n):
-            lo, hi = REGION_RANGES[n]
-            nc.sync.dma_start(out=regions_raw[n][:], in_=regions_new.rearrange("(p t) n -> p t n", t=PACK)[:, :, lo:hi])
+        def load_regions(h):
+            rows = regions_new.rearrange("(p t) n -> p t n", t=PACK)
+            nc.sync.dma_start(out=regions_raw[h][:], in_=rows[:, :, HALF * h : HALF * h + HALF])
 
         def load_new(n):
             lo, hi = NEW_RANGES[n]
             nc.sync.dma_start(out=new_raw[n][:], in_=seeds_new.rearrange("(p t) n -> p t n", t=PACK)[:, :, lo:hi])
 
-        def load_old(g, n):
-            lo, hi = OLD_RANGES[n]
-            rows = seeds_old_bytes.rearrange("(g p t) n -> g p t n", p=P, t=PACK)[g]
-            nc.sync.dma_start(out=old_bytes[g][n][:], in_=rows[:, :, lo:hi])
+        def load_old(n):
+            for g in range(GROUPS):
+                rows = seeds_old_bytes.rearrange("(g p t) n -> g p t n", p=P, t=PACK)[g]
+                nc.sync.dma_start(out=old_bytes[g][n][:], in_=rows[:, :, HALF * n : HALF * n + HALF])
 
-        def load_d(half):
+        def load_d(h):
             words = old_words.rearrange("g p w -> p g w")
-            nc.sync.dma_start(out=d_words[half][:], in_=words[:, :, 2 * HALF * half : 2 * HALF * half + 2 * HALF])
+            nc.sync.dma_start(out=d_words[h][:], in_=words[:, :, 2 * HALF * h : 2 * HALF * h + 2 * HALF])
 
         def load_scale_rows(tile, rows, groups):
             for q in range(4):
@@ -113,56 +117,60 @@ def tile_pooled_fisher_connectivity_s3_kernel(
             out=old_factor[:], in_=seeds_old_scale.rearrange("(g p t) o -> p g (t o)", p=P, t=PACK)
         )
         nc.scalar.dma_start(out=weights[:], in_=precision.rearrange("(h p t) -> p h t", p=P, t=PACK))
-        load_old(0, 0)
-        load_old(1, 0)
+        load_old(0)
         load_regions(0)
-        load_old(2, 0)
-        load_regions(1)
         load_scale_rows(d_scales, old_scales, GROUPS)
         load_d(0)
         load_new(0)
-        load_regions(2)
+        load_regions(1)
         load_d(1)
         load_new(1)
-        for g in range(GROUPS):
-            load_old(g, 1)
+        load_old(1)
         load_new(2)
         nc.sync.dma_start(out=p_words[:], in_=net_words.rearrange("g p w -> p g w"))
         load_scale_rows(p_scales, net_scales, 2)
 
         nc.scalar.activation(out=one[:], in_=one[:], func=ACT.Ln)
 
-        wide = [
-            keep.tile([P, PACK, GROUPS, CHUNK], BF16, align_bytes=64, name=f"wide_{c}") for c in range(M // CHUNK)
-        ]
+        wide = kept("wide", CHUNKS, [P, PACK, GROUPS, CHUNK], BF16)
 
-        def widen(c, g, engine, planes=range(PACK), cols=slice(0, CHUNK)):
-            n, lo = find(OLD_RANGES, CHUNK * c)
-            for t in planes:
-                src = old_bytes[g][n][:, t, lo + cols.start : lo + cols.stop].bitcast(FP8)
-                factor = old_factor[:, g, t : t + 1]
-                if engine == "scalar":
-                    nc.scalar.activation(out=wide[c][:, t, g, cols], in_=src, func=ACT.Copy, scale=factor)
-                else:
-                    nc.vector.tensor_scalar(out=wide[c][:, t, g, cols], in0=src, scalar1=factor, scalar2=None, op0=ALU.mult)
+        def widen(c, g, t, on_vector):
+            n, lo = divmod(CHUNK * c, HALF)
+            src = old_bytes[g][n][:, t, lo : lo + CHUNK].bitcast(FP8)
+            factor = old_factor[:, g, t : t + 1]
+            if on_vector:
+                nc.vector.tensor_scalar(out=wide[c][:, t, g, :], in0=src, scalar1=factor, scalar2=None, op0=ALU.mult)
+            else:
+                nc.scalar.activation(out=wide[c][:, t, g, :], in_=src, func=ACT.Copy, scale=factor)
 
-        def interleave(dst, src, copy=nc.vector.tensor_copy):
+        def widen_group(c, g, on_vector):
+            for t in range(PACK):
+                widen(c, g, t, on_vector)
+
+        def interleave(copy, dst, src):
             copy(out=dst, in_=src.rearrange("p t n -> p n t"))
 
         def gpsimd_copy(out, in_):
             nc.gpsimd.tensor_scalar(out=out, in0=in_, scalar1=1.0, scalar2=0.0, op0=ALU.mult, op1=ALU.add)
 
-        def interleave_regions(n, copy=nc.vector.tensor_copy):
-            lo, hi = REGION_RANGES[n]
-            h = lo // HALF
-            interleave(regions_grouped[h][:, lo - HALF * h : hi - HALF * h, :], regions_raw[n][:], copy)
+        def quantise(codes_ap, scales_ap, values_ap):
+            nc.vector.quantize_mx(out=codes_ap.bitcast(FP8X4), scales=scales_ap, in_=values_ap)
+
+        def interleave_regions(h):
+            interleave(nc.vector.tensor_copy, regions_grouped[h][:], regions_raw[h][:])
 
         def quantise_regions(h):
-            nc.vector.quantize_mx(
-                out=regions_codes[h][:].bitcast(FP8X4),
-                scales=regions_scales[h][:],
-                in_=regions_grouped[h][:].rearrange("p n t -> p (n t)"),
-            )
+            quantise(regions_codes[h][:], regions_scales[h][:], regions_grouped[h][:].rearrange("p n t -> p (n t)"))
+
+        first_grouped = keep.tile([P, PASSES, CHUNK, PACK], BF16, align_bytes=64)
+        first_codes = keep.tile([P, PASSES, CHUNK], U32, align_bytes=64)
+        first_scales = keep.tile([P, PASSES, CHUNK], U8, align_bytes=64)
+
+        def interleave_first(k, copy=nc.vector.tensor_copy):
+            interleave(copy, first_grouped[:, k, :, :], new_raw[0][:] if k == 0 else wide[0][:, :, k - 1, :])
+
+        def quantise_first(k):
+            quantise(first_codes[:, k, :], first_scales[:, k, :], first_grouped[:, k, :, :].rearrange("p n t -> p (n t)"))
 
         grouped, codes, scales = {}, {}, {}
 
@@ -172,106 +180,84 @@ def tile_pooled_fisher_connectivity_s3_kernel(
                 codes[i] = work.tile([P, PASSES, P], U32, align_bytes=64, name="codes")
                 scales[i] = work.tile([P, PASSES, P], U8, align_bytes=64, name="scales")
             if k == 0:
-                n, lo = find(NEW_RANGES, P * i)
+                n = [lo <= P * i < hi for lo, hi in NEW_RANGES].index(True)
+                lo = P * i - NEW_RANGES[n][0]
                 src = new_raw[n][:, :, lo : lo + P]
             else:
                 c, j = divmod(i, CHUNK // P)
                 src = wide[c][:, :, k - 1, P * j : P * j + P]
-            interleave(grouped[i][:, k, :, :], src, copy)
+            interleave(copy, grouped[i][:, k, :, :], src)
 
-        first_grouped = keep.tile([P, PASSES, CHUNK, PACK], BF16, align_bytes=64)
-        first_codes = keep.tile([P, PASSES, CHUNK], U32, align_bytes=64)
-        first_scales = keep.tile([P, PASSES, CHUNK], U8, align_bytes=64)
-
-        def interleave_first(k):
-            interleave(first_grouped[:, k, :, :], new_raw[0][:] if k == 0 else wide[0][:, :, k - 1, :])
-
-        def quantise_first(k):
-            nc.vector.quantize_mx(
-                out=first_codes[:, k, :].bitcast(FP8X4),
-                scales=first_scales[:, k, :],
-                in_=first_grouped[:, k, :, :].rearrange("p n t -> p (n t)"),
-            )
-
-        def stationary(i, k):
-            if P * i < CHUNK:
-                return first_codes[:, k, P * i : P * i + P], first_scales[:, k, P * i : P * i + P]
-            return codes[i][:, k, :], scales[i][:, k, :]
-
-        def interleave_old(i, groups=slice(0, GROUPS)):
+        def interleave_old(i, groups):
             c, j = divmod(i, CHUNK // P)
             nc.vector.tensor_copy(
-                out=grouped[i][:, 1 + groups.start : 1 + groups.stop, :, :].rearrange("p g (a n) t -> p a g n t", a=2),
-                in_=wide[c][:, :, groups, P * j : P * j + P].rearrange("p t g (a n) -> p a g n t", a=2),
+                out=grouped[i][:, 1 : 1 + groups, :, :].rearrange("p g (a n) t -> p a g n t", a=2),
+                in_=wide[c][:, :, :groups, P * j : P * j + P].rearrange("p t g (a n) -> p a g n t", a=2),
             )
 
-        def quantise_seeds(i, first, last):
-            nc.vector.quantize_mx(
-                out=codes[i][:, first:last, :].rearrange("p k n -> p (k n)").bitcast(FP8X4),
-                scales=scales[i][:, first:last, :].rearrange("p k n -> p (k n)"),
-                in_=grouped[i][:, first:last, :, :].rearrange("p k n t -> p (k n t)"),
+        def quantise_seeds(i):
+            quantise(
+                codes[i][:].rearrange("p k n -> p (k n)"),
+                scales[i][:].rearrange("p k n -> p (k n)"),
+                grouped[i][:].rearrange("p k n t -> p (k n t)"),
             )
 
         r = {}
 
-        def correlate_pair(units):
-            for i, h in units:
-                r[i, h] = psum.tile([P, HALF], F32, name=f"bank_{len(r) % 4}")
-            for n, k in enumerate(PASS_ORDER):
-                for i, h in units:
-                    if k == 0:
-                        moving = regions_codes[h][:].bitcast(FP8X4)
-                        moving_scale = regions_scales[h][:]
-                    else:
-                        moving = d_words[h][:, k - 1, :].bitcast(FP4X4)
-                        moving_scale = d_scales[:, k - 1, HALF * h : HALF * h + HALF]
-                    nc.tensor.matmul_mx(
-                        out=r[i, h][:],
-                        lhsT=stationary(i, k)[0].bitcast(FP8X4),
-                        lhsT_scale=stationary(i, k)[1],
-                        rhs=moving,
-                        rhs_scale=moving_scale,
-                        start=(n == 0),
-                        stop=(n == PASSES - 1),
-                    )
+        def correlate(order):
+            for n, (i, h) in order:
+                if n == 0:
+                    r[i, h] = bank(len(r) % R_BANKS, [P, HALF])
+                k = PASS_ORDER[n]
+                if P * i < CHUNK:
+                    fixed, fixed_scale = first_codes[:, k, P * i : P * i + P], first_scales[:, k, P * i : P * i + P]
+                else:
+                    fixed, fixed_scale = codes[i][:, k, :], scales[i][:, k, :]
+                if k == 0:
+                    moving, moving_scale = regions_codes[h][:].bitcast(FP8X4), regions_scales[h][:]
+                else:
+                    moving = d_words[h][:, k - 1, :].bitcast(FP4X4)
+                    moving_scale = d_scales[:, k - 1, HALF * h : HALF * h + HALF]
+                nc.tensor.matmul_mx(
+                    out=r[i, h][:],
+                    lhsT=fixed.bitcast(FP8X4),
+                    lhsT_scale=fixed_scale,
+                    rhs=moving,
+                    rhs_scale=moving_scale,
+                    start=(n == 0),
+                    stop=(n == PASSES - 1),
+                )
 
-        def correlate(i, h):
-            correlate_pair(((i, h),))
-
-        steps = [((0, 0), (1, 0)), ((0, 1), (1, 1))] + [((i, 0), (i, 1)) for i in range(2, TILES)]
         ln_plus, ln_minus, difference = {}, {}, {}
+        all_planes = slice(0, PACK)
 
-        def take_logarithms(s, n, planes=slice(0, PACK)):
-            if n == 0 and planes.start == 0:
+        def take_logarithms(s, n, planes=all_planes):
+            if s not in ln_plus:
                 ln_plus[s] = work.tile([P, 2, PACK, P], F32, name="ln_plus")
                 ln_minus[s] = work.tile([P, 2, PACK, P], F32, name="ln_minus")
                 difference[s] = work.tile([P, 2, PACK, P], F32, name="difference")
-            by_t = r[steps[s][n]][:].rearrange("s (p t) -> s t p", t=PACK)[:, planes, :]
+            by_t = r[STEPS[s][n]][:].rearrange("s (p t) -> s t p", t=PACK)[:, planes, :]
             nc.scalar.activation(out=ln_minus[s][:, n, planes, :], in_=by_t, func=ACT.Ln, bias=1.0, scale=-1.0)
             nc.scalar.activation(out=ln_plus[s][:, n, planes, :], in_=by_t, func=ACT.Ln, bias=1.0, scale=1.0)
 
-        def form_difference(s, units=slice(0, 2), planes=slice(0, PACK)):
-            dst = difference[s][:, units, planes, :]
-            if (s, units.start) in PSUM_DIFFERENCE:
-                nc.vector.tensor_scalar(
-                    out=dst, in0=ln_minus[s][:, units, planes, :], scalar1=-1.0, scalar2=None, op0=ALU.mult
-                )
+        def form_difference(s, pieces, planes=all_planes):
+            dst = difference[s][:, pieces, planes, :]
+            minus = ln_minus[s][:, pieces, planes, :]
+            if adds_in_psum(s, pieces.start):
+                nc.vector.tensor_scalar(out=dst, in0=minus, scalar1=-1.0, scalar2=None, op0=ALU.mult)
             else:
-                nc.vector.tensor_tensor(
-                    out=dst, in0=ln_plus[s][:, units, planes, :], in1=ln_minus[s][:, units, planes, :], op=ALU.subtract
-                )
+                nc.vector.tensor_tensor(out=dst, in0=ln_plus[s][:, pieces, planes, :], in1=minus, op=ALU.subtract)
 
         turned = {}
 
-        def turn(s, n, bank, planes=slice(0, PACK)):
-            unit = steps[s][n]
-            if planes.start == 0:
-                turned[unit] = psum.tile([P, P // 2, PACK, 2], F32, name=f"bank_{bank}")
-            parts = (difference[s], ln_plus[s]) if (s, n) in PSUM_DIFFERENCE else (difference[s],)
-            for t in range(planes.start, planes.stop):
+        def turn(s, n, number):
+            piece = STEPS[s][n]
+            turned[piece] = bank(number, [P, P // 2, PACK, 2])
+            parts = (difference[s], ln_plus[s]) if adds_in_psum(s, n) else (difference[s],)
+            for t in range(PACK):
                 for m, part in enumerate(parts):
                     nc.tensor.matmul(
-                        turned[unit][:, :, t, :],
+                        turned[piece][:, :, t, :],
                         lhsT=part[:, n, t, :],
                         rhs=identity[:],
                         start=(m == 0),
@@ -293,128 +279,139 @@ def tile_pooled_fisher_connectivity_s3_kernel(
                 op=ALU.mult,
             )
 
-        def quantise_z(i, first, last):
-            nc.vector.quantize_mx(
-                out=z_codes[i][:, first:last, :].rearrange("p h n -> p (h n)").bitcast(FP8X4),
-                scales=z_scales[i][:, first:last, :].rearrange("p h n -> p (h n)"),
-                in_=z_grouped[i][:, first:last, :, :].rearrange("p h n t -> p (h n t)"),
+        def quantise_z(i, halves=slice(0, 2)):
+            quantise(
+                z_codes[i][:, halves, :].rearrange("p h n -> p (h n)"),
+                z_scales[i][:, halves, :].rearrange("p h n -> p (h n)"),
+                z_grouped[i][:, halves, :, :].rearrange("p h n t -> p (h n t)"),
+            )
+
+        def project_pass(dst, i, h, lo, hi):
+            nc.tensor.matmul_mx(
+                out=dst,
+                lhsT=z_codes[i][:, h, :].bitcast(FP8X4),
+                lhsT_scale=z_scales[i][:, h, :],
+                rhs=p_words[:, h, 2 * lo : 2 * hi].bitcast(FP4X4),
+                rhs_scale=p_scales[:, h, lo:hi],
+                start=(h == 0),
+                stop=(h == 1),
             )
 
         out_bank = {}
 
-        def project(i, bank, halves=(0, 1)):
-            for h in halves:
-                if h == 0:
-                    out_bank[i] = psum.tile([P, E], F32, name=f"bank_{bank}")
-                nc.tensor.matmul_mx(
-                    out=out_bank[i][:],
-                    lhsT=z_codes[i][:, h, :].bitcast(FP8X4),
-                    lhsT_scale=z_scales[i][:, h, :],
-                    rhs=p_words[:, h, :].bitcast(FP4X4),
-                    rhs_scale=p_scales[:, h, :],
-                    start=(h == 0),
-                    stop=(h == 1),
-                )
+        def project(i, number):
+            out_bank[i] = bank(number, [P, E])
+            for h in range(2):
+                project_pass(out_bank[i][:], i, h, 0, E)
 
-        def store(i, copy):
+        def store(i):
             result = work.tile([P, E], F32, bufs=4)
-            copy(out=result[:], in_=out_bank[i][:])
+            nc.scalar.copy(out=result[:], in_=out_bank[i][:])
             nc.sync.dma_start(out=out[P * i : P * i + P, :], in_=result[:])
 
-        widen(0, 0, "vector")
-        widen(1, 0, "scalar")
-        widen(0, 1, "scalar")
-        widen(0, 2, "scalar")
+        widen_group(0, 0, True)
+        widen_group(1, 0, False)
+        widen_group(0, 1, True)
+        widen_group(1, 1, False)
+        widen_group(0, 2, False)
         interleave_first(1)
-        interleave_regions(0)
-        quantise_first(1)
         interleave_first(2)
-        interleave_regions(1)
+        quantise_first(1)
+        interleave_first(3, nc.scalar.copy)
+        interleave_regions(0)
         quantise_first(2)
-        interleave_first(3)
         quantise_regions(0)
         quantise_first(3)
         interleave_first(0)
+        interleave_seeds(2, 1)
         quantise_first(0)
-        correlate_pair(((0, 0), (1, 0)))
-        widen(1, 1, "scalar")
-        widen(1, 2, "scalar")
-        interleave_regions(2)
-        interleave_seeds(2, 0)
+        first, second = STEPS[0]
+        correlate([(n, piece) for n in range(2) for piece in STEPS[0]])
+        correlate([(2, first), (3, first), (2, second), (3, second)])
+        widen_group(1, 2, False)
+        interleave_seeds(2, 2, nc.scalar.copy)
+        interleave_seeds(2, 3, nc.scalar.copy)
+        interleave_regions(1)
         quantise_regions(1)
-        correlate_pair(((0, 1), (1, 1)))
+        correlate([(n, piece) for n in range(PASSES) for piece in STEPS[1]])
 
-        last = TILES - 1
-        for s in range(-1, last - 1):
-            projected = {2: (0,), 3: (1,), 4: (2,3)}.get(s, ())
+        for s in range(-1, LAST - 1):
+            projected = range(max(s - 2, 0), s - 1 + (s == WIDENING_ENDS + 1)) if s < LAST - 2 else ()
+            c, j = divmod(s + 5, 2)
+            planes = [(g, t) for g in range(GROUPS) for t in range(PACK)][6 * j : 6 * j + 6] if c < CHUNKS else []
+            on_vector = VECTOR_PLANES.get(c, 0)
             if s >= 0:
-                turn(s, 0, 4)
-                turn(s, 1, 5)
+                turn(s, 0, TURN_BANK)
+                turn(s, 1, TURN_BANK + 1)
             take_logarithms(s + 1, 0)
             take_logarithms(s + 1, 1)
             if s >= 0:
-                for i, h in steps[s]:
+                for i, h in STEPS[s]:
                     weigh(i, h)
-            c, j = divmod(s + 5, 2)
-            jobs = [(g, t) for g in range(GROUPS) for t in range(PACK)][6 * j : 6 * j + 6] if c < M // CHUNK else []
-            for g, t in jobs[: 1]:
-                widen(c, g, "vector", (t,))
-            form_difference(s + 1)
-            if s < 0:
-                interleave_old(2)
+            if adds_in_psum(s + 1, 1):
+                form_difference(s + 1, slice(0, 1))
+                if s < 0:
+                    interleave_seeds(2, 0)
+                form_difference(s + 1, slice(1, 2))
+            else:
+                form_difference(s + 1, slice(0, 2))
+            for g, t in planes[:on_vector]:
+                widen(c, g, t, True)
             for i in projected:
-                project(i, 6 + i % 2)
+                project(i, OUT_BANK + i % 2)
             if s >= 0:
-                correlate(s + 2, 0)
-                correlate(s + 2, 1)
-            for g, t in jobs[1 :]:
-                widen(c, g, "scalar", (t,))
-            if 3 <= s + 3 < TILES:
-                interleave_seeds(s + 3, 0, gpsimd_copy if s + 3 in range(8) else nc.vector.tensor_copy)
-                if s + 3 in (6,7):
+                correlate([(n, piece) for piece in STEPS[s + 2] for n in range(PASSES)])
+            for g, t in planes[on_vector:]:
+                widen(c, g, t, False)
+            if 0 <= s < TILES - 3:
+                interleave_seeds(s + 3, 0, gpsimd_copy)
+                if s >= WIDENING_ENDS:
                     interleave_seeds(s + 3, GROUPS, nc.scalar.copy)
-                    interleave_old(s + 3, slice(0, GROUPS - 1))
+                    interleave_old(s + 3, GROUPS - 1)
                 else:
-                    interleave_old(s + 3)
+                    interleave_old(s + 3, GROUPS)
             for i in projected:
-                store(i, nc.scalar.copy)
-            if s >= 0:
-                if s < 2:
-                    for i, h in steps[s]:
-                        quantise_z(i, h, h + 1)
-                else:
-                    quantise_z(s, 0, 2)
-            if s + 3 < TILES:
-                quantise_seeds(s + 3, 0, PASSES)
-        first, second = slice(0, 2), slice(2, 4)
-        take_logarithms(last, 0)
-        turn(last - 1, 0, 4)
-        turn(last - 1, 1, 5)
-        project(last - 3, 6)
-        project(last - 2, 7)
-        form_difference(last, slice(0, 1))
-        take_logarithms(last, 1, first)
-        take_logarithms(last, 1, second)
-        turn(last, 0, 0)
-        weigh(last - 1, 0)
-        form_difference(last, slice(1, 2), first)
-        weigh(last - 1, 1)
-        form_difference(last, slice(1, 2), second)
-        turn(last, 1, 1, first)
-        turn(last, 1, 1, second)
-        store(last - 3, nc.scalar.copy)
-        store(last - 2, nc.scalar.copy)
-        quantise_z(last - 1, 0, 2)
-        weigh(last, 0)
-        weigh(last, 1)
-        project(last - 1, 2)
-        quantise_z(last, 0, 1)
-        project(last, 3, (0,))
-        quantise_z(last, 1, 2)
-        project(last, 3, (1,))
-        store(last - 1, nc.scalar.copy)
-        for half in range(2):
-            cols = slice(half * E // 2, (half + 1) * E // 2)
-            result_half = work.tile([P, E // 2], F32)
-            nc.vector.tensor_copy(out=result_half[:], in_=out_bank[last][:, cols])
-            nc.sync.dma_start(out=out[P * last : P * last + P, cols], in_=result_half[:])
+                store(i)
+            if s >= 2:
+                quantise_z(s)
+            elif s >= 0:
+                for i, h in STEPS[s]:
+                    quantise_z(i, slice(h, h + 1))
+            if s < TILES - 3:
+                quantise_seeds(s + 3)
+
+        low, high = slice(0, 2), slice(2, PACK)
+        take_logarithms(LAST, 0)
+        turn(LAST - 1, 0, TURN_BANK)
+        turn(LAST - 1, 1, TURN_BANK + 1)
+        project(LAST - 3, OUT_BANK)
+        project(LAST - 2, OUT_BANK + 1)
+        form_difference(LAST, slice(0, 1))
+        take_logarithms(LAST, 1, low)
+        take_logarithms(LAST, 1, high)
+        turn(LAST, 0, 0)
+        weigh(LAST - 1, 0)
+        form_difference(LAST, slice(1, 2), low)
+        weigh(LAST - 1, 1)
+        form_difference(LAST, slice(1, 2), high)
+        turn(LAST, 1, 1)
+        store(LAST - 3)
+        store(LAST - 2)
+        quantise_z(LAST - 1)
+        weigh(LAST, 0)
+        weigh(LAST, 1)
+        project(LAST - 1, 2)
+        quarters = [bank(3 + q, [P, P]) for q in range(4)]
+        for h in range(2):
+            quantise_z(LAST, slice(h, h + 1))
+            for q in range(4):
+                project_pass(quarters[q][:], LAST, h, P * q, P * q + P)
+        store(LAST - 1)
+        for n, (copy, queue) in enumerate(((nc.vector.tensor_copy, nc.sync), (nc.scalar.copy, nc.scalar))):
+            result_half = work.tile([P, 2, P], F32)
+            for q in range(2):
+                copy(out=result_half[:, q, :], in_=quarters[2 * n + q][:])
+            queue.dma_start(
+                out=out[P * LAST : P * LAST + P, 2 * P * n : 2 * P * n + 2 * P],
+                in_=result_half[:].rearrange("p q n -> p (q n)"),
+            )

@@ -33,11 +33,11 @@ NEW_RANGES = ((0, CHUNK), (CHUNK, HALF), (HALF, M))
 STEPS = [((0, 0), (1, 0)), ((0, 1), (1, 1))] + [((i, 0), (i, 1)) for i in range(2, TILES)]
 VECTOR_PLANES = {2: 2, 3: 1}
 WIDENING_ENDS = 3
-R_BANKS, TURN_BANK, OUT_BANK = 4, 4, 6
+R_BANKS, TURN_BANK, OUT_BANK, THROUGH_BANK = 4, 4, 6, 7
 
 
 def adds_in_psum(s, n):
-    return n == 1 and (s <= WIDENING_ENDS or s == LAST)
+    return n == 1 and s in (0,1,2,3,7)
 
 
 def tile_pooled_fisher_connectivity_s3_kernel(
@@ -81,11 +81,13 @@ def tile_pooled_fisher_connectivity_s3_kernel(
         regions_scales = kept("regions_scales", 2, [P, HALF], U8)
 
         identity = keep.tile([P, P], F32)
+        identity_bf16 = keep.tile([P, P], BF16)
         one = keep.tile([P, 1], F32)
 
         nc.vector.memset(one[:], 1.0)
         nc.vector.memset(d_scales[:].rearrange("p g n -> p (g n)").bitcast(I32), 0)
         nc.gpsimd.memset(p_scales[:].rearrange("p g n -> p (g n)").bitcast(I32), 0)
+        make_identity(nc, identity_bf16[:])
         make_identity(nc, identity[:])
 
         def load_regions(h):
@@ -116,7 +118,6 @@ def tile_pooled_fisher_connectivity_s3_kernel(
         nc.scalar.dma_start(
             out=old_factor[:], in_=seeds_old_scale.rearrange("(g p t) o -> p g (t o)", p=P, t=PACK)
         )
-        nc.scalar.dma_start(out=weights[:], in_=precision.rearrange("(h p t) -> p h t", p=P, t=PACK))
         load_old(0)
         load_regions(0)
         load_scale_rows(d_scales, old_scales, GROUPS)
@@ -125,6 +126,7 @@ def tile_pooled_fisher_connectivity_s3_kernel(
         load_regions(1)
         load_d(1)
         load_new(1)
+        nc.sync.dma_start(out=weights[:], in_=precision.rearrange("(h p t) -> p h t", p=P, t=PACK))
         load_old(1)
         load_new(2)
         nc.sync.dma_start(out=p_words[:], in_=net_words.rearrange("g p w -> p g w"))
@@ -149,6 +151,18 @@ def tile_pooled_fisher_connectivity_s3_kernel(
 
         def interleave(copy, dst, src):
             copy(out=dst, in_=src.rearrange("p t n -> p n t"))
+
+        def through_matmul(out, in_):
+            through = psum.tile([P, P, PACK], BF16, name=f"bank_{THROUGH_BANK}")
+            nc.tensor.matmul(through[:], lhsT=identity_bf16[:], rhs=in_, start=True, stop=True)
+            waiting.append((out, through))
+
+        waiting = []
+
+        def empty_through():
+            for dst, through in waiting:
+                nc.scalar.copy(out=dst.rearrange("p n t -> p (n t)"), in_=through[:].rearrange("p n t -> p (n t)"))
+            waiting.clear()
 
         def gpsimd_copy(out, in_):
             nc.gpsimd.tensor_scalar(out=out, in0=in_, scalar1=1.0, scalar2=0.0, op0=ALU.mult, op1=ALU.add)
@@ -188,11 +202,11 @@ def tile_pooled_fisher_connectivity_s3_kernel(
                 src = wide[c][:, :, k - 1, P * j : P * j + P]
             interleave(copy, grouped[i][:, k, :, :], src)
 
-        def interleave_old(i, groups):
+        def interleave_old(i, lo, hi):
             c, j = divmod(i, CHUNK // P)
             nc.vector.tensor_copy(
-                out=grouped[i][:, 1 : 1 + groups, :, :].rearrange("p g (a n) t -> p a g n t", a=2),
-                in_=wide[c][:, :, :groups, P * j : P * j + P].rearrange("p t g (a n) -> p a g n t", a=2),
+                out=grouped[i][:, 1 + lo : 1 + hi, :, :].rearrange("p g (a n) t -> p a g n t", a=2),
+                in_=wide[c][:, :, lo:hi, P * j : P * j + P].rearrange("p t g (a n) -> p a g n t", a=2),
             )
 
         def quantise_seeds(i):
@@ -336,10 +350,10 @@ def tile_pooled_fisher_connectivity_s3_kernel(
         correlate([(n, piece) for n in range(PASSES) for piece in STEPS[1]])
 
         for s in range(-1, LAST - 1):
-            projected = range(max(s - 2, 0), s - 1 + (s == WIDENING_ENDS + 1)) if s < LAST - 2 else ()
+            projected = (s - 2,) if s >= 2 else ()
             c, j = divmod(s + 5, 2)
             planes = [(g, t) for g in range(GROUPS) for t in range(PACK)][6 * j : 6 * j + 6] if c < CHUNKS else []
-            on_vector = VECTOR_PLANES.get(c, 0)
+            on_vector = {-1:3,0:3,1:3,2:2}.get(s, 0)
             if s >= 0:
                 turn(s, 0, TURN_BANK)
                 turn(s, 1, TURN_BANK + 1)
@@ -348,7 +362,7 @@ def tile_pooled_fisher_connectivity_s3_kernel(
             if s >= 0:
                 for i, h in STEPS[s]:
                     weigh(i, h)
-            if adds_in_psum(s + 1, 1):
+            if s + 1 in (0, 1, 2, 3):
                 form_difference(s + 1, slice(0, 1))
                 if s < 0:
                     interleave_seeds(2, 0)
@@ -358,18 +372,23 @@ def tile_pooled_fisher_connectivity_s3_kernel(
             for g, t in planes[:on_vector]:
                 widen(c, g, t, True)
             for i in projected:
-                project(i, OUT_BANK + i % 2)
+                project(i, OUT_BANK)
+            if 0 <= s < TILES - 3:
+                interleave_seeds(s + 3, 0, gpsimd_copy)
+                if s in (0,1,2):
+                    interleave_seeds(s + 3, 1, through_matmul)
             if s >= 0:
                 correlate([(n, piece) for piece in STEPS[s + 2] for n in range(PASSES)])
+            empty_through()
             for g, t in planes[on_vector:]:
                 widen(c, g, t, False)
             if 0 <= s < TILES - 3:
-                interleave_seeds(s + 3, 0, gpsimd_copy)
-                if s >= WIDENING_ENDS:
+                lo = 1 if s in (0,1,2) else 0
+                if s in (3, 4):
                     interleave_seeds(s + 3, GROUPS, nc.scalar.copy)
-                    interleave_old(s + 3, GROUPS - 1)
+                    interleave_old(s + 3, lo, GROUPS - 1)
                 else:
-                    interleave_old(s + 3, GROUPS)
+                    interleave_old(s + 3, lo, GROUPS)
             for i in projected:
                 store(i)
             if s >= 2:

@@ -33,11 +33,11 @@ NEW_RANGES = ((0, CHUNK), (CHUNK, HALF), (HALF, M))
 STEPS = [((0, 0), (1, 0)), ((0, 1), (1, 1))] + [((i, 0), (i, 1)) for i in range(2, TILES)]
 VECTOR_PLANES = {2: 2, 3: 1}
 WIDENING_ENDS = 3
-R_BANKS, TURN_BANK, OUT_BANK, THROUGH_BANK = 4, 4, 6, 7
+R_BANKS, TURN_BANK, OUT_BANK = 4, 4, 6
 
 
 def adds_in_psum(s, n):
-    return n == 1 and s in (0,1,2,3,7)
+    return n == 1 and s in (0,2,3,7)
 
 
 def tile_pooled_fisher_connectivity_s3_kernel(
@@ -152,17 +152,22 @@ def tile_pooled_fisher_connectivity_s3_kernel(
         def interleave(copy, dst, src):
             copy(out=dst, in_=src.rearrange("p t n -> p n t"))
 
-        def through_matmul(out, in_):
-            through = psum.tile([P, P, PACK], BF16, name=f"bank_{THROUGH_BANK}")
-            nc.tensor.matmul(through[:], lhsT=identity_bf16[:], rhs=in_, start=True, stop=True)
-            waiting.append((out, through))
+        through = []
 
-        waiting = []
+        def turn_by_matmul(src, number):
+            through.append(psum.tile([P, 2, P, PACK], BF16, name=f"bank_{number}"))
+            for j in range(2):
+                nc.tensor.matmul(
+                    through[-1][:, j, :, :],
+                    lhsT=identity_bf16[:],
+                    rhs=src[:, :, P * j : P * j + P].rearrange("p t n -> p n t"),
+                    start=True,
+                    stop=True,
+                )
 
-        def empty_through():
-            for dst, through in waiting:
-                nc.scalar.copy(out=dst.rearrange("p n t -> p (n t)"), in_=through[:].rearrange("p n t -> p (n t)"))
-            waiting.clear()
+        def empty_through(dst):
+            nc.scalar.copy(out=dst.rearrange("p n t -> p (n t)"), in_=through[0][:].rearrange("p j n t -> p (j n t)"))
+            through.remove(through[0])
 
         def gpsimd_copy(out, in_):
             nc.gpsimd.tensor_scalar(out=out, in0=in_, scalar1=1.0, scalar2=0.0, op0=ALU.mult, op1=ALU.add)
@@ -176,23 +181,26 @@ def tile_pooled_fisher_connectivity_s3_kernel(
         def quantise_regions(h):
             quantise(regions_codes[h][:], regions_scales[h][:], regions_grouped[h][:].rearrange("p n t -> p (n t)"))
 
-        first_grouped = keep.tile([P, PASSES, CHUNK, PACK], BF16, align_bytes=64)
-        first_codes = keep.tile([P, PASSES, CHUNK], U32, align_bytes=64)
-        first_scales = keep.tile([P, PASSES, CHUNK], U8, align_bytes=64)
+        early_grouped = kept("early_grouped", 2, [P, PASSES, CHUNK, PACK], BF16)
+        early_codes = kept("early_codes", 2, [P, PASSES, CHUNK], U32)
+        early_scales = kept("early_scales", 2, [P, PASSES, CHUNK], U8)
 
-        def interleave_first(k, copy=nc.vector.tensor_copy):
-            interleave(copy, first_grouped[:, k, :, :], new_raw[0][:] if k == 0 else wide[0][:, :, k - 1, :])
+        def interleave_early(c, k, copy=nc.vector.tensor_copy):
+            interleave(copy, early_grouped[c][:, k, :, :], new_raw[0][:] if k == 0 else wide[c][:, :, k - 1, :])
 
-        def quantise_first(k):
-            quantise(first_codes[:, k, :], first_scales[:, k, :], first_grouped[:, k, :, :].rearrange("p n t -> p (n t)"))
+        def quantise_early(c, k):
+            quantise(
+                early_codes[c][:, k, :], early_scales[c][:, k, :], early_grouped[c][:, k, :, :].rearrange("p n t -> p (n t)")
+            )
 
         grouped, codes, scales = {}, {}, {}
 
         def interleave_seeds(i, k, copy=nc.vector.tensor_copy):
             if i not in grouped:
-                grouped[i] = work.tile([P, PASSES, P, PACK], BF16, align_bytes=64, name="grouped", bufs=1)
-                codes[i] = work.tile([P, PASSES, P], U32, align_bytes=64, name="codes")
-                scales[i] = work.tile([P, PASSES, P], U8, align_bytes=64, name="scales")
+                passes = 1 if P * i < HALF else PASSES
+                grouped[i] = work.tile([P, passes, P, PACK], BF16, align_bytes=64, name="grouped", bufs=1)
+                codes[i] = work.tile([P, passes, P], U32, align_bytes=64, name="codes")
+                scales[i] = work.tile([P, passes, P], U8, align_bytes=64, name="scales")
             if k == 0:
                 n = [lo <= P * i < hi for lo, hi in NEW_RANGES].index(True)
                 lo = P * i - NEW_RANGES[n][0]
@@ -202,11 +210,11 @@ def tile_pooled_fisher_connectivity_s3_kernel(
                 src = wide[c][:, :, k - 1, P * j : P * j + P]
             interleave(copy, grouped[i][:, k, :, :], src)
 
-        def interleave_old(i, lo, hi):
+        def interleave_old(i, groups):
             c, j = divmod(i, CHUNK // P)
             nc.vector.tensor_copy(
-                out=grouped[i][:, 1 + lo : 1 + hi, :, :].rearrange("p g (a n) t -> p a g n t", a=2),
-                in_=wide[c][:, :, lo:hi, P * j : P * j + P].rearrange("p t g (a n) -> p a g n t", a=2),
+                out=grouped[i][:, 1 : 1 + groups, :, :].rearrange("p g (a n) t -> p a g n t", a=2),
+                in_=wide[c][:, :, :groups, P * j : P * j + P].rearrange("p t g (a n) -> p a g n t", a=2),
             )
 
         def quantise_seeds(i):
@@ -223,8 +231,9 @@ def tile_pooled_fisher_connectivity_s3_kernel(
                 if n == 0:
                     r[i, h] = bank(len(r) % R_BANKS, [P, HALF])
                 k = PASS_ORDER[n]
-                if P * i < CHUNK:
-                    fixed, fixed_scale = first_codes[:, k, P * i : P * i + P], first_scales[:, k, P * i : P * i + P]
+                c, j = divmod(i, CHUNK // P)
+                if c == 0 or (c == 1 and k > 0):
+                    fixed, fixed_scale = early_codes[c][:, k, P * j : P * j + P], early_scales[c][:, k, P * j : P * j + P]
                 else:
                     fixed, fixed_scale = codes[i][:, k, :], scales[i][:, k, :]
                 if k == 0:
@@ -328,32 +337,36 @@ def tile_pooled_fisher_connectivity_s3_kernel(
         widen_group(0, 1, True)
         widen_group(1, 1, False)
         widen_group(0, 2, False)
-        interleave_first(1)
-        interleave_first(2)
-        quantise_first(1)
-        interleave_first(3, nc.scalar.copy)
+        for k in PASS_ORDER[:2]:
+            turn_by_matmul(wide[1][:, :, k - 1, :], TURN_BANK + k - 1)
+        interleave_early(0, 1)
+        interleave_early(0, 2)
+        quantise_early(0, 1)
+        empty_through(early_grouped[1][:, 1, :, :])
+        interleave_early(0, 3, nc.scalar.copy)
         interleave_regions(0)
-        quantise_first(2)
+        quantise_early(0, 2)
         quantise_regions(0)
-        quantise_first(3)
-        interleave_first(0)
-        interleave_seeds(2, 1)
-        quantise_first(0)
+        widen_group(1, 2, False)
+        empty_through(early_grouped[1][:, 2, :, :])
+        interleave_early(0, 0)
+        quantise_early(0, 3)
+        quantise_early(0, 0)
         first, second = STEPS[0]
         correlate([(n, piece) for n in range(2) for piece in STEPS[0]])
         correlate([(2, first), (3, first), (2, second), (3, second)])
-        widen_group(1, 2, False)
-        interleave_seeds(2, 2, nc.scalar.copy)
-        interleave_seeds(2, 3, nc.scalar.copy)
+        interleave(nc.scalar.copy, early_grouped[1][:, 3, :P, :], wide[1][:, :, 2, :P])
         interleave_regions(1)
+        interleave(nc.vector.tensor_copy, early_grouped[1][:, 3, P:, :], wide[1][:, :, 2, P:])
         quantise_regions(1)
+        quantise_early(1, 1)
         correlate([(n, piece) for n in range(PASSES) for piece in STEPS[1]])
 
         for s in range(-1, LAST - 1):
             projected = (s - 2,) if s >= 2 else ()
             c, j = divmod(s + 5, 2)
-            planes = [(g, t) for g in range(GROUPS) for t in range(PACK)][6 * j : 6 * j + 6] if c < CHUNKS else []
-            on_vector = {-1:3,0:3,1:3,2:2}.get(s, 0)
+            planes = [(g, t) for g in range(GROUPS) for t in range(PACK)][{-1:slice(0,2),0:slice(2,12)}.get(s, slice(6 * j, 6 * j + 6))] if c < CHUNKS else []
+            on_vector = {0:6,1:1,2:1}.get(s, 0)
             if s >= 0:
                 turn(s, 0, TURN_BANK)
                 turn(s, 1, TURN_BANK + 1)
@@ -362,33 +375,28 @@ def tile_pooled_fisher_connectivity_s3_kernel(
             if s >= 0:
                 for i, h in STEPS[s]:
                     weigh(i, h)
-            if s + 1 in (0, 1, 2, 3):
+            for g, t in planes[:on_vector]:
+                widen(c, g, t, True)
+            if s + 1 in (0,1,2,3):
                 form_difference(s + 1, slice(0, 1))
                 if s < 0:
                     interleave_seeds(2, 0)
                 form_difference(s + 1, slice(1, 2))
             else:
                 form_difference(s + 1, slice(0, 2))
-            for g, t in planes[:on_vector]:
-                widen(c, g, t, True)
             for i in projected:
-                project(i, OUT_BANK)
-            if 0 <= s < TILES - 3:
-                interleave_seeds(s + 3, 0, gpsimd_copy)
-                if s in (0,1,2):
-                    interleave_seeds(s + 3, 1, through_matmul)
+                project(i, OUT_BANK + i % 2)
             if s >= 0:
                 correlate([(n, piece) for piece in STEPS[s + 2] for n in range(PASSES)])
-            empty_through()
             for g, t in planes[on_vector:]:
                 widen(c, g, t, False)
             if 0 <= s < TILES - 3:
-                lo = 1 if s in (0,1,2) else 0
-                if s in (3, 4):
+                interleave_seeds(s + 3, 0, gpsimd_copy)
+                if s >= WIDENING_ENDS:
                     interleave_seeds(s + 3, GROUPS, nc.scalar.copy)
-                    interleave_old(s + 3, lo, GROUPS - 1)
-                else:
-                    interleave_old(s + 3, lo, GROUPS)
+                    interleave_old(s + 3, GROUPS - 1)
+                elif s > 0:
+                    interleave_old(s + 3, GROUPS)
             for i in projected:
                 store(i)
             if s >= 2:
@@ -396,6 +404,9 @@ def tile_pooled_fisher_connectivity_s3_kernel(
             elif s >= 0:
                 for i, h in STEPS[s]:
                     quantise_z(i, slice(h, h + 1))
+            if s < 0:
+                quantise_early(1, 2)
+                quantise_early(1, 3)
             if s < TILES - 3:
                 quantise_seeds(s + 3)
 

@@ -31,13 +31,14 @@ PASS_ORDER = (1, 2, 3, 0)
 NEW_RANGES = ((0, CHUNK), (CHUNK, HALF), (HALF, M))
 
 STEPS = [((0, 0), (1, 0)), ((0, 1), (1, 1))] + [((i, 0), (i, 1)) for i in range(2, TILES)]
-VECTOR_PLANES = {2: 2, 3: 1}
+FIRST_STEP_PLANES = {2: 2, 3: 6}
+VECTOR_PLANES = {0: 6, 1: 1, 2: 1}
 WIDENING_ENDS = 3
 R_BANKS, TURN_BANK, OUT_BANK = 4, 4, 6
 
 
 def adds_in_psum(s, n):
-    return n == 1 and s in (0,2,3,7)
+    return n == 1 and s != 1 and (s <= WIDENING_ENDS or s == LAST)
 
 
 def tile_pooled_fisher_connectivity_s3_kernel(
@@ -118,6 +119,7 @@ def tile_pooled_fisher_connectivity_s3_kernel(
         nc.scalar.dma_start(
             out=old_factor[:], in_=seeds_old_scale.rearrange("(g p t) o -> p g (t o)", p=P, t=PACK)
         )
+        nc.scalar.dma_start(out=weights[:], in_=precision.rearrange("(h p t) -> p h t", p=P, t=PACK))
         load_old(0)
         load_regions(0)
         load_scale_rows(d_scales, old_scales, GROUPS)
@@ -126,7 +128,6 @@ def tile_pooled_fisher_connectivity_s3_kernel(
         load_regions(1)
         load_d(1)
         load_new(1)
-        nc.sync.dma_start(out=weights[:], in_=precision.rearrange("(h p t) -> p h t", p=P, t=PACK))
         load_old(1)
         load_new(2)
         nc.sync.dma_start(out=p_words[:], in_=net_words.rearrange("g p w -> p g w"))
@@ -337,8 +338,8 @@ def tile_pooled_fisher_connectivity_s3_kernel(
         widen_group(0, 1, True)
         widen_group(1, 1, False)
         widen_group(0, 2, False)
-        for k in PASS_ORDER[:2]:
-            turn_by_matmul(wide[1][:, :, k - 1, :], TURN_BANK + k - 1)
+        for g in range(2):
+            turn_by_matmul(wide[1][:, :, g, :], TURN_BANK + g)
         interleave_early(0, 1)
         interleave_early(0, 2)
         quantise_early(0, 1)
@@ -365,8 +366,10 @@ def tile_pooled_fisher_connectivity_s3_kernel(
         for s in range(-1, LAST - 1):
             projected = (s - 2,) if s >= 2 else ()
             c, j = divmod(s + 5, 2)
-            planes = [(g, t) for g in range(GROUPS) for t in range(PACK)][{-1:slice(0,2),0:slice(2,12)}.get(s, slice(6 * j, 6 * j + 6))] if c < CHUNKS else []
-            on_vector = {0:6,1:1,2:1}.get(s, 0)
+            planes = [(g, t) for g in range(GROUPS) for t in range(PACK)] if c < CHUNKS else []
+            cut = FIRST_STEP_PLANES.get(c, 0)
+            planes = planes[cut:] if j else planes[:cut]
+            on_vector = VECTOR_PLANES.get(s, 0)
             if s >= 0:
                 turn(s, 0, TURN_BANK)
                 turn(s, 1, TURN_BANK + 1)
@@ -377,7 +380,7 @@ def tile_pooled_fisher_connectivity_s3_kernel(
                     weigh(i, h)
             for g, t in planes[:on_vector]:
                 widen(c, g, t, True)
-            if s + 1 in (0,1,2,3):
+            if s + 1 <= WIDENING_ENDS:
                 form_difference(s + 1, slice(0, 1))
                 if s < 0:
                     interleave_seeds(2, 0)

@@ -350,8 +350,9 @@ def tile_pooled_fisher_connectivity_s3_kernel(
         quantise_regions(0)
         widen_group(1, 2, False)
         empty_through(early_grouped[1][:, 2, :, :])
-        interleave_early(0, 0)
         quantise_early(0, 3)
+        interleave_early(0, 0)
+        quantise_early(1, 1)
         quantise_early(0, 0)
         first, second = STEPS[0]
         correlate([(n, piece) for n in range(2) for piece in STEPS[0]])
@@ -360,11 +361,10 @@ def tile_pooled_fisher_connectivity_s3_kernel(
         interleave_regions(1)
         interleave(nc.vector.tensor_copy, early_grouped[1][:, 3, P:, :], wide[1][:, :, 2, P:])
         quantise_regions(1)
-        quantise_early(1, 1)
         correlate([(n, piece) for n in range(PASSES) for piece in STEPS[1]])
 
         for s in range(-1, LAST - 1):
-            projected = (s - 2,) if s >= 2 else ()
+            projected = range(max(s - 2, 0), s - 1 + (s == WIDENING_ENDS + 1)) if s < LAST - 2 else ()
             c, j = divmod(s + 5, 2)
             planes = [(g, t) for g in range(GROUPS) for t in range(PACK)] if c < CHUNKS else []
             cut = FIRST_STEP_PLANES.get(c, 0)

@@ -28,11 +28,12 @@ CHUNKS = M // CHUNK
 LAST = TILES - 1
 
 PASS_ORDER = (1, 2, 3, 0)
+FIRST_STEP_ORDER = (1, 2, 0, 3)
 NEW_RANGES = ((0, CHUNK), (CHUNK, HALF), (HALF, M))
 
 STEPS = [((0, 0), (1, 0)), ((0, 1), (1, 1))] + [((i, 0), (i, 1)) for i in range(2, TILES)]
-FIRST_STEP_PLANES = {2: 2, 3: 6}
-VECTOR_PLANES = {0: 6, 1: 1, 2: 1}
+FIRST_STEP_PLANES = {2: 4, 3: 6}
+VECTOR_PLANES = {-1: 4, 0: 6, 1: 1, 2: 1}
 WIDENING_ENDS = 3
 R_BANKS, TURN_BANK, OUT_BANK = 4, 4, 6
 
@@ -69,7 +70,10 @@ def tile_pooled_fisher_connectivity_s3_kernel(
 
         regions_raw = kept("regions_raw", 2, [P, PACK, HALF], BF16)
         new_raw = [keep.tile([P, PACK, hi - lo], BF16, align_bytes=64, name=f"new_raw_{lo}") for lo, hi in NEW_RANGES]
-        old_bytes = [kept(f"old_bytes_{g}", 2, [P, PACK, HALF], U8) for g in range(GROUPS)]
+        old_bytes = [
+            [kept(f"old_bytes_{g}_{n}", 1 + (g + n == 0), [P, PACK // (1 + (g + n == 0)), HALF], U8) for n in range(2)]
+            for g in range(GROUPS)
+        ]
         old_factor = keep.tile([P, GROUPS, PACK], F32)
         d_words = kept("d_words", 2, [P, GROUPS, 2 * HALF], U8)
         d_scales = keep.tile([P, GROUPS, R], U8, align_bytes=64)
@@ -102,7 +106,11 @@ def tile_pooled_fisher_connectivity_s3_kernel(
         def load_old(n):
             for g in range(GROUPS):
                 rows = seeds_old_bytes.rearrange("(g p t) n -> g p t n", p=P, t=PACK)[g]
-                nc.sync.dma_start(out=old_bytes[g][n][:], in_=rows[:, :, HALF * n : HALF * n + HALF])
+                planes = PACK // len(old_bytes[g][n])
+                for u, tile in enumerate(old_bytes[g][n]):
+                    nc.sync.dma_start(
+                        out=tile[:], in_=rows[:, planes * u : planes * u + planes, HALF * n : HALF * n + HALF]
+                    )
 
         def load_d(h):
             words = old_words.rearrange("g p w -> p g w")
@@ -122,9 +130,9 @@ def tile_pooled_fisher_connectivity_s3_kernel(
         nc.scalar.dma_start(out=weights[:], in_=precision.rearrange("(h p t) -> p h t", p=P, t=PACK))
         load_old(0)
         load_regions(0)
-        load_scale_rows(d_scales, old_scales, GROUPS)
-        load_d(0)
         load_new(0)
+        load_d(0)
+        load_scale_rows(d_scales, old_scales, GROUPS)
         load_regions(1)
         load_d(1)
         load_new(1)
@@ -139,7 +147,8 @@ def tile_pooled_fisher_connectivity_s3_kernel(
 
         def widen(c, g, t, on_vector):
             n, lo = divmod(CHUNK * c, HALF)
-            src = old_bytes[g][n][:, t, lo : lo + CHUNK].bitcast(FP8)
+            u, row = divmod(t, PACK // len(old_bytes[g][n]))
+            src = old_bytes[g][n][u][:, row, lo : lo + CHUNK].bitcast(FP8)
             factor = old_factor[:, g, t : t + 1]
             if on_vector:
                 nc.vector.tensor_scalar(out=wide[c][:, t, g, :], in0=src, scalar1=factor, scalar2=None, op0=ALU.mult)
@@ -227,11 +236,11 @@ def tile_pooled_fisher_connectivity_s3_kernel(
 
         r = {}
 
-        def correlate(order):
+        def correlate(order, passes=PASS_ORDER):
             for n, (i, h) in order:
                 if n == 0:
                     r[i, h] = bank(len(r) % R_BANKS, [P, HALF])
-                k = PASS_ORDER[n]
+                k = passes[n]
                 c, j = divmod(i, CHUNK // P)
                 if c == 0 or (c == 1 and k > 0):
                     fixed, fixed_scale = early_codes[c][:, k, P * j : P * j + P], early_scales[c][:, k, P * j : P * j + P]
@@ -253,24 +262,25 @@ def tile_pooled_fisher_connectivity_s3_kernel(
                 )
 
         ln_plus, ln_minus, difference = {}, {}, {}
-        all_planes = slice(0, PACK)
 
-        def take_logarithms(s, n, planes=all_planes):
+        def take_logarithms(s, n):
             if s not in ln_plus:
                 ln_plus[s] = work.tile([P, 2, PACK, P], F32, name="ln_plus")
                 ln_minus[s] = work.tile([P, 2, PACK, P], F32, name="ln_minus")
                 difference[s] = work.tile([P, 2, PACK, P], F32, name="difference")
-            by_t = r[STEPS[s][n]][:].rearrange("s (p t) -> s t p", t=PACK)[:, planes, :]
-            nc.scalar.activation(out=ln_minus[s][:, n, planes, :], in_=by_t, func=ACT.Ln, bias=1.0, scale=-1.0)
-            nc.scalar.activation(out=ln_plus[s][:, n, planes, :], in_=by_t, func=ACT.Ln, bias=1.0, scale=1.0)
+            by_t = r[STEPS[s][n]][:].rearrange("s (p t) -> s t p", t=PACK)
+            nc.scalar.activation(out=ln_minus[s][:, n, :, :], in_=by_t, func=ACT.Ln, bias=1.0, scale=-1.0)
+            nc.scalar.activation(out=ln_plus[s][:, n, :, :], in_=by_t, func=ACT.Ln, bias=1.0, scale=1.0)
 
-        def form_difference(s, pieces, planes=all_planes):
-            dst = difference[s][:, pieces, planes, :]
-            minus = ln_minus[s][:, pieces, planes, :]
-            if adds_in_psum(s, pieces.start):
+        def form_difference(s, pieces):
+            dst = difference[s][:, pieces, :, :]
+            minus = ln_minus[s][:, pieces, :, :]
+            if not adds_in_psum(s, pieces.start):
+                nc.vector.tensor_tensor(out=dst, in0=ln_plus[s][:, pieces, :, :], in1=minus, op=ALU.subtract)
+            elif s < LAST:
                 nc.vector.tensor_scalar(out=dst, in0=minus, scalar1=-1.0, scalar2=None, op0=ALU.mult)
             else:
-                nc.vector.tensor_tensor(out=dst, in0=ln_plus[s][:, pieces, planes, :], in1=minus, op=ALU.subtract)
+                nc.scalar.activation(out=dst, in_=minus, func=ACT.Copy, scale=-1.0)
 
         turned = {}
 
@@ -335,33 +345,33 @@ def tile_pooled_fisher_connectivity_s3_kernel(
 
         widen_group(0, 0, True)
         widen_group(1, 0, False)
+        interleave_early(0, 1)
         widen_group(0, 1, True)
         widen_group(1, 1, False)
-        widen_group(0, 2, False)
-        for g in range(2):
-            turn_by_matmul(wide[1][:, :, g, :], TURN_BANK + g)
-        interleave_early(0, 1)
+        turn_by_matmul(wide[1][:, :, 0, :], TURN_BANK)
         interleave_early(0, 2)
         quantise_early(0, 1)
-        empty_through(early_grouped[1][:, 1, :, :])
+        quantise_early(0, 2)
+        widen_group(0, 2, False)
+        turn_by_matmul(wide[1][:, :, 1, :], TURN_BANK + 1)
+        widen_group(1, 2, False)
+        turn_by_matmul(wide[1][:, :, 2, :], OUT_BANK)
         interleave_early(0, 3, nc.scalar.copy)
         interleave_regions(0)
-        quantise_early(0, 2)
-        quantise_regions(0)
-        widen_group(1, 2, False)
-        empty_through(early_grouped[1][:, 2, :, :])
-        quantise_early(0, 3)
         interleave_early(0, 0)
-        quantise_early(1, 1)
+        quantise_regions(0)
         quantise_early(0, 0)
-        first, second = STEPS[0]
-        correlate([(n, piece) for n in range(2) for piece in STEPS[0]])
-        correlate([(2, first), (3, first), (2, second), (3, second)])
-        interleave(nc.scalar.copy, early_grouped[1][:, 3, :P, :], wide[1][:, :, 2, :P])
+        quantise_early(0, 3)
+        for g in range(GROUPS):
+            empty_through(early_grouped[1][:, 1 + g, :, :])
+        correlate([(n, piece) for piece in STEPS[0] for n in range(PASSES)], FIRST_STEP_ORDER)
+        quantise_early(1, 1)
+        quantise_early(1, 2)
         interleave_regions(1)
-        interleave(nc.vector.tensor_copy, early_grouped[1][:, 3, P:, :], wide[1][:, :, 2, P:])
+        quantise_early(1, 3)
         quantise_regions(1)
-        correlate([(n, piece) for n in range(PASSES) for piece in STEPS[1]])
+        correlate([(n, piece) for piece in STEPS[1] for n in range(GROUPS)])
+        correlate([(GROUPS, piece) for piece in STEPS[1]])
 
         for s in range(-1, LAST - 1):
             projected = range(max(s - 2, 0), s - 1 + (s == WIDENING_ENDS + 1)) if s < LAST - 2 else ()
@@ -378,15 +388,17 @@ def tile_pooled_fisher_connectivity_s3_kernel(
             if s >= 0:
                 for i, h in STEPS[s]:
                     weigh(i, h)
-            for g, t in planes[:on_vector]:
-                widen(c, g, t, True)
+                for g, t in planes[:on_vector]:
+                    widen(c, g, t, True)
             if s + 1 <= WIDENING_ENDS:
                 form_difference(s + 1, slice(0, 1))
-                if s < 0:
-                    interleave_seeds(2, 0)
                 form_difference(s + 1, slice(1, 2))
             else:
                 form_difference(s + 1, slice(0, 2))
+            if s < 0:
+                interleave_seeds(2, 0, nc.scalar.copy)
+                for g, t in planes[:on_vector]:
+                    widen(c, g, t, True)
             for i in projected:
                 project(i, OUT_BANK + i % 2)
             if s >= 0:
@@ -395,38 +407,34 @@ def tile_pooled_fisher_connectivity_s3_kernel(
                 widen(c, g, t, False)
             if 0 <= s < TILES - 3:
                 interleave_seeds(s + 3, 0, gpsimd_copy)
-                if s >= WIDENING_ENDS:
-                    interleave_seeds(s + 3, GROUPS, nc.scalar.copy)
-                    interleave_old(s + 3, GROUPS - 1)
-                elif s > 0:
-                    interleave_old(s + 3, GROUPS)
+                on_scalar = max(s + 1 - WIDENING_ENDS, 0)
+                for k in range(PASSES - on_scalar, PASSES):
+                    interleave_seeds(s + 3, k, nc.scalar.copy)
+                if s > 0:
+                    interleave_old(s + 3, GROUPS - on_scalar)
             for i in projected:
                 store(i)
-            if s >= 2:
+            if s == LAST - 2:
                 quantise_z(s)
-            elif s >= 0:
-                for i, h in STEPS[s]:
+            else:
+                pieces = STEPS[s] if s >= 0 else ()
+                for i, h in pieces[:1]:
                     quantise_z(i, slice(h, h + 1))
-            if s < 0:
-                quantise_early(1, 2)
-                quantise_early(1, 3)
-            if s < TILES - 3:
                 quantise_seeds(s + 3)
+                for i, h in pieces[1:]:
+                    quantise_z(i, slice(h, h + 1))
 
-        low, high = slice(0, 2), slice(2, PACK)
         take_logarithms(LAST, 0)
         turn(LAST - 1, 0, TURN_BANK)
         turn(LAST - 1, 1, TURN_BANK + 1)
         project(LAST - 3, OUT_BANK)
         project(LAST - 2, OUT_BANK + 1)
         form_difference(LAST, slice(0, 1))
-        take_logarithms(LAST, 1, low)
-        take_logarithms(LAST, 1, high)
+        take_logarithms(LAST, 1)
         turn(LAST, 0, 0)
         weigh(LAST - 1, 0)
-        form_difference(LAST, slice(1, 2), low)
+        form_difference(LAST, slice(1, 2))
         weigh(LAST - 1, 1)
-        form_difference(LAST, slice(1, 2), high)
         turn(LAST, 1, 1)
         store(LAST - 3)
         store(LAST - 2)

@@ -28,12 +28,11 @@ CHUNKS = M // CHUNK
 LAST = TILES - 1
 
 PASS_ORDER = (1, 2, 3, 0)
-FIRST_STEP_ORDER = (1, 2, 0, 3)
 NEW_RANGES = ((0, CHUNK), (CHUNK, HALF), (HALF, M))
 
 STEPS = [((0, 0), (1, 0)), ((0, 1), (1, 1))] + [((i, 0), (i, 1)) for i in range(2, TILES)]
-FIRST_STEP_PLANES = {2: 4, 3: 6}
-VECTOR_PLANES = {-1: 4, 0: 6, 1: 1, 2: 1}
+FIRST_STEP_PLANES = {2: 2, 3: 6}
+VECTOR_PLANES = {0: 6, 1: 1, 2: 1}
 WIDENING_ENDS = 3
 R_BANKS, TURN_BANK, OUT_BANK = 4, 4, 6
 
@@ -130,9 +129,9 @@ def tile_pooled_fisher_connectivity_s3_kernel(
         nc.scalar.dma_start(out=weights[:], in_=precision.rearrange("(h p t) -> p h t", p=P, t=PACK))
         load_old(0)
         load_regions(0)
-        load_new(0)
-        load_d(0)
         load_scale_rows(d_scales, old_scales, GROUPS)
+        load_d(0)
+        load_new(0)
         load_regions(1)
         load_d(1)
         load_new(1)
@@ -236,11 +235,11 @@ def tile_pooled_fisher_connectivity_s3_kernel(
 
         r = {}
 
-        def correlate(order, passes=PASS_ORDER):
+        def correlate(order):
             for n, (i, h) in order:
                 if n == 0:
                     r[i, h] = bank(len(r) % R_BANKS, [P, HALF])
-                k = passes[n]
+                k = PASS_ORDER[n]
                 c, j = divmod(i, CHUNK // P)
                 if c == 0 or (c == 1 and k > 0):
                     fixed, fixed_scale = early_codes[c][:, k, P * j : P * j + P], early_scales[c][:, k, P * j : P * j + P]
@@ -348,30 +347,30 @@ def tile_pooled_fisher_connectivity_s3_kernel(
         interleave_early(0, 1)
         widen_group(0, 1, True)
         widen_group(1, 1, False)
-        turn_by_matmul(wide[1][:, :, 0, :], TURN_BANK)
+        widen_group(0, 2, False)
+        for g in range(2):
+            turn_by_matmul(wide[1][:, :, g, :], TURN_BANK + g)
         interleave_early(0, 2)
         quantise_early(0, 1)
-        quantise_early(0, 2)
-        widen_group(0, 2, False)
-        turn_by_matmul(wide[1][:, :, 1, :], TURN_BANK + 1)
-        widen_group(1, 2, False)
-        turn_by_matmul(wide[1][:, :, 2, :], OUT_BANK)
         interleave_early(0, 3, nc.scalar.copy)
         interleave_regions(0)
-        interleave_early(0, 0)
+        quantise_early(0, 2)
         quantise_regions(0)
-        quantise_early(0, 0)
+        widen_group(1, 2, False)
+        empty_through(early_grouped[1][:, 1, :, :])
         quantise_early(0, 3)
-        for g in range(GROUPS):
-            empty_through(early_grouped[1][:, 1 + g, :, :])
-        correlate([(n, piece) for piece in STEPS[0] for n in range(PASSES)], FIRST_STEP_ORDER)
+        interleave_early(0, 0)
         quantise_early(1, 1)
-        quantise_early(1, 2)
+        quantise_early(0, 0)
+        empty_through(early_grouped[1][:, 2, :, :])
+        first, second = STEPS[0]
+        correlate([(n, piece) for n in range(2) for piece in STEPS[0]])
+        correlate([(2, first), (3, first), (2, second), (3, second)])
+        interleave(nc.scalar.copy, early_grouped[1][:, 3, :P, :], wide[1][:, :, 2, :P])
         interleave_regions(1)
-        quantise_early(1, 3)
+        interleave(nc.vector.tensor_copy, early_grouped[1][:, 3, P:, :], wide[1][:, :, 2, P:])
         quantise_regions(1)
-        correlate([(n, piece) for piece in STEPS[1] for n in range(GROUPS)])
-        correlate([(GROUPS, piece) for piece in STEPS[1]])
+        correlate([(n, piece) for n in range(PASSES) for piece in STEPS[1]])
 
         for s in range(-1, LAST - 1):
             projected = range(max(s - 2, 0), s - 1 + (s == WIDENING_ENDS + 1)) if s < LAST - 2 else ()
@@ -388,17 +387,15 @@ def tile_pooled_fisher_connectivity_s3_kernel(
             if s >= 0:
                 for i, h in STEPS[s]:
                     weigh(i, h)
-                for g, t in planes[:on_vector]:
-                    widen(c, g, t, True)
+            for g, t in planes[:on_vector]:
+                widen(c, g, t, True)
             if s + 1 <= WIDENING_ENDS:
                 form_difference(s + 1, slice(0, 1))
+                if s < 0:
+                    interleave_seeds(2, 0)
                 form_difference(s + 1, slice(1, 2))
             else:
                 form_difference(s + 1, slice(0, 2))
-            if s < 0:
-                interleave_seeds(2, 0, nc.scalar.copy)
-                for g, t in planes[:on_vector]:
-                    widen(c, g, t, True)
             for i in projected:
                 project(i, OUT_BANK + i % 2)
             if s >= 0:
@@ -407,7 +404,7 @@ def tile_pooled_fisher_connectivity_s3_kernel(
                 widen(c, g, t, False)
             if 0 <= s < TILES - 3:
                 interleave_seeds(s + 3, 0, gpsimd_copy)
-                on_scalar = max(s + 1 - WIDENING_ENDS, 0)
+                on_scalar = int(s >= WIDENING_ENDS)
                 for k in range(PASSES - on_scalar, PASSES):
                     interleave_seeds(s + 3, k, nc.scalar.copy)
                 if s > 0:
@@ -417,6 +414,9 @@ def tile_pooled_fisher_connectivity_s3_kernel(
             if s == LAST - 2:
                 quantise_z(s)
             else:
+                if s < 0:
+                    quantise_early(1, 2)
+                    quantise_early(1, 3)
                 pieces = STEPS[s] if s >= 0 else ()
                 for i, h in pieces[:1]:
                     quantise_z(i, slice(h, h + 1))

@@ -27,18 +27,20 @@ TILES = M // P
 CHUNKS = M // CHUNK
 LAST = TILES - 1
 
-PASS_ORDER = (1, 2, 3, 0)
 NEW_RANGES = ((0, CHUNK), (CHUNK, HALF), (HALF, M))
 
 STEPS = [((0, 0), (1, 0)), ((0, 1), (1, 1))] + [((i, 0), (i, 1)) for i in range(2, TILES)]
-FIRST_STEP_PLANES = {2: 2, 3: 6}
-VECTOR_PLANES = {0: 6, 1: 1, 2: 1}
-WIDENING_ENDS = 3
-R_BANKS, TURN_BANK, OUT_BANK = 4, 4, 6
+ADDING_ENDS = 3
+SCALAR_INTERLEAVES = 6
+TURN_BANK, OUT_BANK = 4, 6
+
+
+def r_bank(s):
+    return OUT_BANK if s == 2 else 2 * ((s if s < 2 else s - 1) % 2)
 
 
 def adds_in_psum(s, n):
-    return n == 1 and s != 1 and (s <= WIDENING_ENDS or s == LAST)
+    return s == 0 or (n == 1 and (s <= ADDING_ENDS or s == LAST))
 
 
 def tile_pooled_fisher_connectivity_s3_kernel(
@@ -69,12 +71,9 @@ def tile_pooled_fisher_connectivity_s3_kernel(
 
         regions_raw = kept("regions_raw", 2, [P, PACK, HALF], BF16)
         new_raw = [keep.tile([P, PACK, hi - lo], BF16, align_bytes=64, name=f"new_raw_{lo}") for lo, hi in NEW_RANGES]
-        old_bytes = [
-            [kept(f"old_bytes_{g}_{n}", 1 + (g + n == 0), [P, PACK // (1 + (g + n == 0)), HALF], U8) for n in range(2)]
-            for g in range(GROUPS)
-        ]
+        old_bytes = [kept(f"old_bytes_{g}", 1 + (g == 0), [P, PACK // (1 + (g == 0)), M], U8) for g in range(GROUPS)]
         old_factor = keep.tile([P, GROUPS, PACK], F32)
-        d_words = kept("d_words", 2, [P, GROUPS, 2 * HALF], U8)
+        d_words = kept("d_words", GROUPS, [P, 2 * R], U8)
         d_scales = keep.tile([P, GROUPS, R], U8, align_bytes=64)
         p_words = keep.tile([P, 2, 2 * E], U8, align_bytes=64)
         p_scales = keep.tile([P, 2, E], U8, align_bytes=64)
@@ -102,40 +101,36 @@ def tile_pooled_fisher_connectivity_s3_kernel(
             lo, hi = NEW_RANGES[n]
             nc.sync.dma_start(out=new_raw[n][:], in_=seeds_new.rearrange("(p t) n -> p t n", t=PACK)[:, :, lo:hi])
 
-        def load_old(n):
-            for g in range(GROUPS):
-                rows = seeds_old_bytes.rearrange("(g p t) n -> g p t n", p=P, t=PACK)[g]
-                planes = PACK // len(old_bytes[g][n])
-                for u, tile in enumerate(old_bytes[g][n]):
-                    nc.sync.dma_start(
-                        out=tile[:], in_=rows[:, planes * u : planes * u + planes, HALF * n : HALF * n + HALF]
-                    )
+        def load_old(g):
+            rows = seeds_old_bytes.rearrange("(g p t) n -> g p t n", p=P, t=PACK)[g]
+            planes = PACK // len(old_bytes[g])
+            for u, tile in enumerate(old_bytes[g]):
+                nc.sync.dma_start(out=tile[:], in_=rows[:, planes * u : planes * u + planes, :])
 
-        def load_d(h):
-            words = old_words.rearrange("g p w -> p g w")
-            nc.sync.dma_start(out=d_words[h][:], in_=words[:, :, 2 * HALF * h : 2 * HALF * h + 2 * HALF])
+        def load_d(g):
+            nc.sync.dma_start(out=d_words[g][:], in_=old_words[g])
 
         def load_scale_rows(tile, rows, groups):
-            for q in range(4):
-                quadrant = tile[32 * q : 32 * q + 4].rearrange("p g n -> p (g n)").bitcast(I32)
+            for j in range(4):
                 nc.sync.dma_start(
-                    out=quadrant.rearrange("p (g n) -> p g n", g=groups),
-                    in_=rows[:, 4 * q : 4 * q + 4, :].bitcast(I32).rearrange("g r n -> r g n"),
+                    out=tile[j:P:32].rearrange("p g n -> p (g n)").bitcast(I32).rearrange("p (g n) -> p g n", g=groups),
+                    in_=rows.bitcast(I32).rearrange("g (q j) n -> j q g n", j=4)[j],
                 )
 
         nc.scalar.dma_start(
             out=old_factor[:], in_=seeds_old_scale.rearrange("(g p t) o -> p g (t o)", p=P, t=PACK)
         )
         nc.scalar.dma_start(out=weights[:], in_=precision.rearrange("(h p t) -> p h t", p=P, t=PACK))
-        load_old(0)
-        load_regions(0)
+        for g in range(GROUPS):
+            load_old(g)
         load_scale_rows(d_scales, old_scales, GROUPS)
         load_d(0)
+        load_regions(0)
         load_new(0)
-        load_regions(1)
         load_d(1)
+        load_d(2)
+        load_regions(1)
         load_new(1)
-        load_old(1)
         load_new(2)
         nc.sync.dma_start(out=p_words[:], in_=net_words.rearrange("g p w -> p g w"))
         load_scale_rows(p_scales, net_scales, 2)
@@ -145,17 +140,16 @@ def tile_pooled_fisher_connectivity_s3_kernel(
         wide = kept("wide", CHUNKS, [P, PACK, GROUPS, CHUNK], BF16)
 
         def widen(c, g, t, on_vector):
-            n, lo = divmod(CHUNK * c, HALF)
-            u, row = divmod(t, PACK // len(old_bytes[g][n]))
-            src = old_bytes[g][n][u][:, row, lo : lo + CHUNK].bitcast(FP8)
+            u, row = divmod(t, PACK // len(old_bytes[g]))
+            src = old_bytes[g][u][:, row, CHUNK * c : CHUNK * c + CHUNK].bitcast(FP8)
             factor = old_factor[:, g, t : t + 1]
             if on_vector:
                 nc.vector.tensor_scalar(out=wide[c][:, t, g, :], in0=src, scalar1=factor, scalar2=None, op0=ALU.mult)
             else:
                 nc.scalar.activation(out=wide[c][:, t, g, :], in_=src, func=ACT.Copy, scale=factor)
 
-        def widen_group(c, g, on_vector):
-            for t in range(PACK):
+        def widen_group(c, g, on_vector, planes=range(PACK)):
+            for t in planes:
                 widen(c, g, t, on_vector)
 
         def interleave(copy, dst, src):
@@ -195,7 +189,7 @@ def tile_pooled_fisher_connectivity_s3_kernel(
         early_scales = kept("early_scales", 2, [P, PASSES, CHUNK], U8)
 
         def interleave_early(c, k, copy=nc.vector.tensor_copy):
-            interleave(copy, early_grouped[c][:, k, :, :], new_raw[0][:] if k == 0 else wide[c][:, :, k - 1, :])
+            interleave(copy, early_grouped[c][:, k, :, :], new_raw[c][:] if k == 0 else wide[c][:, :, k - 1, :])
 
         def quantise_early(c, k):
             quantise(
@@ -206,10 +200,9 @@ def tile_pooled_fisher_connectivity_s3_kernel(
 
         def interleave_seeds(i, k, copy=nc.vector.tensor_copy):
             if i not in grouped:
-                passes = 1 if P * i < HALF else PASSES
-                grouped[i] = work.tile([P, passes, P, PACK], BF16, align_bytes=64, name="grouped", bufs=1)
-                codes[i] = work.tile([P, passes, P], U32, align_bytes=64, name="codes")
-                scales[i] = work.tile([P, passes, P], U8, align_bytes=64, name="scales")
+                grouped[i] = work.tile([P, PASSES, P, PACK], BF16, align_bytes=64, name="grouped", bufs=1)
+                codes[i] = work.tile([P, PASSES, P], U32, align_bytes=64, name="codes")
+                scales[i] = work.tile([P, PASSES, P], U8, align_bytes=64, name="scales")
             if k == 0:
                 n = [lo <= P * i < hi for lo, hi in NEW_RANGES].index(True)
                 lo = P * i - NEW_RANGES[n][0]
@@ -233,22 +226,24 @@ def tile_pooled_fisher_connectivity_s3_kernel(
                 grouped[i][:].rearrange("p k n t -> p (k n t)"),
             )
 
-        r = {}
+        r, passes_done = {}, {}
 
-        def correlate(order):
-            for n, (i, h) in order:
-                if n == 0:
-                    r[i, h] = bank(len(r) % R_BANKS, [P, HALF])
-                k = PASS_ORDER[n]
+        def correlate(s, passes, pieces=(0, 1)):
+            for n, k in [(n, k) for n in pieces for k in passes]:
+                i, h = STEPS[s][n]
+                if (i, h) not in r:
+                    r[i, h] = bank(r_bank(s) + n, [P, HALF])
+                done = passes_done.get((i, h), 0)
+                passes_done[i, h] = done + 1
                 c, j = divmod(i, CHUNK // P)
-                if c == 0 or (c == 1 and k > 0):
+                if c < 2:
                     fixed, fixed_scale = early_codes[c][:, k, P * j : P * j + P], early_scales[c][:, k, P * j : P * j + P]
                 else:
                     fixed, fixed_scale = codes[i][:, k, :], scales[i][:, k, :]
                 if k == 0:
                     moving, moving_scale = regions_codes[h][:].bitcast(FP8X4), regions_scales[h][:]
                 else:
-                    moving = d_words[h][:, k - 1, :].bitcast(FP4X4)
+                    moving = d_words[k - 1][:, 2 * HALF * h : 2 * HALF * h + 2 * HALF].bitcast(FP4X4)
                     moving_scale = d_scales[:, k - 1, HALF * h : HALF * h + HALF]
                 nc.tensor.matmul_mx(
                     out=r[i, h][:],
@@ -256,8 +251,8 @@ def tile_pooled_fisher_connectivity_s3_kernel(
                     lhsT_scale=fixed_scale,
                     rhs=moving,
                     rhs_scale=moving_scale,
-                    start=(n == 0),
-                    stop=(n == PASSES - 1),
+                    start=(done == 0),
+                    stop=(done == PASSES - 1),
                 )
 
         ln_plus, ln_minus, difference = {}, {}, {}
@@ -303,8 +298,8 @@ def tile_pooled_fisher_connectivity_s3_kernel(
         def weigh(i, h):
             if h == 0:
                 z_grouped[i] = work.tile([P, 2, P, PACK], BF16, align_bytes=64, name="z_grouped", bufs=4)
-                z_codes[i] = work.tile([P, 2, P], U32, align_bytes=64, name="z_codes", bufs=4)
-                z_scales[i] = work.tile([P, 2, P], U8, align_bytes=64, name="z_scales", bufs=4)
+                z_codes[i] = work.tile([P, 2, P], U32, align_bytes=64, name="z_codes", bufs=5)
+                z_scales[i] = work.tile([P, 2, P], U8, align_bytes=64, name="z_scales", bufs=5)
             nc.vector.tensor_tensor(
                 out=z_grouped[i][:, h, :, :].rearrange("p (n e) t -> p n t e", e=2),
                 in0=turned[i, h][:],
@@ -342,107 +337,129 @@ def tile_pooled_fisher_connectivity_s3_kernel(
             nc.scalar.copy(out=result[:], in_=out_bank[i][:])
             nc.sync.dma_start(out=out[P * i : P * i + P, :], in_=result[:])
 
+        low, high = range(2), range(2, PACK)
         widen_group(0, 0, True)
         widen_group(1, 0, False)
         interleave_early(0, 1)
+        widen_group(2, 0, False, low)
         widen_group(0, 1, True)
         widen_group(1, 1, False)
         widen_group(0, 2, False)
         for g in range(2):
             turn_by_matmul(wide[1][:, :, g, :], TURN_BANK + g)
-        interleave_early(0, 2)
         quantise_early(0, 1)
-        interleave_early(0, 3, nc.scalar.copy)
-        interleave_regions(0)
+        interleave_early(0, 2)
+        widen_group(1, 2, True)
         quantise_early(0, 2)
-        quantise_regions(0)
-        widen_group(1, 2, False)
         empty_through(early_grouped[1][:, 1, :, :])
-        quantise_early(0, 3)
-        interleave_early(0, 0)
+        interleave_early(0, 3, nc.scalar.copy)
+        interleave_early(1, 3)
         quantise_early(1, 1)
-        quantise_early(0, 0)
+        quantise_early(1, 3)
         empty_through(early_grouped[1][:, 2, :, :])
-        first, second = STEPS[0]
-        correlate([(n, piece) for n in range(2) for piece in STEPS[0]])
-        correlate([(2, first), (3, first), (2, second), (3, second)])
-        interleave(nc.scalar.copy, early_grouped[1][:, 3, :P, :], wide[1][:, :, 2, :P])
+        widen_group(2, 0, True, high)
+        interleave_regions(0)
+        quantise_early(0, 3)
+        quantise_regions(0)
+        quantise_early(1, 2)
+        interleave_early(0, 0, nc.scalar.copy)
+        quantise_early(0, 0)
+        widen_group(2, 1, True)
+        widen_group(2, 2, False)
+        for s in range(3):
+            correlate(s, [1])
+        correlate(0, [2])
+        correlate(0, [3])
+        correlate(1, [2], [0])
+        correlate(0, [0])
+        correlate(1, [2], [1])
+        correlate(1, [3])
+        correlate(2, [2, 3])
+        take_logarithms(0, 0)
+        take_logarithms(0, 1)
         interleave_regions(1)
-        interleave(nc.vector.tensor_copy, early_grouped[1][:, 3, P:, :], wide[1][:, :, 2, P:])
+        form_difference(0, slice(0, 1))
         quantise_regions(1)
-        correlate([(n, piece) for n in range(PASSES) for piece in STEPS[1]])
+        form_difference(0, slice(1, 2))
+        handover = work.tile([P, CHUNK, PACK], BF16, align_bytes=64, name="grouped", bufs=1)
+        interleave(nc.vector.tensor_copy, handover[:], new_raw[1][:])
+        widen(3, 0, 0, True)
+        quantise(early_codes[1][:, 0, :], early_scales[1][:, 0, :], handover[:].rearrange("p n t -> p (n t)"))
 
-        for s in range(-1, LAST - 1):
-            projected = range(max(s - 2, 0), s - 1 + (s == WIDENING_ENDS + 1)) if s < LAST - 2 else ()
-            c, j = divmod(s + 5, 2)
-            planes = [(g, t) for g in range(GROUPS) for t in range(PACK)] if c < CHUNKS else []
-            cut = FIRST_STEP_PLANES.get(c, 0)
-            planes = planes[cut:] if j else planes[:cut]
-            on_vector = VECTOR_PLANES.get(s, 0)
-            if s >= 0:
-                turn(s, 0, TURN_BANK)
-                turn(s, 1, TURN_BANK + 1)
+        for s in range(LAST - 2):
+            turn(s, 0, TURN_BANK)
+            turn(s, 1, TURN_BANK + 1)
+            if s == 0:
+                correlate(1, [0])
+                widen_group(3, 0, False, range(1, PACK))
+                widen_group(3, 1, False)
             take_logarithms(s + 1, 0)
             take_logarithms(s + 1, 1)
-            if s >= 0:
-                for i, h in STEPS[s]:
-                    weigh(i, h)
-            for g, t in planes[:on_vector]:
-                widen(c, g, t, True)
-            if s + 1 <= WIDENING_ENDS:
+            if s == 1:
+                widen_group(3, 2, False)
+            for i, h in STEPS[s]:
+                weigh(i, h)
+            preparing = s + 4 < TILES
+            on_scalar = int(s + 4 >= SCALAR_INTERLEAVES)
+            if preparing:
+                interleave_seeds(s + 4, 0, gpsimd_copy)
+            if s == 0:
+                correlate(2, [0])
+                interleave_old(4, GROUPS)
+                quantise_z(0, slice(0, 1))
+            if adds_in_psum(s + 1, 1):
                 form_difference(s + 1, slice(0, 1))
-                if s < 0:
-                    interleave_seeds(2, 0)
                 form_difference(s + 1, slice(1, 2))
             else:
                 form_difference(s + 1, slice(0, 2))
-            for i in projected:
-                project(i, OUT_BANK + i % 2)
-            if s >= 0:
-                correlate([(n, piece) for piece in STEPS[s + 2] for n in range(PASSES)])
-            for g, t in planes[on_vector:]:
-                widen(c, g, t, False)
-            if 0 <= s < TILES - 3:
-                interleave_seeds(s + 3, 0, gpsimd_copy)
-                on_scalar = int(s >= WIDENING_ENDS)
-                for k in range(PASSES - on_scalar, PASSES):
-                    interleave_seeds(s + 3, k, nc.scalar.copy)
-                if s > 0:
-                    interleave_old(s + 3, GROUPS - on_scalar)
-            for i in projected:
-                store(i)
-            if s == LAST - 2:
+            if s >= 2:
+                project(s - 2, OUT_BANK + s % 2)
+            correlate(s + 3, (1, 2, 3, 0))
+            if preparing and s > 0:
+                if on_scalar:
+                    interleave_seeds(s + 4, GROUPS, nc.scalar.copy)
+                interleave_old(s + 4, GROUPS - on_scalar)
+            if 2 <= s < LAST - 3:
+                store(s - 2)
+            if s >= 2:
                 quantise_z(s)
             else:
-                if s < 0:
-                    quantise_early(1, 2)
-                    quantise_early(1, 3)
-                pieces = STEPS[s] if s >= 0 else ()
-                for i, h in pieces[:1]:
+                for i, h in STEPS[s][1 - s :]:
                     quantise_z(i, slice(h, h + 1))
-                quantise_seeds(s + 3)
-                for i, h in pieces[1:]:
-                    quantise_z(i, slice(h, h + 1))
+            if preparing:
+                quantise_seeds(s + 4)
 
+        take_logarithms(LAST - 1, 0)
+        take_logarithms(LAST - 1, 1)
+        store(LAST - 5)
+        turn(LAST - 2, 0, TURN_BANK)
+        turn(LAST - 2, 1, TURN_BANK + 1)
+        project(LAST - 4, OUT_BANK + 1)
+        form_difference(LAST - 1, slice(0, 2))
         take_logarithms(LAST, 0)
-        turn(LAST - 1, 0, TURN_BANK)
-        turn(LAST - 1, 1, TURN_BANK + 1)
-        project(LAST - 3, OUT_BANK)
-        project(LAST - 2, OUT_BANK + 1)
-        form_difference(LAST, slice(0, 1))
         take_logarithms(LAST, 1)
-        turn(LAST, 0, 0)
-        weigh(LAST - 1, 0)
+        turn(LAST - 1, 0, r_bank(LAST - 1))
+        turn(LAST - 1, 1, r_bank(LAST - 1) + 1)
+        project(LAST - 3, OUT_BANK)
+        weigh(LAST - 2, 0)
+        weigh(LAST - 2, 1)
+        form_difference(LAST, slice(0, 1))
+        quantise_z(LAST - 2)
         form_difference(LAST, slice(1, 2))
-        weigh(LAST - 1, 1)
-        turn(LAST, 1, 1)
+        store(LAST - 4)
         store(LAST - 3)
-        store(LAST - 2)
-        quantise_z(LAST - 1)
+        weigh(LAST - 1, 0)
+        weigh(LAST - 1, 1)
+        turn(LAST, 0, r_bank(LAST))
+        turn(LAST, 1, r_bank(LAST) + 1)
+        project(LAST - 2, TURN_BANK)
+        for h in range(2):
+            quantise_z(LAST - 1, slice(h, h + 1))
         weigh(LAST, 0)
         weigh(LAST, 1)
-        project(LAST - 1, 2)
-        quarters = [bank(3 + q, [P, P]) for q in range(4)]
+        project(LAST - 1, TURN_BANK + 1)
+        store(LAST - 2)
+        quarters = [bank(number, [P, P]) for number in (r_bank(LAST - 1), r_bank(LAST - 1) + 1, OUT_BANK, OUT_BANK + 1)]
         for h in range(2):
             quantise_z(LAST, slice(h, h + 1))
             for q in range(4):

@@ -30,8 +30,7 @@ LAST = TILES - 1
 NEW_RANGES = ((0, CHUNK), (CHUNK, HALF), (HALF, M))
 
 STEPS = [((0, 0), (1, 0)), ((0, 1), (1, 1))] + [((i, 0), (i, 1)) for i in range(2, TILES)]
-ADDING_ENDS = 3
-SCALAR_INTERLEAVES = 6
+ADDING_ENDS = 2
 TURN_BANK, OUT_BANK = 4, 6
 
 
@@ -137,20 +136,20 @@ def tile_pooled_fisher_connectivity_s3_kernel(
 
         nc.scalar.activation(out=one[:], in_=one[:], func=ACT.Ln)
 
-        wide = kept("wide", CHUNKS, [P, PACK, GROUPS, CHUNK], BF16)
+        halves = kept("wide", 2, [P, PACK, GROUPS, HALF], BF16)
+        wide = [halves[c // 2][:, :, :, CHUNK * (c % 2) : CHUNK * (c % 2) + CHUNK] for c in range(CHUNKS)]
 
-        def widen(c, g, t, on_vector):
-            u, row = divmod(t, PACK // len(old_bytes[g]))
-            src = old_bytes[g][u][:, row, CHUNK * c : CHUNK * c + CHUNK].bitcast(FP8)
-            factor = old_factor[:, g, t : t + 1]
-            if on_vector:
-                nc.vector.tensor_scalar(out=wide[c][:, t, g, :], in0=src, scalar1=factor, scalar2=None, op0=ALU.mult)
-            else:
-                nc.scalar.activation(out=wide[c][:, t, g, :], in_=src, func=ACT.Copy, scale=factor)
-
-        def widen_group(c, g, on_vector, planes=range(PACK)):
+        def widen(chunks, g, planes, on_vector):
+            lo, hi = CHUNK * chunks[0], CHUNK * (chunks[-1] + 1)
             for t in planes:
-                widen(c, g, t, on_vector)
+                u, row = divmod(t, PACK // len(old_bytes[g]))
+                src = old_bytes[g][u][:, row, lo:hi].bitcast(FP8)
+                dst = halves[lo // HALF][:, t, g, lo % HALF : lo % HALF + hi - lo]
+                factor = old_factor[:, g, t : t + 1]
+                if on_vector:
+                    nc.vector.tensor_scalar(out=dst, in0=src, scalar1=factor, scalar2=None, op0=ALU.mult)
+                else:
+                    nc.scalar.activation(out=dst, in_=src, func=ACT.Copy, scale=factor)
 
         def interleave(copy, dst, src):
             copy(out=dst, in_=src.rearrange("p t n -> p n t"))
@@ -337,19 +336,20 @@ def tile_pooled_fisher_connectivity_s3_kernel(
             nc.scalar.copy(out=result[:], in_=out_bank[i][:])
             nc.sync.dma_start(out=out[P * i : P * i + P, :], in_=result[:])
 
-        low, high = range(2), range(2, PACK)
-        widen_group(0, 0, True)
-        widen_group(1, 0, False)
+        planes = range(PACK)
+        widen((0, 1), 0, planes[:3], True)
+        widen((0,), 0, planes[3:], True)
+        widen((1,), 0, planes[3:], True)
+        widen((2, 3), 0, planes, False)
+        turn_by_matmul(wide[1][:, :, 0, :], TURN_BANK)
         interleave_early(0, 1)
-        widen_group(2, 0, False, low)
-        widen_group(0, 1, True)
-        widen_group(1, 1, False)
-        widen_group(0, 2, False)
-        for g in range(2):
-            turn_by_matmul(wide[1][:, :, g, :], TURN_BANK + g)
+        widen((0,), 1, planes, True)
+        widen((1,), 1, planes, False)
+        widen((0,), 2, planes, False)
+        turn_by_matmul(wide[1][:, :, 1, :], TURN_BANK + 1)
         quantise_early(0, 1)
         interleave_early(0, 2)
-        widen_group(1, 2, True)
+        widen((1,), 2, planes, True)
         quantise_early(0, 2)
         empty_through(early_grouped[1][:, 1, :, :])
         interleave_early(0, 3, nc.scalar.copy)
@@ -357,15 +357,14 @@ def tile_pooled_fisher_connectivity_s3_kernel(
         quantise_early(1, 1)
         quantise_early(1, 3)
         empty_through(early_grouped[1][:, 2, :, :])
-        widen_group(2, 0, True, high)
         interleave_regions(0)
         quantise_early(0, 3)
         quantise_regions(0)
         quantise_early(1, 2)
         interleave_early(0, 0, nc.scalar.copy)
         quantise_early(0, 0)
-        widen_group(2, 1, True)
-        widen_group(2, 2, False)
+        widen((2, 3), 1, planes[:2], True)
+        widen((2, 3), 2, planes[:3], False)
         for s in range(3):
             correlate(s, [1])
         correlate(0, [2])
@@ -383,7 +382,7 @@ def tile_pooled_fisher_connectivity_s3_kernel(
         form_difference(0, slice(1, 2))
         handover = work.tile([P, CHUNK, PACK], BF16, align_bytes=64, name="grouped", bufs=1)
         interleave(nc.vector.tensor_copy, handover[:], new_raw[1][:])
-        widen(3, 0, 0, True)
+        widen((2, 3), 1, planes[2:3], True)
         quantise(early_codes[1][:, 0, :], early_scales[1][:, 0, :], handover[:].rearrange("p n t -> p (n t)"))
 
         for s in range(LAST - 2):
@@ -391,16 +390,14 @@ def tile_pooled_fisher_connectivity_s3_kernel(
             turn(s, 1, TURN_BANK + 1)
             if s == 0:
                 correlate(1, [0])
-                widen_group(3, 0, False, range(1, PACK))
-                widen_group(3, 1, False)
+                widen((2, 3), 1, planes[3:], False)
+                widen((2, 3), 2, planes[3:], False)
             take_logarithms(s + 1, 0)
             take_logarithms(s + 1, 1)
-            if s == 1:
-                widen_group(3, 2, False)
             for i, h in STEPS[s]:
                 weigh(i, h)
             preparing = s + 4 < TILES
-            on_scalar = int(s + 4 >= SCALAR_INTERLEAVES)
+            on_scalar = min(s, 1)
             if preparing:
                 interleave_seeds(s + 4, 0, gpsimd_copy)
             if s == 0:
@@ -416,8 +413,8 @@ def tile_pooled_fisher_connectivity_s3_kernel(
                 project(s - 2, OUT_BANK + s % 2)
             correlate(s + 3, (1, 2, 3, 0))
             if preparing and s > 0:
-                if on_scalar:
-                    interleave_seeds(s + 4, GROUPS, nc.scalar.copy)
+                for k in range(PASSES - on_scalar, PASSES):
+                    interleave_seeds(s + 4, k, nc.scalar.copy)
                 interleave_old(s + 4, GROUPS - on_scalar)
             if 2 <= s < LAST - 3:
                 store(s - 2)
@@ -431,7 +428,6 @@ def tile_pooled_fisher_connectivity_s3_kernel(
 
         take_logarithms(LAST - 1, 0)
         take_logarithms(LAST - 1, 1)
-        store(LAST - 5)
         turn(LAST - 2, 0, TURN_BANK)
         turn(LAST - 2, 1, TURN_BANK + 1)
         project(LAST - 4, OUT_BANK + 1)
@@ -440,26 +436,26 @@ def tile_pooled_fisher_connectivity_s3_kernel(
         take_logarithms(LAST, 1)
         turn(LAST - 1, 0, r_bank(LAST - 1))
         turn(LAST - 1, 1, r_bank(LAST - 1) + 1)
-        project(LAST - 3, OUT_BANK)
         weigh(LAST - 2, 0)
         weigh(LAST - 2, 1)
+        project(LAST - 3, TURN_BANK)
         form_difference(LAST, slice(0, 1))
         quantise_z(LAST - 2)
         form_difference(LAST, slice(1, 2))
-        store(LAST - 4)
-        store(LAST - 3)
+        for i in range(LAST - 5, LAST - 2):
+            store(i)
         weigh(LAST - 1, 0)
         weigh(LAST - 1, 1)
         turn(LAST, 0, r_bank(LAST))
         turn(LAST, 1, r_bank(LAST) + 1)
-        project(LAST - 2, TURN_BANK)
+        project(LAST - 2, OUT_BANK)
         for h in range(2):
             quantise_z(LAST - 1, slice(h, h + 1))
         weigh(LAST, 0)
         weigh(LAST, 1)
         project(LAST - 1, TURN_BANK + 1)
         store(LAST - 2)
-        quarters = [bank(number, [P, P]) for number in (r_bank(LAST - 1), r_bank(LAST - 1) + 1, OUT_BANK, OUT_BANK + 1)]
+        quarters = [bank(number, [P, P]) for number in (r_bank(LAST - 1), r_bank(LAST - 1) + 1, OUT_BANK + 1, TURN_BANK)]
         for h in range(2):
             quantise_z(LAST, slice(h, h + 1))
             for q in range(4):

@@ -259,17 +259,18 @@ def tile_pooled_fisher_connectivity_s3_kernel(
         def take_logarithms(s, n):
             if s not in ln_plus:
                 ln_plus[s] = work.tile([P, 2, PACK, P], F32, name="ln_plus")
-                ln_minus[s] = work.tile([P, 2, PACK, P], F32, name="ln_minus")
-                difference[s] = work.tile([P, 2, PACK, P], F32, name="difference")
+                ln_minus[s] = work.tile([P, 2, PACK, P], F32, name="ln_minus", bufs=2)
+                if s < LAST:
+                    difference[s] = work.tile([P, 2, PACK, P], F32, name="difference")
             by_t = r[STEPS[s][n]][:].rearrange("s (p t) -> s t p", t=PACK)
             nc.scalar.activation(out=ln_minus[s][:, n, :, :], in_=by_t, func=ACT.Ln, bias=1.0, scale=-1.0)
             nc.scalar.activation(out=ln_plus[s][:, n, :, :], in_=by_t, func=ACT.Ln, bias=1.0, scale=1.0)
 
-        def form_difference(s, pieces):
+        def form_difference(s, pieces, engine=nc.vector):
             dst = difference[s][:, pieces, :, :]
             minus = ln_minus[s][:, pieces, :, :]
             if not adds_in_psum(s, pieces.start):
-                nc.vector.tensor_tensor(out=dst, in0=ln_plus[s][:, pieces, :, :], in1=minus, op=ALU.subtract)
+                engine.tensor_tensor(out=dst, in0=ln_plus[s][:, pieces, :, :], in1=minus, op=ALU.subtract)
             elif s < LAST:
                 nc.vector.tensor_scalar(out=dst, in0=minus, scalar1=-1.0, scalar2=None, op0=ALU.mult)
             else:
@@ -432,25 +433,26 @@ def tile_pooled_fisher_connectivity_s3_kernel(
         turn(LAST - 2, 1, TURN_BANK + 1)
         project(LAST - 4, OUT_BANK + 1)
         form_difference(LAST - 1, slice(0, 2))
+        store(LAST - 5)
         take_logarithms(LAST, 0)
         take_logarithms(LAST, 1)
+        difference[LAST] = work.tile([P, 2, PACK, P], F32, name="ln_minus", bufs=2)
+        form_difference(LAST, slice(0, 1), nc.gpsimd)
+        form_difference(LAST, slice(1, 2))
         turn(LAST - 1, 0, r_bank(LAST - 1))
         turn(LAST - 1, 1, r_bank(LAST - 1) + 1)
         weigh(LAST - 2, 0)
         weigh(LAST - 2, 1)
         project(LAST - 3, TURN_BANK)
-        form_difference(LAST, slice(0, 1))
-        quantise_z(LAST - 2)
-        form_difference(LAST, slice(1, 2))
-        for i in range(LAST - 5, LAST - 2):
+        for i in range(LAST - 4, LAST - 2):
             store(i)
         weigh(LAST - 1, 0)
         weigh(LAST - 1, 1)
         turn(LAST, 0, r_bank(LAST))
         turn(LAST, 1, r_bank(LAST) + 1)
+        quantise_z(LAST - 2)
         project(LAST - 2, OUT_BANK)
-        for h in range(2):
-            quantise_z(LAST - 1, slice(h, h + 1))
+        quantise_z(LAST - 1)
         weigh(LAST, 0)
         weigh(LAST, 1)
         project(LAST - 1, TURN_BANK + 1)

@@ -30,16 +30,17 @@ LAST = TILES - 1
 NEW_RANGES = ((0, CHUNK), (CHUNK, HALF), (HALF, M))
 
 STEPS = [((0, 0), (1, 0)), ((0, 1), (1, 1))] + [((i, 0), (i, 1)) for i in range(2, TILES)]
+BOTH_ADDED = 2
 ADDING_ENDS = 2
-TURN_BANK, OUT_BANK = 4, 6
+PAIRS = 4
 
 
 def r_bank(s):
-    return OUT_BANK if s == 2 else 2 * ((s if s < 2 else s - 1) % 2)
+    return 2 * (s % PAIRS)
 
 
 def adds_in_psum(s, n):
-    return s == 0 or (n == 1 and (s <= ADDING_ENDS or s == LAST))
+    return s < BOTH_ADDED or (n == 1 and (s <= ADDING_ENDS or s == LAST))
 
 
 def tile_pooled_fisher_connectivity_s3_kernel(
@@ -70,7 +71,8 @@ def tile_pooled_fisher_connectivity_s3_kernel(
 
         regions_raw = kept("regions_raw", 2, [P, PACK, HALF], BF16)
         new_raw = [keep.tile([P, PACK, hi - lo], BF16, align_bytes=64, name=f"new_raw_{lo}") for lo, hi in NEW_RANGES]
-        old_bytes = [kept(f"old_bytes_{g}", 1 + (g == 0), [P, PACK // (1 + (g == 0)), M], U8) for g in range(GROUPS)]
+        first_bytes = kept("first_bytes", 2, [P, 2, M], U8)
+        old_bytes = [kept(f"old_bytes_{b}", GROUPS - 1, [P, PACK, HALF], U8) for b in range(2)]
         old_factor = keep.tile([P, GROUPS, PACK], F32)
         d_words = kept("d_words", GROUPS, [P, 2 * R], U8)
         d_scales = keep.tile([P, GROUPS, R], U8, align_bytes=64)
@@ -88,7 +90,7 @@ def tile_pooled_fisher_connectivity_s3_kernel(
 
         nc.vector.memset(one[:], 1.0)
         nc.vector.memset(d_scales[:].rearrange("p g n -> p (g n)").bitcast(I32), 0)
-        nc.gpsimd.memset(p_scales[:].rearrange("p g n -> p (g n)").bitcast(I32), 0)
+        nc.vector.memset(p_scales[:].rearrange("p g n -> p (g n)").bitcast(I32), 0)
         make_identity(nc, identity_bf16[:])
         make_identity(nc, identity[:])
 
@@ -100,11 +102,10 @@ def tile_pooled_fisher_connectivity_s3_kernel(
             lo, hi = NEW_RANGES[n]
             nc.sync.dma_start(out=new_raw[n][:], in_=seeds_new.rearrange("(p t) n -> p t n", t=PACK)[:, :, lo:hi])
 
-        def load_old(g):
-            rows = seeds_old_bytes.rearrange("(g p t) n -> g p t n", p=P, t=PACK)[g]
-            planes = PACK // len(old_bytes[g])
-            for u, tile in enumerate(old_bytes[g]):
-                nc.sync.dma_start(out=tile[:], in_=rows[:, planes * u : planes * u + planes, :])
+        old_rows = seeds_old_bytes.rearrange("(g p t) n -> g p t n", p=P, t=PACK)
+
+        def load_old(b, g):
+            nc.sync.dma_start(out=old_bytes[b][g - 1][:], in_=old_rows[g][:, :, HALF * b : HALF * b + HALF])
 
         def load_d(g):
             nc.sync.dma_start(out=d_words[g][:], in_=old_words[g])
@@ -120,16 +121,20 @@ def tile_pooled_fisher_connectivity_s3_kernel(
             out=old_factor[:], in_=seeds_old_scale.rearrange("(g p t) o -> p g (t o)", p=P, t=PACK)
         )
         nc.scalar.dma_start(out=weights[:], in_=precision.rearrange("(h p t) -> p h t", p=P, t=PACK))
-        for g in range(GROUPS):
-            load_old(g)
+        for u in range(2):
+            nc.sync.dma_start(out=first_bytes[u][:], in_=old_rows[0][:, 2 * u : 2 * u + 2, :])
+        load_old(0, 1)
         load_scale_rows(d_scales, old_scales, GROUPS)
         load_d(0)
+        load_old(0, 2)
+        load_d(1)
         load_regions(0)
         load_new(0)
-        load_d(1)
         load_d(2)
         load_regions(1)
         load_new(1)
+        for g in range(1, GROUPS):
+            load_old(1, g)
         load_new(2)
         nc.sync.dma_start(out=p_words[:], in_=net_words.rearrange("g p w -> p g w"))
         load_scale_rows(p_scales, net_scales, 2)
@@ -142,8 +147,10 @@ def tile_pooled_fisher_connectivity_s3_kernel(
         def widen(chunks, g, planes, on_vector):
             lo, hi = CHUNK * chunks[0], CHUNK * (chunks[-1] + 1)
             for t in planes:
-                u, row = divmod(t, PACK // len(old_bytes[g]))
-                src = old_bytes[g][u][:, row, lo:hi].bitcast(FP8)
+                if g == 0:
+                    src = first_bytes[t // 2][:, t % 2, lo:hi].bitcast(FP8)
+                else:
+                    src = old_bytes[lo // HALF][g - 1][:, t, lo % HALF : lo % HALF + hi - lo].bitcast(FP8)
                 dst = halves[lo // HALF][:, t, g, lo % HALF : lo % HALF + hi - lo]
                 factor = old_factor[:, g, t : t + 1]
                 if on_vector:
@@ -218,11 +225,11 @@ def tile_pooled_fisher_connectivity_s3_kernel(
                 in_=wide[c][:, :, :groups, P * j : P * j + P].rearrange("p t g (a n) -> p a g n t", a=2),
             )
 
-        def quantise_seeds(i):
+        def quantise_seeds(i, passes=slice(0, PASSES)):
             quantise(
-                codes[i][:].rearrange("p k n -> p (k n)"),
-                scales[i][:].rearrange("p k n -> p (k n)"),
-                grouped[i][:].rearrange("p k n t -> p (k n t)"),
+                codes[i][:, passes, :].rearrange("p k n -> p (k n)"),
+                scales[i][:, passes, :].rearrange("p k n -> p (k n)"),
+                grouped[i][:, passes, :, :].rearrange("p k n t -> p (k n t)"),
             )
 
         r, passes_done = {}, {}
@@ -259,7 +266,7 @@ def tile_pooled_fisher_connectivity_s3_kernel(
         def take_logarithms(s, n):
             if s not in ln_plus:
                 ln_plus[s] = work.tile([P, 2, PACK, P], F32, name="ln_plus")
-                ln_minus[s] = work.tile([P, 2, PACK, P], F32, name="ln_minus", bufs=2)
+                ln_minus[s] = work.tile([P, 2, PACK, P], F32, name="ln_minus", bufs=3)
                 if s < LAST:
                     difference[s] = work.tile([P, 2, PACK, P], F32, name="difference")
             by_t = r[STEPS[s][n]][:].rearrange("s (p t) -> s t p", t=PACK)
@@ -278,9 +285,9 @@ def tile_pooled_fisher_connectivity_s3_kernel(
 
         turned = {}
 
-        def turn(s, n, number):
+        def turn(s, n):
             piece = STEPS[s][n]
-            turned[piece] = bank(number, [P, P // 2, PACK, 2])
+            turned[piece] = bank(r_bank(s) + n, [P, P // 2, PACK, 2])
             parts = (difference[s], ln_plus[s]) if adds_in_psum(s, n) else (difference[s],)
             for t in range(PACK):
                 for m, part in enumerate(parts):
@@ -338,126 +345,137 @@ def tile_pooled_fisher_connectivity_s3_kernel(
             nc.sync.dma_start(out=out[P * i : P * i + P, :], in_=result[:])
 
         planes = range(PACK)
-        widen((0, 1), 0, planes[:3], True)
+        widen((0, 1), 0, planes[:1], True)
+        widen((0, 1), 0, planes[1:2], False)
+        widen((0, 1), 0, planes[2:3], True)
         widen((0,), 0, planes[3:], True)
-        widen((1,), 0, planes[3:], True)
-        widen((2, 3), 0, planes, False)
-        turn_by_matmul(wide[1][:, :, 0, :], TURN_BANK)
+        widen((1,), 0, planes[3:], False)
+        turn_by_matmul(wide[1][:, :, 0, :], r_bank(PAIRS - 1))
+        widen((2,), 0, planes[:2], False)
+        widen((2,), 0, planes[2:], True)
         interleave_early(0, 1)
-        widen((0,), 1, planes, True)
-        widen((1,), 1, planes, False)
-        widen((0,), 2, planes, False)
-        turn_by_matmul(wide[1][:, :, 1, :], TURN_BANK + 1)
+        widen((0,), 1, planes, False)
+        widen((1,), 1, planes, True)
         quantise_early(0, 1)
         interleave_early(0, 2)
-        widen((1,), 2, planes, True)
-        quantise_early(0, 2)
         empty_through(early_grouped[1][:, 1, :, :])
-        interleave_early(0, 3, nc.scalar.copy)
-        interleave_early(1, 3)
+        widen((0,), 2, planes, False)
+        interleave_early(1, 2)
+        quantise_early(0, 2)
         quantise_early(1, 1)
-        quantise_early(1, 3)
-        empty_through(early_grouped[1][:, 2, :, :])
+        widen((1,), 2, planes, True)
+        quantise_early(1, 2)
+        widen((3,), 0, planes[:1], False)
+        interleave_early(0, 3, nc.scalar.copy)
+        interleave_early(0, 0, nc.scalar.copy)
+        interleave_early(1, 3, nc.scalar.copy)
+        widen((3,), 0, planes[1:2], False)
         interleave_regions(0)
         quantise_early(0, 3)
         quantise_regions(0)
-        quantise_early(1, 2)
-        interleave_early(0, 0, nc.scalar.copy)
         quantise_early(0, 0)
-        widen((2, 3), 1, planes[:2], True)
-        widen((2, 3), 2, planes[:3], False)
-        for s in range(3):
-            correlate(s, [1])
+        correlate(0, [1])
+        correlate(1, [1])
         correlate(0, [2])
+        correlate(2, [1])
+        correlate(3, [1])
+        correlate(1, [2])
+        correlate(2, [2])
         correlate(0, [3])
-        correlate(1, [2], [0])
         correlate(0, [0])
-        correlate(1, [2], [1])
         correlate(1, [3])
-        correlate(2, [2, 3])
+        correlate(3, [2])
+        interleave_regions(1)
+        quantise_early(1, 3)
+        quantise_regions(1)
+        correlate(2, [3])
+        correlate(1, [0])
+        correlate(3, [3])
         take_logarithms(0, 0)
         take_logarithms(0, 1)
-        interleave_regions(1)
-        form_difference(0, slice(0, 1))
-        quantise_regions(1)
-        form_difference(0, slice(1, 2))
+        take_logarithms(1, 0)
+        take_logarithms(1, 1)
         handover = work.tile([P, CHUNK, PACK], BF16, align_bytes=64, name="grouped", bufs=1)
         interleave(nc.vector.tensor_copy, handover[:], new_raw[1][:])
-        widen((2, 3), 1, planes[2:3], True)
+        form_difference(0, slice(0, 1))
+        widen((2,), 1, planes, True)
+        form_difference(0, slice(1, 2))
+        widen((2,), 2, planes, True)
         quantise(early_codes[1][:, 0, :], early_scales[1][:, 0, :], handover[:].rearrange("p n t -> p (n t)"))
 
         for s in range(LAST - 2):
-            turn(s, 0, TURN_BANK)
-            turn(s, 1, TURN_BANK + 1)
+            turn(s, 0)
+            turn(s, 1)
             if s == 0:
-                correlate(1, [0])
-                widen((2, 3), 1, planes[3:], False)
-                widen((2, 3), 2, planes[3:], False)
-            take_logarithms(s + 1, 0)
-            take_logarithms(s + 1, 1)
+                form_difference(1, slice(0, 1))
+                correlate(2, [0])
+                correlate(3, [0])
+                widen((3,), 0, planes[2:], False)
+                widen((3,), 1, planes, False)
+            else:
+                correlate(s + 3, (1, 2, 3, 0))
+            take_logarithms(s + 2, 0)
+            if s >= 3:
+                store(s - 3)
+            take_logarithms(s + 2, 1)
             for i, h in STEPS[s]:
                 weigh(i, h)
             preparing = s + 4 < TILES
-            on_scalar = min(s, 1)
             if preparing:
                 interleave_seeds(s + 4, 0, gpsimd_copy)
             if s == 0:
-                correlate(2, [0])
-                interleave_old(4, GROUPS)
-                quantise_z(0, slice(0, 1))
-            if adds_in_psum(s + 1, 1):
+                form_difference(1, slice(1, 2))
+            elif adds_in_psum(s + 1, 0) == adds_in_psum(s + 1, 1):
+                form_difference(s + 1, slice(0, 2))
+            else:
                 form_difference(s + 1, slice(0, 1))
                 form_difference(s + 1, slice(1, 2))
-            else:
-                form_difference(s + 1, slice(0, 2))
+            if s == 1:
+                widen((3,), 2, planes, False)
             if s >= 2:
-                project(s - 2, OUT_BANK + s % 2)
-            correlate(s + 3, (1, 2, 3, 0))
-            if preparing and s > 0:
+                project(s - 2, r_bank(s) + 1)
+            on_scalar = 1 if s >= 2 else 0
+            if preparing:
                 for k in range(PASSES - on_scalar, PASSES):
                     interleave_seeds(s + 4, k, nc.scalar.copy)
                 interleave_old(s + 4, GROUPS - on_scalar)
-            if 2 <= s < LAST - 3:
-                store(s - 2)
             if s >= 2:
                 quantise_z(s)
             else:
-                for i, h in STEPS[s][1 - s :]:
+                for i, h in STEPS[s][1 - s :] if s else STEPS[s]:
                     quantise_z(i, slice(h, h + 1))
             if preparing:
                 quantise_seeds(s + 4)
 
-        take_logarithms(LAST - 1, 0)
-        take_logarithms(LAST - 1, 1)
-        turn(LAST - 2, 0, TURN_BANK)
-        turn(LAST - 2, 1, TURN_BANK + 1)
-        project(LAST - 4, OUT_BANK + 1)
+        turn(LAST - 2, 0)
+        turn(LAST - 2, 1)
+        project(LAST - 4, r_bank(LAST - 3))
         form_difference(LAST - 1, slice(0, 2))
-        store(LAST - 5)
         take_logarithms(LAST, 0)
+        store(LAST - 5)
         take_logarithms(LAST, 1)
-        difference[LAST] = work.tile([P, 2, PACK, P], F32, name="ln_minus", bufs=2)
+        difference[LAST] = work.tile([P, 2, PACK, P], F32, name="ln_minus", bufs=3)
         form_difference(LAST, slice(0, 1), nc.gpsimd)
         form_difference(LAST, slice(1, 2))
-        turn(LAST - 1, 0, r_bank(LAST - 1))
-        turn(LAST - 1, 1, r_bank(LAST - 1) + 1)
+        turn(LAST - 1, 0)
+        turn(LAST - 1, 1)
         weigh(LAST - 2, 0)
         weigh(LAST - 2, 1)
-        project(LAST - 3, TURN_BANK)
+        project(LAST - 3, r_bank(LAST - 3) + 1)
         for i in range(LAST - 4, LAST - 2):
             store(i)
         weigh(LAST - 1, 0)
         weigh(LAST - 1, 1)
-        turn(LAST, 0, r_bank(LAST))
-        turn(LAST, 1, r_bank(LAST) + 1)
+        turn(LAST, 0)
+        turn(LAST, 1)
         quantise_z(LAST - 2)
-        project(LAST - 2, OUT_BANK)
+        project(LAST - 2, r_bank(LAST - 2))
         quantise_z(LAST - 1)
         weigh(LAST, 0)
         weigh(LAST, 1)
-        project(LAST - 1, TURN_BANK + 1)
+        project(LAST - 1, r_bank(LAST - 2) + 1)
         store(LAST - 2)
-        quarters = [bank(number, [P, P]) for number in (r_bank(LAST - 1), r_bank(LAST - 1) + 1, OUT_BANK + 1, TURN_BANK)]
+        quarters = [bank(number, [P, P]) for number in (r_bank(LAST - 1), r_bank(LAST - 1) + 1, r_bank(LAST - 3), r_bank(LAST - 3) + 1)]
         for h in range(2):
             quantise_z(LAST, slice(h, h + 1))
             for q in range(4):

@@ -30,8 +30,9 @@ LAST = TILES - 1
 NEW_RANGES = ((0, CHUNK), (CHUNK, HALF), (HALF, M))
 
 STEPS = [((0, 0), (1, 0)), ((0, 1), (1, 1))] + [((i, 0), (i, 1)) for i in range(2, TILES)]
-BOTH_ADDED = 2
+BOTH_ADDED = 1
 ADDING_ENDS = 2
+SCALAR_NEGATES = 7
 PAIRS = 4
 
 
@@ -71,8 +72,7 @@ def tile_pooled_fisher_connectivity_s3_kernel(
 
         regions_raw = kept("regions_raw", 2, [P, PACK, HALF], BF16)
         new_raw = [keep.tile([P, PACK, hi - lo], BF16, align_bytes=64, name=f"new_raw_{lo}") for lo, hi in NEW_RANGES]
-        first_bytes = kept("first_bytes", 2, [P, 2, M], U8)
-        old_bytes = [kept(f"old_bytes_{b}", GROUPS - 1, [P, PACK, HALF], U8) for b in range(2)]
+        old_bytes = [kept(f"old_bytes_{g}", 1 + 3 * (g == 0), [P, PACK // (1 + 3 * (g == 0)), M], U8) for g in range(GROUPS)]
         old_factor = keep.tile([P, GROUPS, PACK], F32)
         d_words = kept("d_words", GROUPS, [P, 2 * R], U8)
         d_scales = keep.tile([P, GROUPS, R], U8, align_bytes=64)
@@ -102,10 +102,11 @@ def tile_pooled_fisher_connectivity_s3_kernel(
             lo, hi = NEW_RANGES[n]
             nc.sync.dma_start(out=new_raw[n][:], in_=seeds_new.rearrange("(p t) n -> p t n", t=PACK)[:, :, lo:hi])
 
-        old_rows = seeds_old_bytes.rearrange("(g p t) n -> g p t n", p=P, t=PACK)
-
-        def load_old(b, g):
-            nc.sync.dma_start(out=old_bytes[b][g - 1][:], in_=old_rows[g][:, :, HALF * b : HALF * b + HALF])
+        def load_old(g):
+            rows = seeds_old_bytes.rearrange("(g p t) n -> g p t n", p=P, t=PACK)[g]
+            planes = PACK // len(old_bytes[g])
+            for u, tile in enumerate(old_bytes[g]):
+                nc.sync.dma_start(out=tile[:], in_=rows[:, planes * u : planes * u + planes, :])
 
         def load_d(g):
             nc.sync.dma_start(out=d_words[g][:], in_=old_words[g])
@@ -120,21 +121,17 @@ def tile_pooled_fisher_connectivity_s3_kernel(
         nc.scalar.dma_start(
             out=old_factor[:], in_=seeds_old_scale.rearrange("(g p t) o -> p g (t o)", p=P, t=PACK)
         )
-        nc.scalar.dma_start(out=weights[:], in_=precision.rearrange("(h p t) -> p h t", p=P, t=PACK))
-        for u in range(2):
-            nc.sync.dma_start(out=first_bytes[u][:], in_=old_rows[0][:, 2 * u : 2 * u + 2, :])
-        load_old(0, 1)
+        for g in range(GROUPS):
+            load_old(g)
         load_scale_rows(d_scales, old_scales, GROUPS)
         load_d(0)
-        load_old(0, 2)
-        load_d(1)
         load_regions(0)
         load_new(0)
+        load_d(1)
         load_d(2)
         load_regions(1)
         load_new(1)
-        for g in range(1, GROUPS):
-            load_old(1, g)
+        nc.sync.dma_start(out=weights[:], in_=precision.rearrange("(h p t) -> p h t", p=P, t=PACK))
         load_new(2)
         nc.sync.dma_start(out=p_words[:], in_=net_words.rearrange("g p w -> p g w"))
         load_scale_rows(p_scales, net_scales, 2)
@@ -147,10 +144,8 @@ def tile_pooled_fisher_connectivity_s3_kernel(
         def widen(chunks, g, planes, on_vector):
             lo, hi = CHUNK * chunks[0], CHUNK * (chunks[-1] + 1)
             for t in planes:
-                if g == 0:
-                    src = first_bytes[t // 2][:, t % 2, lo:hi].bitcast(FP8)
-                else:
-                    src = old_bytes[lo // HALF][g - 1][:, t, lo % HALF : lo % HALF + hi - lo].bitcast(FP8)
+                u, row = divmod(t, PACK // len(old_bytes[g]))
+                src = old_bytes[g][u][:, row, lo:hi].bitcast(FP8)
                 dst = halves[lo // HALF][:, t, g, lo % HALF : lo % HALF + hi - lo]
                 factor = old_factor[:, g, t : t + 1]
                 if on_vector:
@@ -202,34 +197,36 @@ def tile_pooled_fisher_connectivity_s3_kernel(
                 early_codes[c][:, k, :], early_scales[c][:, k, :], early_grouped[c][:, k, :, :].rearrange("p n t -> p (n t)")
             )
 
+        PARTS = ((1, 2), (3,), (0,))
         grouped, codes, scales = {}, {}, {}
 
-        def interleave_seeds(i, k, copy=nc.vector.tensor_copy):
-            if i not in grouped:
-                grouped[i] = work.tile([P, PASSES, P, PACK], BF16, align_bytes=64, name="grouped", bufs=1)
-                codes[i] = work.tile([P, PASSES, P], U32, align_bytes=64, name="codes")
-                scales[i] = work.tile([P, PASSES, P], U8, align_bytes=64, name="scales")
-            if k == 0:
-                n = [lo <= P * i < hi for lo, hi in NEW_RANGES].index(True)
-                lo = P * i - NEW_RANGES[n][0]
-                src = new_raw[n][:, :, lo : lo + P]
-            else:
-                c, j = divmod(i, CHUNK // P)
-                src = wide[c][:, :, k - 1, P * j : P * j + P]
-            interleave(copy, grouped[i][:, k, :, :], src)
-
-        def interleave_old(i, groups):
-            c, j = divmod(i, CHUNK // P)
-            nc.vector.tensor_copy(
-                out=grouped[i][:, 1 : 1 + groups, :, :].rearrange("p g (a n) t -> p a g n t", a=2),
-                in_=wide[c][:, :, :groups, P * j : P * j + P].rearrange("p t g (a n) -> p a g n t", a=2),
+        def open_part(i, part):
+            count = len(PARTS[part])
+            grouped[i, part] = work.tile(
+                [P, count, P, PACK], BF16, align_bytes=64, name=f"grouped_{part}", bufs=1 if part == 2 else 2
             )
+            codes[i, part] = work.tile([P, count, P], U32, align_bytes=64, name=f"codes_{part}")
+            scales[i, part] = work.tile([P, count, P], U8, align_bytes=64, name=f"scales_{part}")
 
-        def quantise_seeds(i, passes=slice(0, PASSES)):
+        def interleave_part(i, part, copy=nc.vector.tensor_copy):
+            open_part(i, part)
+            c, j = divmod(i, CHUNK // P)
+            if part == 0:
+                copy(
+                    out=grouped[i, part][:],
+                    in_=wide[c][:, :, :2, P * j : P * j + P].rearrange("p t g n -> p g n t"),
+                )
+            elif part == 1:
+                interleave(copy, grouped[i, part][:, 0, :, :], wide[c][:, :, 2, P * j : P * j + P])
+            else:
+                lo = P * i - NEW_RANGES[2][0]
+                interleave(copy, grouped[i, part][:, 0, :, :], new_raw[2][:, :, lo : lo + P])
+
+        def quantise_part(i, part):
             quantise(
-                codes[i][:, passes, :].rearrange("p k n -> p (k n)"),
-                scales[i][:, passes, :].rearrange("p k n -> p (k n)"),
-                grouped[i][:, passes, :, :].rearrange("p k n t -> p (k n t)"),
+                codes[i, part][:].rearrange("p k n -> p (k n)"),
+                scales[i, part][:].rearrange("p k n -> p (k n)"),
+                grouped[i, part][:].rearrange("p k n t -> p (k n t)"),
             )
 
         r, passes_done = {}, {}
@@ -245,7 +242,9 @@ def tile_pooled_fisher_connectivity_s3_kernel(
                 if c < 2:
                     fixed, fixed_scale = early_codes[c][:, k, P * j : P * j + P], early_scales[c][:, k, P * j : P * j + P]
                 else:
-                    fixed, fixed_scale = codes[i][:, k, :], scales[i][:, k, :]
+                    part = [k in passes_of for passes_of in PARTS].index(True)
+                    slot = PARTS[part].index(k)
+                    fixed, fixed_scale = codes[i, part][:, slot, :], scales[i, part][:, slot, :]
                 if k == 0:
                     moving, moving_scale = regions_codes[h][:].bitcast(FP8X4), regions_scales[h][:]
                 else:
@@ -278,7 +277,7 @@ def tile_pooled_fisher_connectivity_s3_kernel(
             minus = ln_minus[s][:, pieces, :, :]
             if not adds_in_psum(s, pieces.start):
                 engine.tensor_tensor(out=dst, in0=ln_plus[s][:, pieces, :, :], in1=minus, op=ALU.subtract)
-            elif s < LAST:
+            elif s < SCALAR_NEGATES:
                 nc.vector.tensor_scalar(out=dst, in0=minus, scalar1=-1.0, scalar2=None, op0=ALU.mult)
             else:
                 nc.scalar.activation(out=dst, in_=minus, func=ACT.Copy, scale=-1.0)
@@ -345,114 +344,106 @@ def tile_pooled_fisher_connectivity_s3_kernel(
             nc.sync.dma_start(out=out[P * i : P * i + P, :], in_=result[:])
 
         planes = range(PACK)
-        widen((0, 1), 0, planes[:1], True)
-        widen((0, 1), 0, planes[1:2], False)
-        widen((0, 1), 0, planes[2:3], True)
+        widen((0, 1), 0, planes[:3], True)
         widen((0,), 0, planes[3:], True)
-        widen((1,), 0, planes[3:], False)
+        widen((1,), 0, planes[3:], True)
+        widen((2, 3), 0, planes, False)
         turn_by_matmul(wide[1][:, :, 0, :], r_bank(PAIRS - 1))
-        widen((2,), 0, planes[:2], False)
-        widen((2,), 0, planes[2:], True)
         interleave_early(0, 1)
-        widen((0,), 1, planes, False)
-        widen((1,), 1, planes, True)
+        widen((0,), 1, planes, True)
+        widen((1,), 1, planes, False)
+        widen((0,), 2, planes, False)
+        turn_by_matmul(wide[1][:, :, 1, :], r_bank(PAIRS - 1) + 1)
         quantise_early(0, 1)
         interleave_early(0, 2)
-        empty_through(early_grouped[1][:, 1, :, :])
-        widen((0,), 2, planes, False)
-        interleave_early(1, 2)
-        quantise_early(0, 2)
-        quantise_early(1, 1)
         widen((1,), 2, planes, True)
-        quantise_early(1, 2)
-        widen((3,), 0, planes[:1], False)
+        quantise_early(0, 2)
+        empty_through(early_grouped[1][:, 1, :, :])
         interleave_early(0, 3, nc.scalar.copy)
-        interleave_early(0, 0, nc.scalar.copy)
-        interleave_early(1, 3, nc.scalar.copy)
-        widen((3,), 0, planes[1:2], False)
+        interleave_early(1, 3)
+        quantise_early(1, 1)
+        quantise_early(1, 3)
+        empty_through(early_grouped[1][:, 2, :, :])
         interleave_regions(0)
         quantise_early(0, 3)
         quantise_regions(0)
+        quantise_early(1, 2)
+        interleave_early(0, 0, nc.scalar.copy)
         quantise_early(0, 0)
-        correlate(0, [1])
-        correlate(1, [1])
-        correlate(0, [2])
-        correlate(2, [1])
+        widen((2, 3), 1, planes[:2], True)
+        widen((2, 3), 2, planes[:3], False)
+        for s in range(3):
+            correlate(s, [1])
         correlate(3, [1])
-        correlate(1, [2])
-        correlate(2, [2])
+        correlate(0, [2])
         correlate(0, [3])
+        correlate(1, [2])
         correlate(0, [0])
         correlate(1, [3])
-        correlate(3, [2])
-        interleave_regions(1)
-        quantise_early(1, 3)
-        quantise_regions(1)
-        correlate(2, [3])
-        correlate(1, [0])
-        correlate(3, [3])
+        correlate(2, [2, 3])
+        correlate(3, [2], [0])
         take_logarithms(0, 0)
         take_logarithms(0, 1)
-        take_logarithms(1, 0)
-        take_logarithms(1, 1)
-        handover = work.tile([P, CHUNK, PACK], BF16, align_bytes=64, name="grouped", bufs=1)
-        interleave(nc.vector.tensor_copy, handover[:], new_raw[1][:])
+        interleave_regions(1)
         form_difference(0, slice(0, 1))
-        widen((2,), 1, planes, True)
+        quantise_regions(1)
+        correlate(1, [0])
+        handover = work.tile([P, CHUNK, PACK], BF16, align_bytes=64, name="grouped_2", bufs=1)
+        interleave(nc.vector.tensor_copy, handover[:], new_raw[1][:])
         form_difference(0, slice(1, 2))
-        widen((2,), 2, planes, True)
+        widen((2, 3), 1, planes[2:3], True)
         quantise(early_codes[1][:, 0, :], early_scales[1][:, 0, :], handover[:].rearrange("p n t -> p (n t)"))
+        widen((2, 3), 2, planes[3:], True)
 
+        widen((2, 3), 1, planes[3:], False)
+        take_logarithms(1, 0)
         for s in range(LAST - 2):
+            tile = s + PAIRS
+            preparing = tile < TILES
             turn(s, 0)
             turn(s, 1)
-            if s == 0:
-                form_difference(1, slice(0, 1))
-                correlate(2, [0])
-                correlate(3, [0])
-                widen((3,), 0, planes[2:], False)
-                widen((3,), 1, planes, False)
-            else:
-                correlate(s + 3, (1, 2, 3, 0))
-            take_logarithms(s + 2, 0)
-            if s >= 3:
-                store(s - 3)
-            take_logarithms(s + 2, 1)
+            take_logarithms(s + 1, 1)
+            if preparing:
+                interleave_part(tile, 1, nc.scalar.copy)
             for i, h in STEPS[s]:
                 weigh(i, h)
-            preparing = s + 4 < TILES
             if preparing:
-                interleave_seeds(s + 4, 0, gpsimd_copy)
+                interleave_part(tile, 2, gpsimd_copy)
             if s == 0:
-                form_difference(1, slice(1, 2))
-            elif adds_in_psum(s + 1, 0) == adds_in_psum(s + 1, 1):
-                form_difference(s + 1, slice(0, 2))
-            else:
+                correlate(3, [2], [1])
+                correlate(2, [0])
+                correlate(3, [3, 0])
+            if adds_in_psum(s + 1, 0) != adds_in_psum(s + 1, 1):
                 form_difference(s + 1, slice(0, 1))
                 form_difference(s + 1, slice(1, 2))
-            if s == 1:
-                widen((3,), 2, planes, False)
-            if s >= 2:
-                project(s - 2, r_bank(s) + 1)
-            on_scalar = 1 if s >= 2 else 0
+            else:
+                form_difference(s + 1, slice(0, 2))
+            projecting = 2 <= s < LAST - 3
+            if projecting:
+                project(s - 2, r_bank(s - 1) + 1)
+            if projecting:
+                store(s - 2)
+            take_logarithms(s + 2, 0)
+            if s > 0:
+                correlate(s + 3, (3, 0, 1, 2))
             if preparing:
-                for k in range(PASSES - on_scalar, PASSES):
-                    interleave_seeds(s + 4, k, nc.scalar.copy)
-                interleave_old(s + 4, GROUPS - on_scalar)
+                interleave_part(tile, 0)
             if s >= 2:
                 quantise_z(s)
-            else:
-                for i, h in STEPS[s][1 - s :] if s else STEPS[s]:
-                    quantise_z(i, slice(h, h + 1))
+            elif s == 1:
+                quantise_z(0)
+                quantise_z(1)
             if preparing:
-                quantise_seeds(s + 4)
+                for part in (1, 2, 0):
+                    quantise_part(tile, part)
 
+        project(LAST - 5, r_bank(LAST - 3))
+        take_logarithms(LAST - 1, 1)
         turn(LAST - 2, 0)
         turn(LAST - 2, 1)
-        project(LAST - 4, r_bank(LAST - 3))
+        project(LAST - 4, r_bank(LAST - 3) + 1)
         form_difference(LAST - 1, slice(0, 2))
         take_logarithms(LAST, 0)
-        store(LAST - 5)
         take_logarithms(LAST, 1)
         difference[LAST] = work.tile([P, 2, PACK, P], F32, name="ln_minus", bufs=3)
         form_difference(LAST, slice(0, 1), nc.gpsimd)
@@ -461,21 +452,21 @@ def tile_pooled_fisher_connectivity_s3_kernel(
         turn(LAST - 1, 1)
         weigh(LAST - 2, 0)
         weigh(LAST - 2, 1)
-        project(LAST - 3, r_bank(LAST - 3) + 1)
-        for i in range(LAST - 4, LAST - 2):
+        project(LAST - 3, r_bank(LAST - 2))
+        for i in range(LAST - 5, LAST - 2):
             store(i)
         weigh(LAST - 1, 0)
         weigh(LAST - 1, 1)
         turn(LAST, 0)
         turn(LAST, 1)
         quantise_z(LAST - 2)
-        project(LAST - 2, r_bank(LAST - 2))
+        project(LAST - 2, r_bank(LAST - 2) + 1)
         quantise_z(LAST - 1)
         weigh(LAST, 0)
         weigh(LAST, 1)
-        project(LAST - 1, r_bank(LAST - 2) + 1)
+        project(LAST - 1, r_bank(LAST - 1))
         store(LAST - 2)
-        quarters = [bank(number, [P, P]) for number in (r_bank(LAST - 1), r_bank(LAST - 1) + 1, r_bank(LAST - 3), r_bank(LAST - 3) + 1)]
+        quarters = [bank(number, [P, P]) for number in (r_bank(LAST - 3), r_bank(LAST - 3) + 1, r_bank(LAST - 1) + 1, r_bank(LAST - 2))]
         for h in range(2):
             quantise_z(LAST, slice(h, h + 1))
             for q in range(4):

@@ -30,9 +30,10 @@ LAST = TILES - 1
 NEW_RANGES = ((0, CHUNK), (CHUNK, HALF), (HALF, M))
 
 STEPS = [((0, 0), (1, 0)), ((0, 1), (1, 1))] + [((i, 0), (i, 1)) for i in range(2, TILES)]
-BOTH_ADDED = 1
+BOTH_ADDED = 3
 ADDING_ENDS = 2
-SCALAR_NEGATES = 7
+HANDED = 2
+LOG_REVERSED = 3
 PAIRS = 4
 
 
@@ -72,7 +73,7 @@ def tile_pooled_fisher_connectivity_s3_kernel(
 
         regions_raw = kept("regions_raw", 2, [P, PACK, HALF], BF16)
         new_raw = [keep.tile([P, PACK, hi - lo], BF16, align_bytes=64, name=f"new_raw_{lo}") for lo, hi in NEW_RANGES]
-        old_bytes = [kept(f"old_bytes_{g}", 1 + 3 * (g == 0), [P, PACK // (1 + 3 * (g == 0)), M], U8) for g in range(GROUPS)]
+        old_bytes = [kept(f"old_bytes_{g}", 1 + (g == 0), [P, PACK // (1 + (g == 0)), M], U8) for g in range(GROUPS)]
         old_factor = keep.tile([P, GROUPS, PACK], F32)
         d_words = kept("d_words", GROUPS, [P, 2 * R], U8)
         d_scales = keep.tile([P, GROUPS, R], U8, align_bytes=64)
@@ -121,6 +122,7 @@ def tile_pooled_fisher_connectivity_s3_kernel(
         nc.scalar.dma_start(
             out=old_factor[:], in_=seeds_old_scale.rearrange("(g p t) o -> p g (t o)", p=P, t=PACK)
         )
+        nc.scalar.dma_start(out=weights[:], in_=precision.rearrange("(h p t) -> p h t", p=P, t=PACK))
         for g in range(GROUPS):
             load_old(g)
         load_scale_rows(d_scales, old_scales, GROUPS)
@@ -131,7 +133,6 @@ def tile_pooled_fisher_connectivity_s3_kernel(
         load_d(2)
         load_regions(1)
         load_new(1)
-        nc.sync.dma_start(out=weights[:], in_=precision.rearrange("(h p t) -> p h t", p=P, t=PACK))
         load_new(2)
         nc.sync.dma_start(out=p_words[:], in_=net_words.rearrange("g p w -> p g w"))
         load_scale_rows(p_scales, net_scales, 2)
@@ -192,42 +193,50 @@ def tile_pooled_fisher_connectivity_s3_kernel(
         def interleave_early(c, k, copy=nc.vector.tensor_copy):
             interleave(copy, early_grouped[c][:, k, :, :], new_raw[c][:] if k == 0 else wide[c][:, :, k - 1, :])
 
-        def quantise_early(c, k):
+        def quantise_early(c, k, count=1):
+            passes = slice(k, k + count)
             quantise(
-                early_codes[c][:, k, :], early_scales[c][:, k, :], early_grouped[c][:, k, :, :].rearrange("p n t -> p (n t)")
+                early_codes[c][:, passes, :].rearrange("p k n -> p (k n)"),
+                early_scales[c][:, passes, :].rearrange("p k n -> p (k n)"),
+                early_grouped[c][:, passes, :, :].rearrange("p k n t -> p (k n t)"),
             )
 
-        PARTS = ((1, 2), (3,), (0,))
-        grouped, codes, scales = {}, {}, {}
+        old_grouped, old_codes, old_scale_rows = {}, {}, {}
+        new_grouped, new_codes, new_scale_rows = {}, {}, {}
 
-        def open_part(i, part):
-            count = len(PARTS[part])
-            grouped[i, part] = work.tile(
-                [P, count, P, PACK], BF16, align_bytes=64, name=f"grouped_{part}", bufs=1 if part == 2 else 2
-            )
-            codes[i, part] = work.tile([P, count, P], U32, align_bytes=64, name=f"codes_{part}")
-            scales[i, part] = work.tile([P, count, P], U8, align_bytes=64, name=f"scales_{part}")
+        def handed(turn_number, shape, dtype):
+            return work.tile(shape, dtype, align_bytes=64, name=f"handed_{turn_number % HANDED}", bufs=1)
 
-        def interleave_part(i, part, copy=nc.vector.tensor_copy):
-            open_part(i, part)
+        def open_old(i):
+            old_grouped[i] = work.tile([P, GROUPS, P, PACK], BF16, align_bytes=64, name="old_grouped", bufs=2)
+            old_codes[i] = work.tile([P, GROUPS, P], U32, align_bytes=64, name="old_codes")
+            old_scale_rows[i] = work.tile([P, GROUPS, P], U8, align_bytes=64, name="old_scale_rows")
+
+        def interleave_old(i, lo, hi, copy=nc.vector.tensor_copy):
+            if i not in old_grouped:
+                open_old(i)
             c, j = divmod(i, CHUNK // P)
-            if part == 0:
-                copy(
-                    out=grouped[i, part][:],
-                    in_=wide[c][:, :, :2, P * j : P * j + P].rearrange("p t g n -> p g n t"),
-                )
-            elif part == 1:
-                interleave(copy, grouped[i, part][:, 0, :, :], wide[c][:, :, 2, P * j : P * j + P])
-            else:
-                lo = P * i - NEW_RANGES[2][0]
-                interleave(copy, grouped[i, part][:, 0, :, :], new_raw[2][:, :, lo : lo + P])
-
-        def quantise_part(i, part):
-            quantise(
-                codes[i, part][:].rearrange("p k n -> p (k n)"),
-                scales[i, part][:].rearrange("p k n -> p (k n)"),
-                grouped[i, part][:].rearrange("p k n t -> p (k n t)"),
+            copy(
+                out=old_grouped[i][:, lo:hi, :, :].rearrange("p g (a n) t -> p a g n t", a=2),
+                in_=wide[c][:, :, lo:hi, P * j : P * j + P].rearrange("p t g (a n) -> p a g n t", a=2),
             )
+
+        def interleave_new(i):
+            new_grouped[i] = handed(i + 1 if i > 5 else 1, [P, P, PACK], BF16)
+            new_codes[i] = work.tile([P, P], U32, align_bytes=64, name="new_codes")
+            new_scale_rows[i] = work.tile([P, P], U8, align_bytes=64, name="new_scale_rows")
+            lo = P * i - NEW_RANGES[2][0]
+            interleave(gpsimd_copy, new_grouped[i][:], new_raw[2][:, :, lo : lo + P])
+
+        def quantise_old(i):
+            quantise(
+                old_codes[i][:].rearrange("p k n -> p (k n)"),
+                old_scale_rows[i][:].rearrange("p k n -> p (k n)"),
+                old_grouped[i][:].rearrange("p k n t -> p (k n t)"),
+            )
+
+        def quantise_new(i):
+            quantise(new_codes[i][:], new_scale_rows[i][:], new_grouped[i][:].rearrange("p n t -> p (n t)"))
 
         r, passes_done = {}, {}
 
@@ -241,10 +250,10 @@ def tile_pooled_fisher_connectivity_s3_kernel(
                 c, j = divmod(i, CHUNK // P)
                 if c < 2:
                     fixed, fixed_scale = early_codes[c][:, k, P * j : P * j + P], early_scales[c][:, k, P * j : P * j + P]
+                elif k == 0:
+                    fixed, fixed_scale = new_codes[i][:], new_scale_rows[i][:]
                 else:
-                    part = [k in passes_of for passes_of in PARTS].index(True)
-                    slot = PARTS[part].index(k)
-                    fixed, fixed_scale = codes[i, part][:, slot, :], scales[i, part][:, slot, :]
+                    fixed, fixed_scale = old_codes[i][:, k - 1, :], old_scale_rows[i][:, k - 1, :]
                 if k == 0:
                     moving, moving_scale = regions_codes[h][:].bitcast(FP8X4), regions_scales[h][:]
                 else:
@@ -264,7 +273,7 @@ def tile_pooled_fisher_connectivity_s3_kernel(
 
         def take_logarithms(s, n):
             if s not in ln_plus:
-                ln_plus[s] = work.tile([P, 2, PACK, P], F32, name="ln_plus")
+                ln_plus[s] = work.tile([P, 2, PACK, P], F32, name="ln_plus", bufs=4)
                 ln_minus[s] = work.tile([P, 2, PACK, P], F32, name="ln_minus", bufs=3)
                 if s < LAST:
                     difference[s] = work.tile([P, 2, PACK, P], F32, name="difference")
@@ -277,7 +286,7 @@ def tile_pooled_fisher_connectivity_s3_kernel(
             minus = ln_minus[s][:, pieces, :, :]
             if not adds_in_psum(s, pieces.start):
                 engine.tensor_tensor(out=dst, in0=ln_plus[s][:, pieces, :, :], in1=minus, op=ALU.subtract)
-            elif s < SCALAR_NEGATES:
+            elif s < LAST:
                 nc.vector.tensor_scalar(out=dst, in0=minus, scalar1=-1.0, scalar2=None, op0=ALU.mult)
             else:
                 nc.scalar.activation(out=dst, in_=minus, func=ACT.Copy, scale=-1.0)
@@ -299,13 +308,14 @@ def tile_pooled_fisher_connectivity_s3_kernel(
                         is_transpose=True,
                     )
 
-        z_grouped, z_codes, z_scales = {}, {}, {}
+        z_codes = keep.tile([P, TILES, 2, P], U32, align_bytes=64)
+        z_scales = keep.tile([P, TILES, 2, P], U8, align_bytes=64)
+        z_first = keep.tile([P, 2, 2, P, PACK], BF16, align_bytes=64)
+        z_grouped = {0: z_first[:, 0, :, :, :], 1: z_first[:, 1, :, :, :]}
 
         def weigh(i, h):
-            if h == 0:
-                z_grouped[i] = work.tile([P, 2, P, PACK], BF16, align_bytes=64, name="z_grouped", bufs=4)
-                z_codes[i] = work.tile([P, 2, P], U32, align_bytes=64, name="z_codes", bufs=5)
-                z_scales[i] = work.tile([P, 2, P], U8, align_bytes=64, name="z_scales", bufs=5)
+            if i not in z_grouped:
+                z_grouped[i] = handed(i, [P, 2, P, PACK], BF16)[:]
             nc.vector.tensor_tensor(
                 out=z_grouped[i][:, h, :, :].rearrange("p (n e) t -> p n t e", e=2),
                 in0=turned[i, h][:],
@@ -315,16 +325,23 @@ def tile_pooled_fisher_connectivity_s3_kernel(
 
         def quantise_z(i, halves=slice(0, 2)):
             quantise(
-                z_codes[i][:, halves, :].rearrange("p h n -> p (h n)"),
-                z_scales[i][:, halves, :].rearrange("p h n -> p (h n)"),
+                z_codes[:, i, halves, :].rearrange("p h n -> p (h n)"),
+                z_scales[:, i, halves, :].rearrange("p h n -> p (h n)"),
                 z_grouped[i][:, halves, :, :].rearrange("p h n t -> p (h n t)"),
+            )
+
+        def quantise_first_z():
+            quantise(
+                z_codes[:, :2, :, :].rearrange("p i h n -> p (i h n)"),
+                z_scales[:, :2, :, :].rearrange("p i h n -> p (i h n)"),
+                z_first[:].rearrange("p i h n t -> p (i h n t)"),
             )
 
         def project_pass(dst, i, h, lo, hi):
             nc.tensor.matmul_mx(
                 out=dst,
-                lhsT=z_codes[i][:, h, :].bitcast(FP8X4),
-                lhsT_scale=z_scales[i][:, h, :],
+                lhsT=z_codes[:, i, h, :].bitcast(FP8X4),
+                lhsT_scale=z_scales[:, i, h, :],
                 rhs=p_words[:, h, 2 * lo : 2 * hi].bitcast(FP4X4),
                 rhs_scale=p_scales[:, h, lo:hi],
                 start=(h == 0),
@@ -339,7 +356,7 @@ def tile_pooled_fisher_connectivity_s3_kernel(
                 project_pass(out_bank[i][:], i, h, 0, E)
 
         def store(i):
-            result = work.tile([P, E], F32, bufs=4)
+            result = work.tile([P, E], F32, bufs=7)
             nc.scalar.copy(out=result[:], in_=out_bank[i][:])
             nc.sync.dma_start(out=out[P * i : P * i + P, :], in_=result[:])
 
@@ -374,21 +391,22 @@ def tile_pooled_fisher_connectivity_s3_kernel(
         widen((2, 3), 2, planes[:3], False)
         for s in range(3):
             correlate(s, [1])
-        correlate(3, [1])
+        correlate(3, [1], [0])
         correlate(0, [2])
-        correlate(0, [3])
+        correlate(3, [1], [1])
         correlate(1, [2])
-        correlate(0, [0])
+        correlate(0, [3])
         correlate(1, [3])
+        correlate(0, [0])
         correlate(2, [2, 3])
-        correlate(3, [2], [0])
+        correlate(3, [2])
         take_logarithms(0, 0)
         take_logarithms(0, 1)
         interleave_regions(1)
         form_difference(0, slice(0, 1))
         quantise_regions(1)
         correlate(1, [0])
-        handover = work.tile([P, CHUNK, PACK], BF16, align_bytes=64, name="grouped_2", bufs=1)
+        handover = handed(1, [P, CHUNK, PACK], BF16)
         interleave(nc.vector.tensor_copy, handover[:], new_raw[1][:])
         form_difference(0, slice(1, 2))
         widen((2, 3), 1, planes[2:3], True)
@@ -402,18 +420,20 @@ def tile_pooled_fisher_connectivity_s3_kernel(
             preparing = tile < TILES
             turn(s, 0)
             turn(s, 1)
-            take_logarithms(s + 1, 1)
+            if s == 1:
+                correlate(3, [3])
+            take_logarithms(s + 1, 0 if LOG_REVERSED <= s + 1 else 1)
+            on_vector = GROUPS - 1
             if preparing:
-                interleave_part(tile, 1, nc.scalar.copy)
+                interleave_old(tile, on_vector, GROUPS, nc.scalar.copy)
             for i, h in STEPS[s]:
                 weigh(i, h)
             if preparing:
-                interleave_part(tile, 2, gpsimd_copy)
+                interleave_new(tile)
             if s == 0:
-                correlate(3, [2], [1])
                 correlate(2, [0])
-                correlate(3, [3, 0])
-            if adds_in_psum(s + 1, 0) != adds_in_psum(s + 1, 1):
+                correlate(3, [0])
+            if adds_in_psum(s + 1, 0) != adds_in_psum(s + 1, 1) or s == 0:
                 form_difference(s + 1, slice(0, 1))
                 form_difference(s + 1, slice(1, 2))
             else:
@@ -421,27 +441,25 @@ def tile_pooled_fisher_connectivity_s3_kernel(
             projecting = 2 <= s < LAST - 3
             if projecting:
                 project(s - 2, r_bank(s - 1) + 1)
-            if projecting:
                 store(s - 2)
-            take_logarithms(s + 2, 0)
+            take_logarithms(s + 2, 1 if LOG_REVERSED <= s + 2 else 0)
             if s > 0:
-                correlate(s + 3, (3, 0, 1, 2))
+                correlate(s + 3, (1, 2, 3, 0))
             if preparing:
-                interleave_part(tile, 0)
+                interleave_old(tile, 0, on_vector)
+            if s == 1:
+                quantise_first_z()
+            if preparing:
+                quantise_new(tile)
+                quantise_old(tile)
             if s >= 2:
                 quantise_z(s)
-            elif s == 1:
-                quantise_z(0)
-                quantise_z(1)
-            if preparing:
-                for part in (1, 2, 0):
-                    quantise_part(tile, part)
 
-        project(LAST - 5, r_bank(LAST - 3))
-        take_logarithms(LAST - 1, 1)
+        project(LAST - 5, r_bank(LAST - 3) + 1)
+        take_logarithms(LAST - 1, 0 if LOG_REVERSED < LAST else 1)
         turn(LAST - 2, 0)
         turn(LAST - 2, 1)
-        project(LAST - 4, r_bank(LAST - 3) + 1)
+        project(LAST - 4, r_bank(LAST - 3))
         form_difference(LAST - 1, slice(0, 2))
         take_logarithms(LAST, 0)
         take_logarithms(LAST, 1)
@@ -450,9 +468,9 @@ def tile_pooled_fisher_connectivity_s3_kernel(
         form_difference(LAST, slice(1, 2))
         turn(LAST - 1, 0)
         turn(LAST - 1, 1)
-        weigh(LAST - 2, 0)
         weigh(LAST - 2, 1)
-        project(LAST - 3, r_bank(LAST - 2))
+        weigh(LAST - 2, 0)
+        project(LAST - 3, r_bank(LAST - 2) + 1)
         for i in range(LAST - 5, LAST - 2):
             store(i)
         weigh(LAST - 1, 0)
@@ -460,13 +478,13 @@ def tile_pooled_fisher_connectivity_s3_kernel(
         turn(LAST, 0)
         turn(LAST, 1)
         quantise_z(LAST - 2)
-        project(LAST - 2, r_bank(LAST - 2) + 1)
+        project(LAST - 2, r_bank(LAST - 2))
         quantise_z(LAST - 1)
         weigh(LAST, 0)
         weigh(LAST, 1)
         project(LAST - 1, r_bank(LAST - 1))
         store(LAST - 2)
-        quarters = [bank(number, [P, P]) for number in (r_bank(LAST - 3), r_bank(LAST - 3) + 1, r_bank(LAST - 1) + 1, r_bank(LAST - 2))]
+        quarters = [bank(number, [P, P]) for number in (r_bank(LAST - 3) + 1, r_bank(LAST - 3), r_bank(LAST - 1) + 1, r_bank(LAST - 2) + 1)]
         for h in range(2):
             quantise_z(LAST, slice(h, h + 1))
             for q in range(4):

@@ -30,7 +30,7 @@ LAST = TILES - 1
 NEW_RANGES = ((0, CHUNK), (CHUNK, HALF), (HALF, M))
 
 STEPS = [((0, 0), (1, 0)), ((0, 1), (1, 1))] + [((i, 0), (i, 1)) for i in range(2, TILES)]
-BOTH_ADDED = 3
+BOTH_ADDED = 1
 ADDING_ENDS = 2
 HANDED = 2
 LOG_REVERSED = 3
@@ -311,7 +311,8 @@ def tile_pooled_fisher_connectivity_s3_kernel(
         z_codes = keep.tile([P, TILES, 2, P], U32, align_bytes=64)
         z_scales = keep.tile([P, TILES, 2, P], U8, align_bytes=64)
         z_first = keep.tile([P, 2, 2, P, PACK], BF16, align_bytes=64)
-        z_grouped = {0: z_first[:, 0, :, :, :], 1: z_first[:, 1, :, :, :]}
+        z_last = keep.tile([P, 2, P, PACK], BF16, align_bytes=64)
+        z_grouped = {0: z_first[:, 0, :, :, :], 1: z_first[:, 1, :, :, :], LAST: z_last[:]}
 
         def weigh(i, h):
             if i not in z_grouped:
@@ -405,23 +406,25 @@ def tile_pooled_fisher_connectivity_s3_kernel(
         interleave_regions(1)
         form_difference(0, slice(0, 1))
         quantise_regions(1)
+        turn(0, 0)
         correlate(1, [0])
         handover = handed(1, [P, CHUNK, PACK], BF16)
         interleave(nc.vector.tensor_copy, handover[:], new_raw[1][:])
         form_difference(0, slice(1, 2))
         widen((2, 3), 1, planes[2:3], True)
         quantise(early_codes[1][:, 0, :], early_scales[1][:, 0, :], handover[:].rearrange("p n t -> p (n t)"))
-        widen((2, 3), 2, planes[3:], True)
 
         widen((2, 3), 1, planes[3:], False)
+        widen((2, 3), 2, planes[3:], False)
         take_logarithms(1, 0)
         for s in range(LAST - 2):
             tile = s + PAIRS
             preparing = tile < TILES
-            turn(s, 0)
-            turn(s, 1)
+            if s > 0:
+                turn(s, 0)
             if s == 1:
                 correlate(3, [3])
+            turn(s, 1)
             take_logarithms(s + 1, 0 if LOG_REVERSED <= s + 1 else 1)
             on_vector = GROUPS - 1
             if preparing:

@@ -201,42 +201,42 @@ def tile_pooled_fisher_connectivity_s3_kernel(
                 early_grouped[c][:, passes, :, :].rearrange("p k n t -> p (k n t)"),
             )
 
-        old_grouped, old_codes, old_scale_rows = {}, {}, {}
-        new_grouped, new_codes, new_scale_rows = {}, {}, {}
+        grouped, codes, scales = {}, {}, {}
 
         def handed(turn_number, shape, dtype):
             return work.tile(shape, dtype, align_bytes=64, name=f"handed_{turn_number % HANDED}", bufs=1)
 
-        def open_old(i):
-            old_grouped[i] = work.tile([P, GROUPS, P, PACK], BF16, align_bytes=64, name="old_grouped", bufs=2)
-            old_codes[i] = work.tile([P, GROUPS, P], U32, align_bytes=64, name="old_codes")
-            old_scale_rows[i] = work.tile([P, GROUPS, P], U8, align_bytes=64, name="old_scale_rows")
+        def open_part(i, part):
+            shape = [P, 2, P, PACK]
+            if part == 0:
+                grouped[i, part] = work.tile(shape, BF16, align_bytes=64, name="grouped", bufs=2)
+            else:
+                grouped[i, part] = handed(i + 1 if i > 5 else 1, shape, BF16)
+            codes[i, part] = work.tile([P, 2, P], U32, align_bytes=64, name=f"codes_{part}")
+            scales[i, part] = work.tile([P, 2, P], U8, align_bytes=64, name=f"scales_{part}")
 
-        def interleave_old(i, lo, hi, copy=nc.vector.tensor_copy):
-            if i not in old_grouped:
-                open_old(i)
+        def interleave_on_vector(i):
+            open_part(i, 0)
             c, j = divmod(i, CHUNK // P)
-            copy(
-                out=old_grouped[i][:, lo:hi, :, :].rearrange("p g (a n) t -> p a g n t", a=2),
-                in_=wide[c][:, :, lo:hi, P * j : P * j + P].rearrange("p t g (a n) -> p a g n t", a=2),
+            nc.vector.tensor_copy(
+                out=grouped[i, 0][:], in_=wide[c][:, :, :2, P * j : P * j + P].rearrange("p t g n -> p g n t")
             )
 
-        def interleave_new(i):
-            new_grouped[i] = handed(i + 1 if i > 5 else 1, [P, P, PACK], BF16)
-            new_codes[i] = work.tile([P, P], U32, align_bytes=64, name="new_codes")
-            new_scale_rows[i] = work.tile([P, P], U8, align_bytes=64, name="new_scale_rows")
+        def interleave_on_scalar(i):
+            open_part(i, 1)
+            c, j = divmod(i, CHUNK // P)
+            interleave(nc.scalar.copy, grouped[i, 1][:, 0, :, :], wide[c][:, :, GROUPS - 1, P * j : P * j + P])
+
+        def interleave_on_gpsimd(i):
             lo = P * i - NEW_RANGES[2][0]
-            interleave(gpsimd_copy, new_grouped[i][:], new_raw[2][:, :, lo : lo + P])
+            interleave(gpsimd_copy, grouped[i, 1][:, 1, :, :], new_raw[2][:, :, lo : lo + P])
 
-        def quantise_old(i):
+        def quantise_part(i, part):
             quantise(
-                old_codes[i][:].rearrange("p k n -> p (k n)"),
-                old_scale_rows[i][:].rearrange("p k n -> p (k n)"),
-                old_grouped[i][:].rearrange("p k n t -> p (k n t)"),
+                codes[i, part][:].rearrange("p k n -> p (k n)"),
+                scales[i, part][:].rearrange("p k n -> p (k n)"),
+                grouped[i, part][:].rearrange("p k n t -> p (k n t)"),
             )
-
-        def quantise_new(i):
-            quantise(new_codes[i][:], new_scale_rows[i][:], new_grouped[i][:].rearrange("p n t -> p (n t)"))
 
         r, passes_done = {}, {}
 
@@ -250,10 +250,9 @@ def tile_pooled_fisher_connectivity_s3_kernel(
                 c, j = divmod(i, CHUNK // P)
                 if c < 2:
                     fixed, fixed_scale = early_codes[c][:, k, P * j : P * j + P], early_scales[c][:, k, P * j : P * j + P]
-                elif k == 0:
-                    fixed, fixed_scale = new_codes[i][:], new_scale_rows[i][:]
                 else:
-                    fixed, fixed_scale = old_codes[i][:, k - 1, :], old_scale_rows[i][:, k - 1, :]
+                    part, slot = divmod((k - 1) % PASSES, 2)
+                    fixed, fixed_scale = codes[i, part][:, slot, :], scales[i, part][:, slot, :]
                 if k == 0:
                     moving, moving_scale = regions_codes[h][:].bitcast(FP8X4), regions_scales[h][:]
                 else:
@@ -274,7 +273,7 @@ def tile_pooled_fisher_connectivity_s3_kernel(
         def take_logarithms(s, n):
             if s not in ln_plus:
                 ln_plus[s] = work.tile([P, 2, PACK, P], F32, name="ln_plus", bufs=4)
-                ln_minus[s] = work.tile([P, 2, PACK, P], F32, name="ln_minus", bufs=3)
+                ln_minus[s] = work.tile([P, 2, PACK, P], F32, name="ln_minus", bufs=2)
                 if s < LAST:
                     difference[s] = work.tile([P, 2, PACK, P], F32, name="difference")
             by_t = r[STEPS[s][n]][:].rearrange("s (p t) -> s t p", t=PACK)
@@ -426,13 +425,12 @@ def tile_pooled_fisher_connectivity_s3_kernel(
                 correlate(3, [3])
             turn(s, 1)
             take_logarithms(s + 1, 0 if LOG_REVERSED <= s + 1 else 1)
-            on_vector = GROUPS - 1
             if preparing:
-                interleave_old(tile, on_vector, GROUPS, nc.scalar.copy)
+                interleave_on_scalar(tile)
             for i, h in STEPS[s]:
                 weigh(i, h)
             if preparing:
-                interleave_new(tile)
+                interleave_on_gpsimd(tile)
             if s == 0:
                 correlate(2, [0])
                 correlate(3, [0])
@@ -449,12 +447,12 @@ def tile_pooled_fisher_connectivity_s3_kernel(
             if s > 0:
                 correlate(s + 3, (1, 2, 3, 0))
             if preparing:
-                interleave_old(tile, 0, on_vector)
+                interleave_on_vector(tile)
             if s == 1:
                 quantise_first_z()
             if preparing:
-                quantise_new(tile)
-                quantise_old(tile)
+                quantise_part(tile, 1)
+                quantise_part(tile, 0)
             if s >= 2:
                 quantise_z(s)
 
@@ -466,7 +464,7 @@ def tile_pooled_fisher_connectivity_s3_kernel(
         form_difference(LAST - 1, slice(0, 2))
         take_logarithms(LAST, 0)
         take_logarithms(LAST, 1)
-        difference[LAST] = work.tile([P, 2, PACK, P], F32, name="ln_minus", bufs=3)
+        difference[LAST] = work.tile([P, 2, PACK, P], F32, name="ln_minus", bufs=2)
         form_difference(LAST, slice(0, 1), nc.gpsimd)
         form_difference(LAST, slice(1, 2))
         turn(LAST - 1, 0)

@@ -22,6 +22,7 @@ PACK = 4
 GROUPS = T2 // (P * PACK)
 PASSES = 1 + GROUPS
 HALF = 512
+RUN = 4
 CHUNK = 256
 TILES = M // P
 CHUNKS = M // CHUNK
@@ -31,9 +32,10 @@ NEW_RANGES = ((0, CHUNK), (CHUNK, HALF), (HALF, M))
 
 STEPS = [((0, 0), (1, 0)), ((0, 1), (1, 1))] + [((i, 0), (i, 1)) for i in range(2, TILES)]
 BOTH_ADDED = 1
-ADDING_ENDS = 2
+ADDED_STEP = 2
 HANDED = 2
 LOG_REVERSED = 3
+LENT = 3
 PAIRS = 4
 
 
@@ -42,7 +44,7 @@ def r_bank(s):
 
 
 def adds_in_psum(s, n):
-    return s < BOTH_ADDED or (n == 1 and (s <= ADDING_ENDS or s == LAST))
+    return s < BOTH_ADDED or (n == 1 and s in (ADDED_STEP, LAST))
 
 
 def tile_pooled_fisher_connectivity_s3_kernel(
@@ -73,7 +75,7 @@ def tile_pooled_fisher_connectivity_s3_kernel(
 
         regions_raw = kept("regions_raw", 2, [P, PACK, HALF], BF16)
         new_raw = [keep.tile([P, PACK, hi - lo], BF16, align_bytes=64, name=f"new_raw_{lo}") for lo, hi in NEW_RANGES]
-        old_bytes = [kept(f"old_bytes_{g}", 1 + (g == 0), [P, PACK // (1 + (g == 0)), M], U8) for g in range(GROUPS)]
+        old_bytes = [kept(f"old_bytes_{g}", 1 + 3 * (g == 0), [P, PACK // (1 + 3 * (g == 0)), M], U8) for g in range(GROUPS)]
         old_factor = keep.tile([P, GROUPS, PACK], F32)
         d_words = kept("d_words", GROUPS, [P, 2 * R], U8)
         d_scales = keep.tile([P, GROUPS, R], U8, align_bytes=64)
@@ -122,7 +124,6 @@ def tile_pooled_fisher_connectivity_s3_kernel(
         nc.scalar.dma_start(
             out=old_factor[:], in_=seeds_old_scale.rearrange("(g p t) o -> p g (t o)", p=P, t=PACK)
         )
-        nc.scalar.dma_start(out=weights[:], in_=precision.rearrange("(h p t) -> p h t", p=P, t=PACK))
         for g in range(GROUPS):
             load_old(g)
         load_scale_rows(d_scales, old_scales, GROUPS)
@@ -133,6 +134,7 @@ def tile_pooled_fisher_connectivity_s3_kernel(
         load_d(2)
         load_regions(1)
         load_new(1)
+        nc.sync.dma_start(out=weights[:], in_=precision.rearrange("(h p t) -> p h t", p=P, t=PACK))
         load_new(2)
         nc.sync.dma_start(out=p_words[:], in_=net_words.rearrange("g p w -> p g w"))
         load_scale_rows(p_scales, net_scales, 2)
@@ -155,7 +157,10 @@ def tile_pooled_fisher_connectivity_s3_kernel(
                     nc.scalar.activation(out=dst, in_=src, func=ACT.Copy, scale=factor)
 
         def interleave(copy, dst, src):
-            copy(out=dst, in_=src.rearrange("p t n -> p n t"))
+            copy(
+                out=dst.rearrange("p (c i) t -> p c t i", i=RUN),
+                in_=src.rearrange("p t (c i) -> p c t i", i=RUN),
+            )
 
         through = []
 
@@ -211,7 +216,7 @@ def tile_pooled_fisher_connectivity_s3_kernel(
             if part == 0:
                 grouped[i, part] = work.tile(shape, BF16, align_bytes=64, name="grouped", bufs=2)
             else:
-                grouped[i, part] = handed(i + 1 if i > 5 else 1, shape, BF16)
+                grouped[i, part] = handed(max(i - PAIRS, 1), shape, BF16)
             codes[i, part] = work.tile([P, 2, P], U32, align_bytes=64, name=f"codes_{part}")
             scales[i, part] = work.tile([P, 2, P], U8, align_bytes=64, name=f"scales_{part}")
 
@@ -219,7 +224,8 @@ def tile_pooled_fisher_connectivity_s3_kernel(
             open_part(i, 0)
             c, j = divmod(i, CHUNK // P)
             nc.vector.tensor_copy(
-                out=grouped[i, 0][:], in_=wide[c][:, :, :2, P * j : P * j + P].rearrange("p t g n -> p g n t")
+                out=grouped[i, 0][:].rearrange("p g (c i) t -> p g c t i", i=RUN),
+                in_=wide[c][:, :, :2, P * j : P * j + P].rearrange("p t g (c i) -> p g c t i", i=RUN),
             )
 
         def interleave_on_scalar(i):
@@ -229,7 +235,7 @@ def tile_pooled_fisher_connectivity_s3_kernel(
 
         def interleave_on_gpsimd(i):
             lo = P * i - NEW_RANGES[2][0]
-            interleave(gpsimd_copy, grouped[i, 1][:, 1, :, :], new_raw[2][:, :, lo : lo + P])
+            gpsimd_copy(out=grouped[i, 1][:, 1, :, :], in_=new_raw[2][:, :, lo : lo + P].rearrange("p t n -> p n t"))
 
         def quantise_part(i, part):
             quantise(
@@ -290,7 +296,11 @@ def tile_pooled_fisher_connectivity_s3_kernel(
             else:
                 nc.scalar.activation(out=dst, in_=minus, func=ACT.Copy, scale=-1.0)
 
-        turned = {}
+        def subtract_planes(engine, s, dst, lo, hi):
+            flat = [part[:].rearrange("s n t p -> s (n t) p")[:, lo:hi, :] for part in (ln_plus[s], ln_minus[s])]
+            engine.tensor_tensor(out=dst, in0=flat[0], in1=flat[1], op=ALU.subtract)
+
+        turned, lent = {}, {}
 
         def turn(s, n):
             piece = STEPS[s][n]
@@ -300,7 +310,7 @@ def tile_pooled_fisher_connectivity_s3_kernel(
                 for m, part in enumerate(parts):
                     nc.tensor.matmul(
                         turned[piece][:, :, t, :],
-                        lhsT=part[:, n, t, :],
+                        lhsT=lent[s][:, t, :] if s in lent and PACK * n + t < LENT else part[:, n, t, :],
                         rhs=identity[:],
                         start=(m == 0),
                         stop=(m == len(parts) - 1),
@@ -309,13 +319,13 @@ def tile_pooled_fisher_connectivity_s3_kernel(
 
         z_codes = keep.tile([P, TILES, 2, P], U32, align_bytes=64)
         z_scales = keep.tile([P, TILES, 2, P], U8, align_bytes=64)
-        z_first = keep.tile([P, 2, 2, P, PACK], BF16, align_bytes=64)
+        z_first = handed(0, [P, 2, 2, P, PACK], BF16)
         z_last = keep.tile([P, 2, P, PACK], BF16, align_bytes=64)
         z_grouped = {0: z_first[:, 0, :, :, :], 1: z_first[:, 1, :, :, :], LAST: z_last[:]}
 
         def weigh(i, h):
             if i not in z_grouped:
-                z_grouped[i] = handed(i, [P, 2, P, PACK], BF16)[:]
+                z_grouped[i] = handed(i + 1, [P, 2, P, PACK], BF16)[:]
             nc.vector.tensor_tensor(
                 out=z_grouped[i][:, h, :, :].rearrange("p (n e) t -> p n t e", e=2),
                 in0=turned[i, h][:],
@@ -394,12 +404,11 @@ def tile_pooled_fisher_connectivity_s3_kernel(
         correlate(3, [1], [0])
         correlate(0, [2])
         correlate(3, [1], [1])
-        correlate(1, [2])
         correlate(0, [3])
-        correlate(1, [3])
+        correlate(1, [2])
         correlate(0, [0])
+        correlate(1, [3])
         correlate(2, [2, 3])
-        correlate(3, [2])
         take_logarithms(0, 0)
         take_logarithms(0, 1)
         interleave_regions(1)
@@ -412,9 +421,9 @@ def tile_pooled_fisher_connectivity_s3_kernel(
         form_difference(0, slice(1, 2))
         widen((2, 3), 1, planes[2:3], True)
         quantise(early_codes[1][:, 0, :], early_scales[1][:, 0, :], handover[:].rearrange("p n t -> p (n t)"))
+        widen((2, 3), 2, planes[3:], True)
 
         widen((2, 3), 1, planes[3:], False)
-        widen((2, 3), 2, planes[3:], False)
         take_logarithms(1, 0)
         for s in range(LAST - 2):
             tile = s + PAIRS
@@ -425,6 +434,8 @@ def tile_pooled_fisher_connectivity_s3_kernel(
                 correlate(3, [3])
             turn(s, 1)
             take_logarithms(s + 1, 0 if LOG_REVERSED <= s + 1 else 1)
+            if s >= 3:
+                store(s - 3)
             if preparing:
                 interleave_on_scalar(tile)
             for i, h in STEPS[s]:
@@ -433,33 +444,42 @@ def tile_pooled_fisher_connectivity_s3_kernel(
                 interleave_on_gpsimd(tile)
             if s == 0:
                 correlate(2, [0])
-                correlate(3, [0])
-            if adds_in_psum(s + 1, 0) != adds_in_psum(s + 1, 1) or s == 0:
+                correlate(3, [2, 0])
+            if not preparing:
+                lent[s + 1] = handed(s, [P, LENT, P], F32)
+                subtract_planes(nc.gpsimd, s + 1, lent[s + 1][:], 0, LENT)
+                rest = difference[s + 1][:].rearrange("s n t p -> s (n t) p")[:, LENT:, :]
+                subtract_planes(nc.vector, s + 1, rest, LENT, 2 * PACK)
+            elif s == 0:
+                form_difference(1, slice(0, 1))
+                interleave_on_vector(tile)
+                form_difference(1, slice(1, 2))
+                quantise_part(tile, 0)
+                quantise_part(tile, 1)
+            elif adds_in_psum(s + 1, 0) != adds_in_psum(s + 1, 1):
                 form_difference(s + 1, slice(0, 1))
                 form_difference(s + 1, slice(1, 2))
             else:
                 form_difference(s + 1, slice(0, 2))
-            projecting = 2 <= s < LAST - 3
-            if projecting:
-                project(s - 2, r_bank(s - 1) + 1)
-                store(s - 2)
             take_logarithms(s + 2, 1 if LOG_REVERSED <= s + 2 else 0)
             if s > 0:
                 correlate(s + 3, (1, 2, 3, 0))
-            if preparing:
+            if 2 <= s < LAST - 3:
+                project(s - 2, r_bank(s) + 1)
+            if preparing and s > 0:
                 interleave_on_vector(tile)
-            if s == 1:
-                quantise_first_z()
-            if preparing:
+            if preparing and s > 0:
                 quantise_part(tile, 1)
                 quantise_part(tile, 0)
+            if s == 1:
+                quantise_first_z()
             if s >= 2:
                 quantise_z(s)
 
-        project(LAST - 5, r_bank(LAST - 3) + 1)
         take_logarithms(LAST - 1, 0 if LOG_REVERSED < LAST else 1)
         turn(LAST - 2, 0)
         turn(LAST - 2, 1)
+        project(LAST - 5, r_bank(LAST - 3) + 1)
         project(LAST - 4, r_bank(LAST - 3))
         form_difference(LAST - 1, slice(0, 2))
         take_logarithms(LAST, 0)

@@ -31,11 +31,11 @@ LAST = TILES - 1
 NEW_RANGES = ((0, CHUNK), (CHUNK, HALF), (HALF, M))
 
 STEPS = [((0, 0), (1, 0)), ((0, 1), (1, 1))] + [((i, 0), (i, 1)) for i in range(2, TILES)]
-BOTH_ADDED = 1
 ADDED_STEP = 2
-HANDED = 2
 LOG_REVERSED = 3
 LENT = 3
+ON_GPSIMD = 40
+ON_SCALAR = 36
 PAIRS = 4
 
 
@@ -44,7 +44,7 @@ def r_bank(s):
 
 
 def adds_in_psum(s, n):
-    return s < BOTH_ADDED or (n == 1 and s in (ADDED_STEP, LAST))
+    return s == 0 or (n == 1 and s in (ADDED_STEP, LAST))
 
 
 def tile_pooled_fisher_connectivity_s3_kernel(
@@ -74,8 +74,10 @@ def tile_pooled_fisher_connectivity_s3_kernel(
             return psum.tile(shape, F32, name=f"bank_{number}")
 
         regions_raw = kept("regions_raw", 2, [P, PACK, HALF], BF16)
-        new_raw = [keep.tile([P, PACK, hi - lo], BF16, align_bytes=64, name=f"new_raw_{lo}") for lo, hi in NEW_RANGES]
+        new_raw = [keep.tile([P, PACK, hi - lo], BF16, align_bytes=64, name=f"new_raw_{lo}") for lo, hi in NEW_RANGES[:2]]
         old_bytes = [kept(f"old_bytes_{g}", 1 + 3 * (g == 0), [P, PACK // (1 + 3 * (g == 0)), M], U8) for g in range(GROUPS)]
+        halves = [keep.tile([P, PACK, GROUPS + b, HALF], BF16, align_bytes=64, name=f"wide_{b}") for b in range(2)]
+        new_raw.append(halves[1][:, :, GROUPS, :])
         old_factor = keep.tile([P, GROUPS, PACK], F32)
         d_words = kept("d_words", GROUPS, [P, 2 * R], U8)
         d_scales = keep.tile([P, GROUPS, R], U8, align_bytes=64)
@@ -95,7 +97,7 @@ def tile_pooled_fisher_connectivity_s3_kernel(
         nc.vector.memset(d_scales[:].rearrange("p g n -> p (g n)").bitcast(I32), 0)
         nc.vector.memset(p_scales[:].rearrange("p g n -> p (g n)").bitcast(I32), 0)
         make_identity(nc, identity_bf16[:])
-        make_identity(nc, identity[:])
+        nc.vector.tensor_copy(out=identity[:], in_=identity_bf16[:])
 
         def load_regions(h):
             rows = regions_new.rearrange("(p t) n -> p t n", t=PACK)
@@ -103,7 +105,7 @@ def tile_pooled_fisher_connectivity_s3_kernel(
 
         def load_new(n):
             lo, hi = NEW_RANGES[n]
-            nc.sync.dma_start(out=new_raw[n][:], in_=seeds_new.rearrange("(p t) n -> p t n", t=PACK)[:, :, lo:hi])
+            nc.sync.dma_start(out=new_raw[n][:, :, :], in_=seeds_new.rearrange("(p t) n -> p t n", t=PACK)[:, :, lo:hi])
 
         def load_old(g):
             rows = seeds_old_bytes.rearrange("(g p t) n -> g p t n", p=P, t=PACK)[g]
@@ -129,8 +131,8 @@ def tile_pooled_fisher_connectivity_s3_kernel(
         load_scale_rows(d_scales, old_scales, GROUPS)
         load_d(0)
         load_regions(0)
-        load_new(0)
         load_d(1)
+        load_new(0)
         load_d(2)
         load_regions(1)
         load_new(1)
@@ -141,7 +143,6 @@ def tile_pooled_fisher_connectivity_s3_kernel(
 
         nc.scalar.activation(out=one[:], in_=one[:], func=ACT.Ln)
 
-        halves = kept("wide", 2, [P, PACK, GROUPS, HALF], BF16)
         wide = [halves[c // 2][:, :, :, CHUNK * (c % 2) : CHUNK * (c % 2) + CHUNK] for c in range(CHUNKS)]
 
         def widen(chunks, g, planes, on_vector):
@@ -208,40 +209,30 @@ def tile_pooled_fisher_connectivity_s3_kernel(
 
         grouped, codes, scales = {}, {}, {}
 
-        def handed(turn_number, shape, dtype):
-            return work.tile(shape, dtype, align_bytes=64, name=f"handed_{turn_number % HANDED}", bufs=1)
+        def handed(shape, dtype):
+            return work.tile(shape, dtype, align_bytes=64, name="grouped", bufs=1)
 
-        def open_part(i, part):
-            shape = [P, 2, P, PACK]
-            if part == 0:
-                grouped[i, part] = work.tile(shape, BF16, align_bytes=64, name="grouped", bufs=2)
-            else:
-                grouped[i, part] = handed(max(i - PAIRS, 1), shape, BF16)
-            codes[i, part] = work.tile([P, 2, P], U32, align_bytes=64, name=f"codes_{part}")
-            scales[i, part] = work.tile([P, 2, P], U8, align_bytes=64, name=f"scales_{part}")
-
-        def interleave_on_vector(i):
-            open_part(i, 0)
+        def share(i, lo, hi):
+            if i not in grouped:
+                grouped[i] = handed([P, PASSES, P, PACK], BF16)
+                codes[i] = work.tile([P, PASSES, P], U32, align_bytes=64, name="codes")
+                scales[i] = work.tile([P, PASSES, P], U8, align_bytes=64, name="scales")
             c, j = divmod(i, CHUNK // P)
-            nc.vector.tensor_copy(
-                out=grouped[i, 0][:].rearrange("p g (c i) t -> p g c t i", i=RUN),
-                in_=wide[c][:, :, :2, P * j : P * j + P].rearrange("p t g (c i) -> p g c t i", i=RUN),
-            )
+            return grouped[i][:, :, lo:hi, :], wide[c][:, :, :, P * j + lo : P * j + hi]
 
-        def interleave_on_scalar(i):
-            open_part(i, 1)
-            c, j = divmod(i, CHUNK // P)
-            interleave(nc.scalar.copy, grouped[i, 1][:, 0, :, :], wide[c][:, :, GROUPS - 1, P * j : P * j + P])
+        def interleave_share(i, lo, hi, copy):
+            dst, src = share(i, lo, hi)
+            copy(out=dst.rearrange("p g (c i) t -> p g c t i", i=RUN), in_=src.rearrange("p t g (c i) -> p g c t i", i=RUN))
 
         def interleave_on_gpsimd(i):
-            lo = P * i - NEW_RANGES[2][0]
-            gpsimd_copy(out=grouped[i, 1][:, 1, :, :], in_=new_raw[2][:, :, lo : lo + P].rearrange("p t n -> p n t"))
+            dst, src = share(i, 0, ON_GPSIMD)
+            gpsimd_copy(out=dst, in_=src.rearrange("p t g n -> p g n t"))
 
-        def quantise_part(i, part):
+        def quantise_seeds(i):
             quantise(
-                codes[i, part][:].rearrange("p k n -> p (k n)"),
-                scales[i, part][:].rearrange("p k n -> p (k n)"),
-                grouped[i, part][:].rearrange("p k n t -> p (k n t)"),
+                codes[i][:].rearrange("p k n -> p (k n)"),
+                scales[i][:].rearrange("p k n -> p (k n)"),
+                grouped[i][:].rearrange("p k n t -> p (k n t)"),
             )
 
         r, passes_done = {}, {}
@@ -257,8 +248,7 @@ def tile_pooled_fisher_connectivity_s3_kernel(
                 if c < 2:
                     fixed, fixed_scale = early_codes[c][:, k, P * j : P * j + P], early_scales[c][:, k, P * j : P * j + P]
                 else:
-                    part, slot = divmod((k - 1) % PASSES, 2)
-                    fixed, fixed_scale = codes[i, part][:, slot, :], scales[i, part][:, slot, :]
+                    fixed, fixed_scale = codes[i][:, (k - 1) % PASSES, :], scales[i][:, (k - 1) % PASSES, :]
                 if k == 0:
                     moving, moving_scale = regions_codes[h][:].bitcast(FP8X4), regions_scales[h][:]
                 else:
@@ -319,39 +309,31 @@ def tile_pooled_fisher_connectivity_s3_kernel(
 
         z_codes = keep.tile([P, TILES, 2, P], U32, align_bytes=64)
         z_scales = keep.tile([P, TILES, 2, P], U8, align_bytes=64)
-        z_first = handed(0, [P, 2, 2, P, PACK], BF16)
-        z_last = keep.tile([P, 2, P, PACK], BF16, align_bytes=64)
-        z_grouped = {0: z_first[:, 0, :, :, :], 1: z_first[:, 1, :, :, :], LAST: z_last[:]}
+        z_grouped = {}
 
-        def weigh(i, h):
-            if i not in z_grouped:
-                z_grouped[i] = handed(i + 1, [P, 2, P, PACK], BF16)[:]
+        def weigh(s, n):
+            if s not in z_grouped:
+                z_grouped[s] = work.tile([P, 2, P, PACK], BF16, align_bytes=64, name="z_grouped", bufs=4)
             nc.vector.tensor_tensor(
-                out=z_grouped[i][:, h, :, :].rearrange("p (n e) t -> p n t e", e=2),
-                in0=turned[i, h][:],
-                in1=weights[:, h, :].unsqueeze(1).unsqueeze(3).to_broadcast([P, P // 2, PACK, 2]),
+                out=z_grouped[s][:, n, :, :].rearrange("p (n e) t -> p n t e", e=2),
+                in0=turned[STEPS[s][n]][:],
+                in1=weights[:, STEPS[s][n][1], :].unsqueeze(1).unsqueeze(3).to_broadcast([P, P // 2, PACK, 2]),
                 op=ALU.mult,
             )
 
-        def quantise_z(i, halves=slice(0, 2)):
+        def quantise_z(s, pieces=slice(0, 2)):
             quantise(
-                z_codes[:, i, halves, :].rearrange("p h n -> p (h n)"),
-                z_scales[:, i, halves, :].rearrange("p h n -> p (h n)"),
-                z_grouped[i][:, halves, :, :].rearrange("p h n t -> p (h n t)"),
-            )
-
-        def quantise_first_z():
-            quantise(
-                z_codes[:, :2, :, :].rearrange("p i h n -> p (i h n)"),
-                z_scales[:, :2, :, :].rearrange("p i h n -> p (i h n)"),
-                z_first[:].rearrange("p i h n t -> p (i h n t)"),
+                z_codes[:, s, pieces, :].rearrange("p h n -> p (h n)"),
+                z_scales[:, s, pieces, :].rearrange("p h n -> p (h n)"),
+                z_grouped[s][:, pieces, :, :].rearrange("p h n t -> p (h n t)"),
             )
 
         def project_pass(dst, i, h, lo, hi):
+            s, n = (h, i) if i < 2 else (i, h)
             nc.tensor.matmul_mx(
                 out=dst,
-                lhsT=z_codes[:, i, h, :].bitcast(FP8X4),
-                lhsT_scale=z_scales[:, i, h, :],
+                lhsT=z_codes[:, s, n, :].bitcast(FP8X4),
+                lhsT_scale=z_scales[:, s, n, :],
                 rhs=p_words[:, h, 2 * lo : 2 * hi].bitcast(FP4X4),
                 rhs_scale=p_scales[:, h, lo:hi],
                 start=(h == 0),
@@ -388,6 +370,7 @@ def tile_pooled_fisher_connectivity_s3_kernel(
         empty_through(early_grouped[1][:, 1, :, :])
         interleave_early(0, 3, nc.scalar.copy)
         interleave_early(1, 3)
+        widen((2, 3), 1, planes[:1], True)
         quantise_early(1, 1)
         quantise_early(1, 3)
         empty_through(early_grouped[1][:, 2, :, :])
@@ -397,29 +380,30 @@ def tile_pooled_fisher_connectivity_s3_kernel(
         quantise_early(1, 2)
         interleave_early(0, 0, nc.scalar.copy)
         quantise_early(0, 0)
-        widen((2, 3), 1, planes[:2], True)
+        widen((2, 3), 1, planes[1:2], True)
         widen((2, 3), 2, planes[:3], False)
         for s in range(3):
             correlate(s, [1])
         correlate(3, [1], [0])
         correlate(0, [2])
+        correlate(1, [2])
         correlate(3, [1], [1])
         correlate(0, [3])
-        correlate(1, [2])
+        correlate(1, [3], [0])
         correlate(0, [0])
-        correlate(1, [3])
+        correlate(1, [3], [1])
         correlate(2, [2, 3])
         take_logarithms(0, 0)
         take_logarithms(0, 1)
         interleave_regions(1)
+        widen((2, 3), 1, planes[2:3], True)
         form_difference(0, slice(0, 1))
         quantise_regions(1)
         turn(0, 0)
         correlate(1, [0])
-        handover = handed(1, [P, CHUNK, PACK], BF16)
+        handover = handed([P, CHUNK, PACK], BF16)
         interleave(nc.vector.tensor_copy, handover[:], new_raw[1][:])
         form_difference(0, slice(1, 2))
-        widen((2, 3), 1, planes[2:3], True)
         quantise(early_codes[1][:, 0, :], early_scales[1][:, 0, :], handover[:].rearrange("p n t -> p (n t)"))
         widen((2, 3), 2, planes[3:], True)
 
@@ -437,44 +421,30 @@ def tile_pooled_fisher_connectivity_s3_kernel(
             if s >= 3:
                 store(s - 3)
             if preparing:
-                interleave_on_scalar(tile)
-            for i, h in STEPS[s]:
-                weigh(i, h)
+                interleave_share(tile, ON_GPSIMD, ON_GPSIMD + ON_SCALAR, nc.scalar.copy)
+            weigh(s, 0)
+            weigh(s, 1)
             if preparing:
                 interleave_on_gpsimd(tile)
             if s == 0:
                 correlate(2, [0])
                 correlate(3, [2, 0])
             if not preparing:
-                lent[s + 1] = handed(s, [P, LENT, P], F32)
+                lent[s + 1] = handed([P, LENT, P], F32)
                 subtract_planes(nc.gpsimd, s + 1, lent[s + 1][:], 0, LENT)
                 rest = difference[s + 1][:].rearrange("s n t p -> s (n t) p")[:, LENT:, :]
                 subtract_planes(nc.vector, s + 1, rest, LENT, 2 * PACK)
-            elif s == 0:
-                form_difference(1, slice(0, 1))
-                interleave_on_vector(tile)
-                form_difference(1, slice(1, 2))
-                quantise_part(tile, 0)
-                quantise_part(tile, 1)
-            elif adds_in_psum(s + 1, 0) != adds_in_psum(s + 1, 1):
-                form_difference(s + 1, slice(0, 1))
-                form_difference(s + 1, slice(1, 2))
             else:
-                form_difference(s + 1, slice(0, 2))
+                form_difference(s + 1, slice(0, 1))
+                interleave_share(tile, ON_GPSIMD + ON_SCALAR, P, nc.vector.tensor_copy)
+                form_difference(s + 1, slice(1, 2))
+                quantise_seeds(tile)
             take_logarithms(s + 2, 1 if LOG_REVERSED <= s + 2 else 0)
             if s > 0:
                 correlate(s + 3, (1, 2, 3, 0))
             if 2 <= s < LAST - 3:
                 project(s - 2, r_bank(s) + 1)
-            if preparing and s > 0:
-                interleave_on_vector(tile)
-            if preparing and s > 0:
-                quantise_part(tile, 1)
-                quantise_part(tile, 0)
-            if s == 1:
-                quantise_first_z()
-            if s >= 2:
-                quantise_z(s)
+            quantise_z(s)
 
         take_logarithms(LAST - 1, 0 if LOG_REVERSED < LAST else 1)
         turn(LAST - 2, 0)

from contextlib import ExitStack

import concourse.mybir as mybir
from concourse.masks import make_identity

T1, T2, M, R, E = 512, 1536, 1024, 1024, 512
FLOPS = 2 * M * R * (T1 + T2) + 2 * M * R * E

F32 = mybir.dt.float32
BF16 = mybir.dt.bfloat16
U32 = mybir.dt.uint32
I32 = mybir.dt.int32
U8 = mybir.dt.uint8
FP8 = mybir.dt.float8_e4m3fn
FP8X4 = mybir.dt.float8_e4m3fn_x4
FP4X4 = mybir.dt.float4_e2m1fn_x4
ACT = mybir.ActivationFunctionType
ALU = mybir.AluOpType

P = 128
PACK = 4
GROUPS = T2 // (P * PACK)
PASSES = 1 + GROUPS
HALF = 512
RUN = 4
CHUNK = 256
TILES = M // P
CHUNKS = M // CHUNK
LAST = TILES - 1

NEW_RANGES = ((0, CHUNK), (CHUNK, HALF), (HALF, M))

STEPS = [((0, 0), (1, 0)), ((0, 1), (1, 1))] + [((i, 0), (i, 1)) for i in range(2, TILES)]
ADDED_STEP = 2
LOG_REVERSED = 3
LENT = 3
ON_GPSIMD = 40
ON_SCALAR = 36
PAIRS = 4


def r_bank(s):
    return 2 * (s % PAIRS)


def adds_in_psum(s, n):
    return s == 0 or (n == 1 and s in (ADDED_STEP, LAST))


def tile_pooled_fisher_connectivity_s3_kernel(
    tc,
    seeds_new,
    regions_new,
    seeds_old_bytes,
    seeds_old_scale,
    old_words,
    old_scales,
    precision,
    net_words,
    net_scales,
    out,
):
    nc = tc.nc
    with ExitStack() as ctx:
        keep = ctx.enter_context(tc.tile_pool(name="keep", bufs=1))
        work = ctx.enter_context(tc.tile_pool(name="work", bufs=3))
        psum = ctx.enter_context(tc.psum_pool(name="psum", bufs=1))
        ctx.enter_context(tc.manual_schedule())

        def kept(name, count, shape, dtype):
            return [keep.tile(shape, dtype, align_bytes=64, name=f"{name}_{n}") for n in range(count)]

        def bank(number, shape):
            return psum.tile(shape, F32, name=f"bank_{number}")

        regions_raw = kept("regions_raw", 2, [P, PACK, HALF], BF16)
        new_raw = [keep.tile([P, PACK, hi - lo], BF16, align_bytes=64, name=f"new_raw_{lo}") for lo, hi in NEW_RANGES[:2]]
        old_bytes = [kept(f"old_bytes_{g}", 1 + 3 * (g == 0), [P, PACK // (1 + 3 * (g == 0)), M], U8) for g in range(GROUPS)]
        halves = [keep.tile([P, PACK, GROUPS + b, HALF], BF16, align_bytes=64, name=f"wide_{b}") for b in range(2)]
        new_raw.append(halves[1][:, :, GROUPS, :])
        old_factor = keep.tile([P, GROUPS, PACK], F32)
        d_words = kept("d_words", GROUPS, [P, 2 * R], U8)
        d_scales = keep.tile([P, GROUPS, R], U8, align_bytes=64)
        p_words = keep.tile([P, 2, 2 * E], U8, align_bytes=64)
        p_scales = keep.tile([P, 2, E], U8, align_bytes=64)
        weights = keep.tile([P, 2, PACK], BF16)

        regions_grouped = kept("regions_grouped", 2, [P, HALF, PACK], BF16)
        regions_codes = kept("regions_codes", 2, [P, HALF], U32)
        regions_scales = kept("regions_scales", 2, [P, HALF], U8)

        identity = keep.tile([P, P], F32)
        identity_bf16 = keep.tile([P, P], BF16)
        one = keep.tile([P, 1], F32)

        nc.vector.memset(one[:], 1.0)
        nc.vector.memset(d_scales[:].rearrange("p g n -> p (g n)").bitcast(I32), 0)
        nc.vector.memset(p_scales[:].rearrange("p g n -> p (g n)").bitcast(I32), 0)
        make_identity(nc, identity_bf16[:])
        nc.vector.tensor_copy(out=identity[:], in_=identity_bf16[:])

        def load_regions(h):
            rows = regions_new.rearrange("(p t) n -> p t n", t=PACK)
            nc.sync.dma_start(out=regions_raw[h][:], in_=rows[:, :, HALF * h : HALF * h + HALF])

        def load_new(n):
            lo, hi = NEW_RANGES[n]
            nc.sync.dma_start(out=new_raw[n][:, :, :], in_=seeds_new.rearrange("(p t) n -> p t n", t=PACK)[:, :, lo:hi])

        def load_old(g):
            rows = seeds_old_bytes.rearrange("(g p t) n -> g p t n", p=P, t=PACK)[g]
            planes = PACK // len(old_bytes[g])
            for u, tile in enumerate(old_bytes[g]):
                nc.sync.dma_start(out=tile[:], in_=rows[:, planes * u : planes * u + planes, :])

        def load_d(g):
            nc.sync.dma_start(out=d_words[g][:], in_=old_words[g])

        def load_scale_rows(tile, rows, groups):
            for j in range(4):
                nc.sync.dma_start(
                    out=tile[j:P:32].rearrange("p g n -> p (g n)").bitcast(I32).rearrange("p (g n) -> p g n", g=groups),
                    in_=rows.bitcast(I32).rearrange("g (q j) n -> j q g n", j=4)[j],
                )

        nc.scalar.dma_start(
            out=old_factor[:], in_=seeds_old_scale.rearrange("(g p t) o -> p g (t o)", p=P, t=PACK)
        )
        for g in range(GROUPS):
            load_old(g)
        load_scale_rows(d_scales, old_scales, GROUPS)
        load_d(0)
        load_regions(0)
        load_d(1)
        load_new(0)
        load_d(2)
        load_regions(1)
        load_new(1)
        nc.sync.dma_start(out=weights[:], in_=precision.rearrange("(h p t) -> p h t", p=P, t=PACK))
        load_new(2)
        nc.sync.dma_start(out=p_words[:], in_=net_words.rearrange("g p w -> p g w"))
        load_scale_rows(p_scales, net_scales, 2)

        nc.scalar.activation(out=one[:], in_=one[:], func=ACT.Ln)

        wide = [halves[c // 2][:, :, :, CHUNK * (c % 2) : CHUNK * (c % 2) + CHUNK] for c in range(CHUNKS)]

        def widen(chunks, g, planes, on_vector):
            lo, hi = CHUNK * chunks[0], CHUNK * (chunks[-1] + 1)
            for t in planes:
                u, row = divmod(t, PACK // len(old_bytes[g]))
                src = old_bytes[g][u][:, row, lo:hi].bitcast(FP8)
                dst = halves[lo // HALF][:, t, g, lo % HALF : lo % HALF + hi - lo]
                factor = old_factor[:, g, t : t + 1]
                if on_vector:
                    nc.vector.tensor_scalar(out=dst, in0=src, scalar1=factor, scalar2=None, op0=ALU.mult)
                else:
                    nc.scalar.activation(out=dst, in_=src, func=ACT.Copy, scale=factor)

        def interleave(copy, dst, src):
            copy(
                out=dst.rearrange("p (c i) t -> p c t i", i=RUN),
                in_=src.rearrange("p t (c i) -> p c t i", i=RUN),
            )

        through = []

        def turn_by_matmul(src, number):
            through.append(psum.tile([P, 2, P, PACK], BF16, name=f"bank_{number}"))
            for j in range(2):
                nc.tensor.matmul(
                    through[-1][:, j, :, :],
                    lhsT=identity_bf16[:],
                    rhs=src[:, :, P * j : P * j + P].rearrange("p t n -> p n t"),
                    start=True,
                    stop=True,
                )

        def empty_through(dst):
            nc.scalar.copy(out=dst.rearrange("p n t -> p (n t)"), in_=through[0][:].rearrange("p j n t -> p (j n t)"))
            through.remove(through[0])

        def gpsimd_copy(out, in_):
            nc.gpsimd.tensor_scalar(out=out, in0=in_, scalar1=1.0, scalar2=0.0, op0=ALU.mult, op1=ALU.add)

        def quantise(codes_ap, scales_ap, values_ap):
            nc.vector.quantize_mx(out=codes_ap.bitcast(FP8X4), scales=scales_ap, in_=values_ap)

        def interleave_regions(h):
            interleave(nc.vector.tensor_copy, regions_grouped[h][:], regions_raw[h][:])

        def quantise_regions(h):
            quantise(regions_codes[h][:], regions_scales[h][:], regions_grouped[h][:].rearrange("p n t -> p (n t)"))

        early_grouped = kept("early_grouped", 2, [P, PASSES, CHUNK, PACK], BF16)
        early_codes = kept("early_codes", 2, [P, PASSES, CHUNK], U32)
        early_scales = kept("early_scales", 2, [P, PASSES, CHUNK], U8)

        def interleave_early(c, k, copy=nc.vector.tensor_copy):
            interleave(copy, early_grouped[c][:, k, :, :], new_raw[c][:] if k == 0 else wide[c][:, :, k - 1, :])

        def quantise_early(c, k, count=1):
            passes = slice(k, k + count)
            quantise(
                early_codes[c][:, passes, :].rearrange("p k n -> p (k n)"),
                early_scales[c][:, passes, :].rearrange("p k n -> p (k n)"),
                early_grouped[c][:, passes, :, :].rearrange("p k n t -> p (k n t)"),
            )

        grouped, codes, scales = {}, {}, {}

        def handed(shape, dtype):
            return work.tile(shape, dtype, align_bytes=64, name="grouped", bufs=1)

        def share(i, lo, hi):
            if i not in grouped:
                grouped[i] = handed([P, PASSES, P, PACK], BF16)
                codes[i] = work.tile([P, PASSES, P], U32, align_bytes=64, name="codes")
                scales[i] = work.tile([P, PASSES, P], U8, align_bytes=64, name="scales")
            c, j = divmod(i, CHUNK // P)
            return grouped[i][:, :, lo:hi, :], wide[c][:, :, :, P * j + lo : P * j + hi]

        def interleave_share(i, lo, hi, copy):
            dst, src = share(i, lo, hi)
            copy(out=dst.rearrange("p g (c i) t -> p g c t i", i=RUN), in_=src.rearrange("p t g (c i) -> p g c t i", i=RUN))

        def interleave_on_gpsimd(i):
            dst, src = share(i, 0, ON_GPSIMD)
            gpsimd_copy(out=dst, in_=src.rearrange("p t g n -> p g n t"))

        def quantise_seeds(i):
            quantise(
                codes[i][:].rearrange("p k n -> p (k n)"),
                scales[i][:].rearrange("p k n -> p (k n)"),
                grouped[i][:].rearrange("p k n t -> p (k n t)"),
            )

        r, passes_done = {}, {}

        def correlate(s, passes, pieces=(0, 1)):
            for n, k in [(n, k) for n in pieces for k in passes]:
                i, h = STEPS[s][n]
                if (i, h) not in r:
                    r[i, h] = bank(r_bank(s) + n, [P, HALF])
                done = passes_done.get((i, h), 0)
                passes_done[i, h] = done + 1
                c, j = divmod(i, CHUNK // P)
                if c < 2:
                    fixed, fixed_scale = early_codes[c][:, k, P * j : P * j + P], early_scales[c][:, k, P * j : P * j + P]
                else:
                    fixed, fixed_scale = codes[i][:, (k - 1) % PASSES, :], scales[i][:, (k - 1) % PASSES, :]
                if k == 0:
                    moving, moving_scale = regions_codes[h][:].bitcast(FP8X4), regions_scales[h][:]
                else:
                    moving = d_words[k - 1][:, 2 * HALF * h : 2 * HALF * h + 2 * HALF].bitcast(FP4X4)
                    moving_scale = d_scales[:, k - 1, HALF * h : HALF * h + HALF]
                nc.tensor.matmul_mx(
                    out=r[i, h][:],
                    lhsT=fixed.bitcast(FP8X4),
                    lhsT_scale=fixed_scale,
                    rhs=moving,
                    rhs_scale=moving_scale,
                    start=(done == 0),
                    stop=(done == PASSES - 1),
                )

        ln_plus, ln_minus, difference = {}, {}, {}

        def take_logarithms(s, n):
            if s not in ln_plus:
                ln_plus[s] = work.tile([P, 2, PACK, P], F32, name="ln_plus", bufs=4)
                ln_minus[s] = work.tile([P, 2, PACK, P], F32, name="ln_minus", bufs=2)
                if s < LAST:
                    difference[s] = work.tile([P, 2, PACK, P], F32, name="difference")
            by_t = r[STEPS[s][n]][:].rearrange("s (p t) -> s t p", t=PACK)
            nc.scalar.activation(out=ln_minus[s][:, n, :, :], in_=by_t, func=ACT.Ln, bias=1.0, scale=-1.0)
            nc.scalar.activation(out=ln_plus[s][:, n, :, :], in_=by_t, func=ACT.Ln, bias=1.0, scale=1.0)

        def form_difference(s, pieces, engine=nc.vector):
            dst = difference[s][:, pieces, :, :]
            minus = ln_minus[s][:, pieces, :, :]
            if not adds_in_psum(s, pieces.start):
                engine.tensor_tensor(out=dst, in0=ln_plus[s][:, pieces, :, :], in1=minus, op=ALU.subtract)
            elif s < LAST:
                nc.vector.tensor_scalar(out=dst, in0=minus, scalar1=-1.0, scalar2=None, op0=ALU.mult)
            else:
                nc.scalar.activation(out=dst, in_=minus, func=ACT.Copy, scale=-1.0)

        def subtract_planes(engine, s, dst, lo, hi):
            flat = [part[:].rearrange("s n t p -> s (n t) p")[:, lo:hi, :] for part in (ln_plus[s], ln_minus[s])]
            engine.tensor_tensor(out=dst, in0=flat[0], in1=flat[1], op=ALU.subtract)

        turned, lent = {}, {}

        def turn(s, n):
            piece = STEPS[s][n]
            turned[piece] = bank(r_bank(s) + n, [P, P // 2, PACK, 2])
            parts = (difference[s], ln_plus[s]) if adds_in_psum(s, n) else (difference[s],)
            for t in range(PACK):
                for m, part in enumerate(parts):
                    nc.tensor.matmul(
                        turned[piece][:, :, t, :],
                        lhsT=lent[s][:, t, :] if s in lent and PACK * n + t < LENT else part[:, n, t, :],
                        rhs=identity[:],
                        start=(m == 0),
                        stop=(m == len(parts) - 1),
                        is_transpose=True,
                    )

        z_codes = keep.tile([P, TILES, 2, P], U32, align_bytes=64)
        z_scales = keep.tile([P, TILES, 2, P], U8, align_bytes=64)
        z_grouped = {}

        def weigh(s, n):
            if s not in z_grouped:
                z_grouped[s] = work.tile([P, 2, P, PACK], BF16, align_bytes=64, name="z_grouped", bufs=4)
            nc.vector.tensor_tensor(
                out=z_grouped[s][:, n, :, :].rearrange("p (n e) t -> p n t e", e=2),
                in0=turned[STEPS[s][n]][:],
                in1=weights[:, STEPS[s][n][1], :].unsqueeze(1).unsqueeze(3).to_broadcast([P, P // 2, PACK, 2]),
                op=ALU.mult,
            )

        def quantise_z(s, pieces=slice(0, 2)):
            quantise(
                z_codes[:, s, pieces, :].rearrange("p h n -> p (h n)"),
                z_scales[:, s, pieces, :].rearrange("p h n -> p (h n)"),
                z_grouped[s][:, pieces, :, :].rearrange("p h n t -> p (h n t)"),
            )

        def project_pass(dst, i, h, lo, hi):
            s, n = (h, i) if i < 2 else (i, h)
            nc.tensor.matmul_mx(
                out=dst,
                lhsT=z_codes[:, s, n, :].bitcast(FP8X4),
                lhsT_scale=z_scales[:, s, n, :],
                rhs=p_words[:, h, 2 * lo : 2 * hi].bitcast(FP4X4),
                rhs_scale=p_scales[:, h, lo:hi],
                start=(h == 0),
                stop=(h == 1),
            )

        out_bank = {}

        def project(i, number):
            out_bank[i] = bank(number, [P, E])
            for h in range(2):
                project_pass(out_bank[i][:], i, h, 0, E)

        def store(i):
            result = work.tile([P, E], F32, bufs=7)
            nc.scalar.copy(out=result[:], in_=out_bank[i][:])
            nc.sync.dma_start(out=out[P * i : P * i + P, :], in_=result[:])

        planes = range(PACK)
        widen((0, 1), 0, planes[:3], True)
        widen((0,), 0, planes[3:], True)
        widen((1,), 0, planes[3:], True)
        widen((2, 3), 0, planes, False)
        turn_by_matmul(wide[1][:, :, 0, :], r_bank(PAIRS - 1))
        interleave_early(0, 1)
        widen((0,), 1, planes, True)
        widen((1,), 1, planes, False)
        widen((0,), 2, planes, False)
        turn_by_matmul(wide[1][:, :, 1, :], r_bank(PAIRS - 1) + 1)
        quantise_early(0, 1)
        interleave_early(0, 2)
        widen((1,), 2, planes, True)
        quantise_early(0, 2)
        empty_through(early_grouped[1][:, 1, :, :])
        interleave_early(0, 3, nc.scalar.copy)
        interleave_early(1, 3)
        widen((2, 3), 1, planes[:1], True)
        quantise_early(1, 1)
        quantise_early(1, 3)
        empty_through(early_grouped[1][:, 2, :, :])
        interleave_regions(0)
        quantise_early(0, 3)
        quantise_regions(0)
        quantise_early(1, 2)
        interleave_early(0, 0, nc.scalar.copy)
        quantise_early(0, 0)
        widen((2, 3), 1, planes[1:2], True)
        widen((2, 3), 2, planes[:3], False)
        for s in range(3):
            correlate(s, [1])
        correlate(3, [1], [0])
        correlate(0, [2])
        correlate(1, [2])
        correlate(3, [1], [1])
        correlate(0, [3])
        correlate(1, [3], [0])
        correlate(0, [0])
        correlate(1, [3], [1])
        correlate(2, [2, 3])
        take_logarithms(0, 0)
        take_logarithms(0, 1)
        interleave_regions(1)
        widen((2, 3), 1, planes[2:3], True)
        form_difference(0, slice(0, 1))
        quantise_regions(1)
        turn(0, 0)
        correlate(1, [0])
        handover = handed([P, CHUNK, PACK], BF16)
        interleave(nc.vector.tensor_copy, handover[:], new_raw[1][:])
        form_difference(0, slice(1, 2))
        quantise(early_codes[1][:, 0, :], early_scales[1][:, 0, :], handover[:].rearrange("p n t -> p (n t)"))
        widen((2, 3), 2, planes[3:], True)

        widen((2, 3), 1, planes[3:], False)
        take_logarithms(1, 0)
        for s in range(LAST - 2):
            tile = s + PAIRS
            preparing = tile < TILES
            if s > 0:
                turn(s, 0)
            if s == 1:
                correlate(3, [3])
            turn(s, 1)
            take_logarithms(s + 1, 0 if LOG_REVERSED <= s + 1 else 1)
            if s >= 3:
                store(s - 3)
            if preparing:
                interleave_share(tile, ON_GPSIMD, ON_GPSIMD + ON_SCALAR, nc.scalar.copy)
            weigh(s, 0)
            weigh(s, 1)
            if preparing:
                interleave_on_gpsimd(tile)
            if s == 0:
                correlate(2, [0])
                correlate(3, [2, 0])
            if not preparing:
                lent[s + 1] = handed([P, LENT, P], F32)
                subtract_planes(nc.gpsimd, s + 1, lent[s + 1][:], 0, LENT)
                rest = difference[s + 1][:].rearrange("s n t p -> s (n t) p")[:, LENT:, :]
                subtract_planes(nc.vector, s + 1, rest, LENT, 2 * PACK)
            else:
                form_difference(s + 1, slice(0, 1))
                interleave_share(tile, ON_GPSIMD + ON_SCALAR, P, nc.vector.tensor_copy)
                form_difference(s + 1, slice(1, 2))
                quantise_seeds(tile)
            take_logarithms(s + 2, 1 if LOG_REVERSED <= s + 2 else 0)
            if s > 0:
                correlate(s + 3, (1, 2, 3, 0))
            if 2 <= s < LAST - 3:
                project(s - 2, r_bank(s) + 1)
            quantise_z(s)

        take_logarithms(LAST - 1, 0 if LOG_REVERSED < LAST else 1)
        turn(LAST - 2, 0)
        turn(LAST - 2, 1)
        project(LAST - 5, r_bank(LAST - 3) + 1)
        project(LAST - 4, r_bank(LAST - 3))
        form_difference(LAST - 1, slice(0, 2))
        take_logarithms(LAST, 0)
        take_logarithms(LAST, 1)
        difference[LAST] = work.tile([P, 2, PACK, P], F32, name="ln_minus", bufs=2)
        form_difference(LAST, slice(0, 1), nc.gpsimd)
        form_difference(LAST, slice(1, 2))
        turn(LAST - 1, 0)
        turn(LAST - 1, 1)
        weigh(LAST - 2, 1)
        weigh(LAST - 2, 0)
        project(LAST - 3, r_bank(LAST - 2) + 1)
        for i in range(LAST - 5, LAST - 2):
            store(i)
        weigh(LAST - 1, 0)
        weigh(LAST - 1, 1)
        turn(LAST, 0)
        turn(LAST, 1)
        quantise_z(LAST - 2)
        project(LAST - 2, r_bank(LAST - 2))
        quantise_z(LAST - 1)
        weigh(LAST, 0)
        weigh(LAST, 1)
        project(LAST - 1, r_bank(LAST - 1))
        store(LAST - 2)
        quarters = [bank(number, [P, P]) for number in (r_bank(LAST - 3) + 1, r_bank(LAST - 3), r_bank(LAST - 1) + 1, r_bank(LAST - 2) + 1)]
        for h in range(2):
            quantise_z(LAST, slice(h, h + 1))
            for q in range(4):
                project_pass(quarters[q][:], LAST, h, P * q, P * q + P)
        store(LAST - 1)
        for n, (copy, queue) in enumerate(((nc.vector.tensor_copy, nc.sync), (nc.scalar.copy, nc.scalar))):
            result_half = work.tile([P, 2, P], F32)
            for q in range(2):
                copy(out=result_half[:, q, :], in_=quarters[2 * n + q][:])
            queue.dma_start(
                out=out[P * LAST : P * LAST + P, 2 * P * n : 2 * P * n + 2 * P],
                in_=result_half[:].rearrange("p q n -> p (q n)"),
            )
